import numpy as np
import ml_dtypes


def mxq(x, axis, fmt="e4m3"):
    dtype, down = {"e4m3": (ml_dtypes.float8_e4m3fn, 7), "e5m2": (ml_dtypes.float8_e5m2, 14)}[fmt]
    v = np.moveaxis(np.asarray(x, np.float32).astype(ml_dtypes.bfloat16).astype(np.float64), axis, -1)
    blocks = v.reshape(v.shape[:-1] + (-1, 32))
    amax = np.abs(blocks).max(-1, keepdims=True)
    byte = np.maximum(np.where(amax > 0, np.frexp(amax)[1] - 1 + 127, 0) - down, 1)
    scale = np.exp2(byte - 127.0)
    codes = (blocks / scale).astype(np.float32).astype(dtype).astype(np.float64)
    return np.moveaxis((codes * scale).reshape(v.shape), -1, axis)


WIDE = False


def mx_kscale(k):
    if not WIDE:
        return np.ones(k)
    levels = np.array([24, -24, 12, -12, 0])
    if k % 512:
        return np.exp2(np.random.permutation(np.resize(levels, k // 32))).repeat(32)
    a = np.empty((k // 512, 16))
    for p in range(k // 512):
        a[p, :8] = np.random.permutation(np.resize(levels, 8))
        for g in range(8):
            far = levels[np.abs(levels - a[p, g]) >= 10]
            a[p, g + 8] = far[np.random.randint(len(far))]
    return np.exp2(a.ravel()).repeat(32)


def f64(x):
    return np.asarray(x).astype(np.float64)


def striped(idx):
    return np.tile(idx.reshape(-1, 16).T, (8, 1)).astype(np.uint16)


def unstriped(offs):
    return offs[:16].T.reshape(-1).astype(np.int64)


E2M1 = np.array([0.0, 0.5, 1.0, 1.5, 2.0, 3.0, 4.0, 6.0, -0.0, -0.5, -1.0, -1.5, -2.0, -3.0, -4.0, -6.0])


def pack_weight(w, fmt):
    k, n = w.shape
    w = f64(np.asarray(w, np.float32).astype(ml_dtypes.bfloat16)).reshape(k // 32, 32, n)
    amax = np.abs(w).max(1)
    if fmt == "e4m3":
        byte = np.frexp(amax)[1] - 1 + 127 - 7
    else:
        mant, ex = np.frexp(amax / 6.0)
        byte = np.where(mant > 0.5, ex, ex - 1) + 127
    byte = np.clip(np.where(amax > 0, byte, 1), 1, 254)
    scaled = (w * np.exp2(127.0 - byte)[:, None, :]).reshape(k, n).astype(np.float32)
    by_word = np.ascontiguousarray(scaled.reshape(k // 512, 128, 4, n).transpose(0, 1, 3, 2))
    if fmt == "e4m3":
        words = by_word.astype(ml_dtypes.float8_e4m3fn).view(np.uint8)
    else:
        c = by_word.astype(ml_dtypes.float4_e2m1fn).view(np.uint8) & 0xF
        words = (c[..., 0::2] | (c[..., 1::2] << 4)).reshape(k // 512, 128, 2 * n)
    return np.ascontiguousarray(words), np.ascontiguousarray(byte.astype(np.uint8).reshape(k // 512, 16, n))


def unpack_weight(words, scales, fmt):
    g, _, n = scales.shape
    words = np.ascontiguousarray(words).reshape(g, 128, n, -1)
    if fmt == "e4m3":
        vals = words.view(ml_dtypes.float8_e4m3fn).astype(np.float64)
    else:
        nib = np.empty((g, 128, n, 4), np.uint8)
        nib[..., 0::2] = words & 0xF
        nib[..., 1::2] = words >> 4
        vals = E2M1[nib]
    vals = vals * np.repeat(np.exp2(scales.astype(np.float64) - 127.0), 8, axis=1)[..., None]
    return vals.transpose(0, 1, 3, 2).reshape(g * 512, n)


def pack_table4(v):
    words, scales = pack_weight(v, "e2m1")
    g, t = words.shape[0] // 2, v.shape[1]
    return np.ascontiguousarray(words.reshape(g, 2, 128, t, 2).transpose(0, 2, 3, 1, 4).reshape(g, 128, t, 4)), scales


def unpack_table4(words, scales):
    g, _, t, _ = words.shape
    return unpack_weight(words.reshape(g, 128, t, 2, 2).transpose(0, 3, 1, 2, 4).reshape(2 * g, 128, 2 * t), scales, "e2m1")


def silu(f):
    return f / (1.0 + np.exp(-np.maximum(f, -700.0)))


K, R, N, T, J = 1024, 512, 512, 2048, 1024


def setup_inputs():
    n = np.random.standard_normal
    s = mx_kscale(K)[:, None]
    u = mx_kscale(R)[:, None]
    p_tab = pack_table4(n((K, T)) * s)
    p_wu = pack_weight(n((K, R)) / np.sqrt(K) / s * u.T, "e2m1")
    p_wd = pack_weight(n((R, N)) / np.sqrt(R) / u, "e4m3")
    return {
        "tab_words": p_tab[0],
        "tab_scales": p_tab[1],
        "wg": (n((K, R)) / np.sqrt(K) / s).astype(np.float32),
        "wu_words": p_wu[0],
        "wu_scales": p_wu[1],
        "wd_words": p_wd[0],
        "wd_scales": p_wd[1],
        "wgo": np.tile(np.random.uniform(0.5, 2.0, J), (128, 1)).astype(np.float32),
        "offs": striped(np.random.permutation(T)[:J]),
    }


def reference(tab_words, tab_scales, wg, wu_words, wu_scales, wd_words, wd_scales, wgo, offs):
    idx = unstriped(offs)
    tab_ = unpack_table4(tab_words, tab_scales)[:, idx]
    wg_ = mxq(f64(wg), 0, "e4m3")
    wu_ = unpack_weight(wu_words, wu_scales, "e2m1")
    ga = wg_.T @ tab_
    ub = wu_.T @ tab_
    h = silu(ga) * ub
    h_ = mxq(h, 0, "e4m3")
    wd_ = unpack_weight(wd_words, wd_scales, "e4m3")
    y = wd_.T @ h_
    out = np.zeros((N, T))
    out[:, idx] = f64(wgo)[0] * (y)
    return out

@@ -1,0 +1,227 @@
+from contextlib import ExitStack
+
+import concourse.mybir as mybir
+from concourse.masks import make_identity
+
+K, R, N, T, J = 1024, 512, 512, 2048, 1024
+FLOPS = 2 * J * (2 * K * R + R * N)
+
+F32 = mybir.dt.float32
+BF16 = mybir.dt.bfloat16
+I32 = mybir.dt.int32
+U32 = mybir.dt.uint32
+U16 = mybir.dt.uint16
+U8 = mybir.dt.uint8
+FP8X4 = mybir.dt.float8_e4m3fn_x4
+FP4X4 = mybir.dt.float4_e2m1fn_x4
+MULT = mybir.AluOpType.mult
+SILU = mybir.ActivationFunctionType.Silu
+
+P = 128
+BLOCK = 128
+GROUP = 256
+GROUPS = J // GROUP
+N_TILES = N // P
+WINDOWS = 3
+
+
+def tile_list_modp_gsilu_none_kernel(
+    tc, tab_words, tab_scales, wg, wu_words, wu_scales, wd_words, wd_scales, wgo, offs, out
+):
+    nc = tc.nc
+    with ExitStack() as ctx:
+        held = ctx.enter_context(tc.tile_pool(name="held", bufs=1))
+        ring = ctx.enter_context(tc.tile_pool(name="ring", bufs=3))
+        psum = ctx.enter_context(tc.psum_pool(name="psum", bufs=1))
+
+        offsets = held.tile([P, J // 16], U16, name="offsets")
+        nc.sync.dma_start(offsets[:], offs)
+
+        table_scales = held.tile([P, T], U8, name="table_scales", tag="scales_then_wd", align_bytes=64)
+        nc.vector.memset(table_scales[:].bitcast(I32), 0)
+        wg_rows = wg.rearrange("(a p i) r -> a p i r", a=2, i=4)
+        wg_raw0 = held.tile([P, 4, R], F32, name="wg_raw0", tag="wg_then_router")
+        nc.sync.dma_start(wg_raw0[:], wg_rows[0])
+        for q in range(4):
+            nc.sync.dma_start(
+                table_scales[32 * q : 32 * q + 8, :].bitcast(I32),
+                tab_scales[:, 4 * q : 4 * q + 4, :].bitcast(I32),
+            )
+        table = held.tile([P, T], I32, name="table")
+        nc.sync.dma_start(table[:], tab_words[0].rearrange("p t b -> p (t b)").bitcast(I32))
+        wu_w = held.tile([P, 2, 2 * R], U8, name="wu_w", align_bytes=64)
+        nc.sync.dma_start(wu_w[:].bitcast(I32), wu_words.rearrange("a p b -> p a b").bitcast(I32))
+        wg_raw1 = []
+        for half in range(2):
+            piece = held.tile([P, 4, R // 2], F32, name="wg_raw1_%d" % half)
+            nc.sync.dma_start(piece[:], wg_rows[1][:, :, half * (R // 2) : (half + 1) * (R // 2)])
+            wg_raw1.append(piece)
+
+        warm_in = held.tile([P, 1], F32, name="warm_in")
+        nc.gpsimd.memset(warm_in[:], 0.0)
+        warm = held.tile([P, 1], F32, name="warm")
+        nc.scalar.activation(warm[:], warm_in[:], SILU)
+
+        wu_s = held.tile([P, 2, R], U8, name="wu_s", align_bytes=64)
+        wd_s = held.tile([P, N], U8, name="wd_s", align_bytes=64)
+        nc.gpsimd.memset(wu_s[:].bitcast(I32), 0)
+        nc.gpsimd.memset(wd_s[:].bitcast(I32), 0)
+        for q in range(4):
+            nc.gpsimd.dma_start(
+                wu_s[32 * q : 32 * q + 4, :, :].bitcast(I32),
+                wu_scales[:, 4 * q : 4 * q + 4, :].rearrange("a r n -> r a n").bitcast(I32),
+            )
+        identity = held.tile([P, P], F32, name="identity")
+        make_identity(nc, identity[:])
+        for q in range(4):
+            nc.gpsimd.dma_start(
+                wd_s[32 * q : 32 * q + 4, :].bitcast(I32), wd_scales[0, 4 * q : 4 * q + 4, :].bitcast(I32)
+            )
+
+        picked_s1 = held.tile([P, J], U8, name="picked_s1", align_bytes=64)
+        nc.vector.memset(picked_s1[:].bitcast(I32), 0)
+        picked_s0 = held.tile([P, J], U8, name="picked_s0", align_bytes=64)
+        nc.vector.tensor_copy(picked_s0[:], table_scales[:].indirect(offsets[:]))
+        for q in range(4):
+            nc.scalar.dma_start(
+                picked_s1[32 * q : 32 * q + 4, :].bitcast(I32), picked_s0[32 * q + 4 : 32 * q + 8, :].bitcast(I32)
+            )
+        picked_s = [picked_s0, picked_s1]
+
+        windows = [held.tile([P, T], F32, name="window%d" % w) for w in range(WINDOWS)]
+        for w in range(WINDOWS):
+            for c in range(2):
+                nc.vector.memset(windows[w][:, c * (T // 2) : (c + 1) * (T // 2)].bitcast(I32), 0)
+
+        wd_w = held.tile([P, 4 * N], U8, name="wd_w", tag="scales_then_wd", align_bytes=64)
+        nc.sync.dma_start(wd_w[:].bitcast(I32), wd_words[0].rearrange("p n i -> p (n i)").bitcast(I32))
+
+        parted = {}
+
+        def pick_words(j0, j1, tag):
+            pairs = held.tile([P, j1 - j0], U32, name="pairs%d" % j0, tag=tag, align_bytes=64)
+            nc.vector.tensor_copy(pairs[:], table[:].bitcast(U32).indirect(offsets[:, j0 // 16 : j1 // 16]))
+            apart = held.tile([P, 2, 2 * (j1 - j0)], U8, name="apart%d" % j0, align_bytes=64)
+            nc.vector.tensor_copy(apart[:].bitcast(U16), pairs[:].bitcast(U16).rearrange("p (j d) -> p d j", d=2))
+            for j in range(j0, j1, BLOCK):
+                parted[j // BLOCK] = (apart, j - j0)
+
+        wg_q = held.tile([P, 2, R], U32, name="wg_q", align_bytes=64)
+        wg_s = held.tile([P, 2, R], U8, name="wg_s", align_bytes=64)
+
+        def round_wg(copy, raw, width, name):
+            grouped = held.tile([P, width, 4], BF16, name=name, tag=name, align_bytes=64)
+            copy(grouped[:].rearrange("p (c e) i -> p c i e", e=4), raw[:].rearrange("p i (c e) -> p c i e", e=4))
+            return grouped
+
+        def quantize_wg(grouped, a, r0, width):
+            nc.vector.quantize_mx(
+                out=wg_q[:, a, r0 : r0 + width].bitcast(FP8X4),
+                scales=wg_s[:, a, r0 : r0 + width],
+                in_=grouped[:].rearrange("p c i -> p (c i)"),
+            )
+
+        g0 = round_wg(nc.scalar.copy, wg_raw0, R, "wg_bf0")
+        g1a = round_wg(nc.scalar.copy, wg_raw1[0], R // 2, "wg_bf1a")
+        pick_words(0, 384, "pairs_first")
+        quantize_wg(g0, 0, 0, R)
+        g1b = round_wg(nc.vector.tensor_copy, wg_raw1[1], R // 2, "wg_bf1b")
+        quantize_wg(g1a, 1, 0, R // 2)
+        quantize_wg(g1b, 1, R // 2, R // 2)
+        pick_words(384, 640, "wg_bf1b")
+
+        router = held.tile([P, J], F32, name="router", tag="wg_then_router")
+        nc.sync.dma_start(router[:], wgo)
+
+        h_grouped = [held.tile([P, GROUP, 4], BF16, name="h_grouped%d" % g, align_bytes=64) for g in range(GROUPS)]
+        y = [held.tile([P, J], F32, name="y%d" % n) for n in range(N_TILES)]
+        stage = {}
+
+        def products(b):
+            apart, j = parted[b]
+            up = psum.tile([P, R], F32, name="up", bufs=3)
+            gate = psum.tile([P, R], F32, name="gate", bufs=3)
+            for acc, is_gate in ((up, False), (gate, True)):
+                for a in range(2):
+                    nc.tensor.matmul_mx(
+                        out=acc[:],
+                        lhsT=apart[:, a, 2 * j : 2 * (j + BLOCK)].bitcast(FP4X4),
+                        lhsT_scale=picked_s[a][:, b * BLOCK : (b + 1) * BLOCK],
+                        rhs=wg_q[:, a, :].bitcast(FP8X4) if is_gate else wu_w[:, a, :].bitcast(FP4X4),
+                        rhs_scale=wg_s[:, a, :] if is_gate else wu_s[:, a, :],
+                        start=(a == 0),
+                        stop=(a == 1),
+                    )
+            act = ring.tile([P, R], F32, name="act")
+            nc.scalar.activation(act[:], gate[:], SILU)
+            stage[b] = (up, act)
+
+        def hidden(b):
+            up, act = stage[b]
+            h = ring.tile([P, R], BF16, name="h")
+            nc.vector.tensor_tensor(h[:], up[:], act[:], MULT)
+            turned = psum.tile([P, 2, BLOCK], F32, name="turned", tag="bank%d" % (b % 2))
+            words = h[:].bitcast(F32)
+            for u in range(2):
+                nc.tensor.transpose(turned[:, u, :], words[:, u : R // 2 : 2], identity[:])
+            g, j = divmod(b * BLOCK, GROUP)
+            nc.scalar.copy(
+                h_grouped[g][:, j : j + BLOCK, :].bitcast(F32), turned[:].rearrange("p u j -> p j u")
+            )
+            if b + 3 < J // BLOCK:
+                products(b + 3)
+
+        h_mx = {}
+
+        def quantize_h(g):
+            codes = held.tile([P, GROUP], U32, name="h_codes%d" % g, align_bytes=64)
+            scales = held.tile([P, GROUP], U8, name="h_scales%d" % g, align_bytes=64)
+            nc.vector.quantize_mx(
+                out=codes[:].bitcast(FP8X4), scales=scales[:], in_=h_grouped[g][:].rearrange("p j i -> p (j i)")
+            )
+            h_mx[g] = (codes, scales)
+
+        def down(n, g):
+            codes, scales = h_mx[g]
+            acc = psum.tile([P, GROUP], F32, name="acc", tag="bank%d" % (n % 2))
+            nc.tensor.matmul_mx(
+                out=acc[:],
+                lhsT=wd_w[:, 4 * P * n : 4 * P * (n + 1)].bitcast(FP8X4),
+                lhsT_scale=wd_s[:, P * n : P * (n + 1)],
+                rhs=codes[:].bitcast(FP8X4),
+                rhs_scale=scales[:],
+                start=True,
+                stop=True,
+            )
+            nc.scalar.copy(y[n][:, g * GROUP : (g + 1) * GROUP], acc[:])
+
+        def place(n, j0, j1):
+            window = windows[n % WINDOWS]
+            nc.vector.tensor_tensor(
+                window[:].indirect(offsets[:, j0 // 16 : j1 // 16]), y[n][:, j0:j1], router[:, j0:j1], MULT
+            )
+            if j1 == J:
+                nc.sync.dma_start(out[n * P : (n + 1) * P, :], window[:])
+
+        def down_and_place(n, g):
+            down(n, g)
+            place(n, g * GROUP, (g + 1) * GROUP)
+
+        for b in range(3):
+            products(b)
+        for g in range(GROUPS):
+            hidden(2 * g)
+            hidden(2 * g + 1)
+            if g == 0:
+                pick_words(640, J, "wg_bf1b")
+            quantize_h(g)
+            if g > 0:
+                down_and_place(1, g - 1)
+            down_and_place(0, g)
+            if g > 0:
+                down_and_place(2, g - 1)
+                down(3, g - 1)
+        down_and_place(1, GROUPS - 1)
+        down_and_place(2, GROUPS - 1)
+        down(3, GROUPS - 1)
+        place(3, 0, J)

@@ -39,52 +39,46 @@ def tile_list_modp_gsilu_none_kernel(
 
         table_scales = held.tile([P, T], U8, name="table_scales", tag="scales_then_wd", align_bytes=64)
         nc.vector.memset(table_scales[:].bitcast(I32), 0)
-        wg_rows = wg.rearrange("(a p i) r -> a p i r", a=2, i=4)
-        wg_raw0 = held.tile([P, 4, R], F32, name="wg_raw0", tag="wg_then_router")
-        nc.sync.dma_start(wg_raw0[:], wg_rows[0])
-        for q in range(4):
-            nc.sync.dma_start(
-                table_scales[32 * q : 32 * q + 8, :].bitcast(I32),
-                tab_scales[:, 4 * q : 4 * q + 4, :].bitcast(I32),
-            )
         table = held.tile([P, T], I32, name="table")
         nc.sync.dma_start(table[:], tab_words[0].rearrange("p t b -> p (t b)").bitcast(I32))
-        wu_w = held.tile([P, 2, 2 * R], U8, name="wu_w", align_bytes=64)
-        nc.sync.dma_start(wu_w[:].bitcast(I32), wu_words.rearrange("a p b -> p a b").bitcast(I32))
-        wg_raw1 = []
-        for half in range(2):
-            piece = held.tile([P, 4, R // 2], F32, name="wg_raw1_%d" % half)
-            nc.sync.dma_start(piece[:], wg_rows[1][:, :, half * (R // 2) : (half + 1) * (R // 2)])
-            wg_raw1.append(piece)
+        scale_rows = tab_scales.rearrange("a (q r) t -> r q a t", r=4)
+        for r in range(4):
+            nc.sync.dma_start(table_scales[r:P:16, :].bitcast(I32), scale_rows[r].bitcast(I32))
 
-        warm_in = held.tile([P, 1], F32, name="warm_in")
-        nc.gpsimd.memset(warm_in[:], 0.0)
-        warm = held.tile([P, 1], F32, name="warm")
-        nc.scalar.activation(warm[:], warm_in[:], SILU)
+        warm_in = held.tile([P, 1], F32, name="warm_in", tag="warm_then_wu", align_bytes=64)
+        warm_bias = held.tile([P, 1], F32, name="warm_bias", tag="wg_raw0")
+        nc.vector.memset(warm_in[:], 0.0)
+        nc.vector.memset(warm_bias[:], 0.0)
+        warm = held.tile([P, 1], F32, name="warm", tag="wg_raw1")
+        nc.scalar.activation(warm[:], warm_in[:], SILU, bias=warm_bias[:])
+
+        wu_w = held.tile([P, 2, 2 * R], U8, name="wu_w", tag="warm_then_wu", align_bytes=64)
+        nc.sync.dma_start(wu_w[:].bitcast(I32), wu_words.rearrange("a p b -> p a b").bitcast(I32))
+        wg_rows = wg.rearrange("(a p i) (c r) -> a c p i r", a=2, i=4, c=2)
+        wg_raw = []
+        for a in range(2):
+            raw = held.tile([P, 2, 4, R // 2], F32, name="wg_raw%d" % a, tag="wg_raw%d" % a)
+            for c in range(2):
+                nc.sync.dma_start(raw[:, c], wg_rows[a, c])
+            wg_raw.append(raw)
 
         wu_s = held.tile([P, 2, R], U8, name="wu_s", align_bytes=64)
-        wd_s = held.tile([P, N], U8, name="wd_s", align_bytes=64)
-        nc.gpsimd.memset(wu_s[:].bitcast(I32), 0)
-        nc.gpsimd.memset(wd_s[:].bitcast(I32), 0)
+        nc.vector.memset(wu_s[:].bitcast(I32), 0)
         for q in range(4):
-            nc.gpsimd.dma_start(
+            nc.scalar.dma_start(
                 wu_s[32 * q : 32 * q + 4, :, :].bitcast(I32),
                 wu_scales[:, 4 * q : 4 * q + 4, :].rearrange("a r n -> r a n").bitcast(I32),
             )
         identity = held.tile([P, P], F32, name="identity")
         make_identity(nc, identity[:])
-        for q in range(4):
-            nc.gpsimd.dma_start(
-                wd_s[32 * q : 32 * q + 4, :].bitcast(I32), wd_scales[0, 4 * q : 4 * q + 4, :].bitcast(I32)
-            )
 
         picked_s1 = held.tile([P, J], U8, name="picked_s1", align_bytes=64)
         nc.vector.memset(picked_s1[:].bitcast(I32), 0)
         picked_s0 = held.tile([P, J], U8, name="picked_s0", align_bytes=64)
         nc.vector.tensor_copy(picked_s0[:], table_scales[:].indirect(offsets[:]))
         for q in range(4):
-            nc.scalar.dma_start(
-                picked_s1[32 * q : 32 * q + 4, :].bitcast(I32), picked_s0[32 * q + 4 : 32 * q + 8, :].bitcast(I32)
+            nc.sync.dma_start(
+                picked_s1[32 * q : 32 * q + 4, :].bitcast(I32), picked_s0[32 * q + 16 : 32 * q + 20, :].bitcast(I32)
             )
         picked_s = [picked_s0, picked_s1]
 
@@ -92,9 +86,6 @@ def tile_list_modp_gsilu_none_kernel(
         for w in range(WINDOWS):
             for c in range(2):
                 nc.vector.memset(windows[w][:, c * (T // 2) : (c + 1) * (T // 2)].bitcast(I32), 0)
-
-        wd_w = held.tile([P, 4 * N], U8, name="wd_w", tag="scales_then_wd", align_bytes=64)
-        nc.sync.dma_start(wd_w[:].bitcast(I32), wd_words[0].rearrange("p n i -> p (n i)").bitcast(I32))
 
         parted = {}
 
@@ -111,7 +102,7 @@ def tile_list_modp_gsilu_none_kernel(
 
         def round_wg(copy, raw, width, name):
             grouped = held.tile([P, width, 4], BF16, name=name, tag=name, align_bytes=64)
-            copy(grouped[:].rearrange("p (c e) i -> p c i e", e=4), raw[:].rearrange("p i (c e) -> p c i e", e=4))
+            copy(grouped[:].rearrange("p (c e) i -> p c i e", e=4), raw.rearrange("p i (c e) -> p c i e", e=4))
             return grouped
 
         def quantize_wg(grouped, a, r0, width):
@@ -121,19 +112,27 @@ def tile_list_modp_gsilu_none_kernel(
                 in_=grouped[:].rearrange("p c i -> p (c i)"),
             )
 
-        g0 = round_wg(nc.scalar.copy, wg_raw0, R, "wg_bf0")
-        g1a = round_wg(nc.scalar.copy, wg_raw1[0], R // 2, "wg_bf1a")
-        pick_words(0, 384, "pairs_first")
-        quantize_wg(g0, 0, 0, R)
-        g1b = round_wg(nc.vector.tensor_copy, wg_raw1[1], R // 2, "wg_bf1b")
-        quantize_wg(g1a, 1, 0, R // 2)
-        quantize_wg(g1b, 1, R // 2, R // 2)
-        pick_words(384, 640, "wg_bf1b")
+        pick_words(0, GROUP, "scales_then_wd")
+        pick_words(2 * GROUP, J, "scales_then_wd")
+        wd_w = held.tile([P, 4 * N], U8, name="wd_w", tag="scales_then_wd", align_bytes=64)
+        nc.sync.dma_start(wd_w[:].bitcast(I32), wd_words[0].rearrange("p n i -> p (n i)").bitcast(I32))
+        for a in range(2):
+            for c in range(2):
+                grouped = round_wg(nc.scalar.copy, wg_raw[a][:, c], R // 2, "wg_bf%d%d" % (a, c))
+                quantize_wg(grouped, a, c * (R // 2), R // 2)
+        pick_words(GROUP, 2 * GROUP, "wg_bf11")
 
-        router = held.tile([P, J], F32, name="router", tag="wg_then_router")
+        wd_s = held.tile([P, N], U8, name="wd_s", tag="wg_bf00", align_bytes=64)
+        nc.vector.memset(wd_s[:].bitcast(I32), 0)
+        for q in range(4):
+            nc.sync.dma_start(
+                wd_s[32 * q : 32 * q + 4, :].bitcast(I32), wd_scales[0, 4 * q : 4 * q + 4, :].bitcast(I32)
+            )
+
+        router = held.tile([P, J], F32, name="router", tag="wg_raw0")
         nc.sync.dma_start(router[:], wgo)
 
-        h_grouped = [held.tile([P, GROUP, 4], BF16, name="h_grouped%d" % g, align_bytes=64) for g in range(GROUPS)]
+        h_grouped = [held.tile([P, GROUP, 4], BF16, name="h_grouped%d" % g, tag="h_then_window%d" % g, align_bytes=64) for g in range(GROUPS)]
         y = [held.tile([P, J], F32, name="y%d" % n) for n in range(N_TILES)]
         stage = {}
 
@@ -168,8 +167,6 @@ def tile_list_modp_gsilu_none_kernel(
             nc.scalar.copy(
                 h_grouped[g][:, j : j + BLOCK, :].bitcast(F32), turned[:].rearrange("p u j -> p j u")
             )
-            if b + 3 < J // BLOCK:
-                products(b + 3)
 
         h_mx = {}
 
@@ -212,12 +209,12 @@ def tile_list_modp_gsilu_none_kernel(
         for g in range(GROUPS):
             hidden(2 * g)
             hidden(2 * g + 1)
-            if g == 0:
-                pick_words(640, J, "wg_bf1b")
             quantize_h(g)
             if g > 0:
                 down_and_place(1, g - 1)
             down_and_place(0, g)
+            for b in range(2 * g + 3, min(2 * g + 5, J // BLOCK)):
+                products(b)
             if g > 0:
                 down_and_place(2, g - 1)
                 down(3, g - 1)

@@ -45,14 +45,7 @@ def tile_list_modp_gsilu_none_kernel(
         for r in range(4):
             nc.sync.dma_start(table_scales[r:P:16, :].bitcast(I32), scale_rows[r].bitcast(I32))
 
-        warm_in = held.tile([P, 1], F32, name="warm_in", tag="warm_then_wu", align_bytes=64)
-        warm_bias = held.tile([P, 1], F32, name="warm_bias", tag="wg_raw0")
-        nc.vector.memset(warm_in[:], 0.0)
-        nc.vector.memset(warm_bias[:], 0.0)
-        warm = held.tile([P, 1], F32, name="warm", tag="wg_raw1")
-        nc.scalar.activation(warm[:], warm_in[:], SILU, bias=warm_bias[:])
-
-        wu_w = held.tile([P, 2, 2 * R], U8, name="wu_w", tag="warm_then_wu", align_bytes=64)
+        wu_w = held.tile([P, 2, 2 * R], U8, name="wu_w", align_bytes=64)
         nc.sync.dma_start(wu_w[:].bitcast(I32), wu_words.rearrange("a p b -> p a b").bitcast(I32))
         wg_rows = wg.rearrange("(a p i) (c r) -> a c p i r", a=2, i=4, c=2)
         wg_raw = []

@@ -22,7 +22,8 @@ BLOCK = 128
 GROUP = 256
 GROUPS = J // GROUP
 N_TILES = N // P
-WINDOWS = 3
+HALF = 512
+SCALAR_COLS = 192
 
 
 def tile_list_modp_gsilu_none_kernel(
@@ -31,59 +32,59 @@ def tile_list_modp_gsilu_none_kernel(
     nc = tc.nc
     with ExitStack() as ctx:
         held = ctx.enter_context(tc.tile_pool(name="held", bufs=1))
+        shared = ctx.enter_context(tc.tile_pool(name="shared", bufs=1))
         ring = ctx.enter_context(tc.tile_pool(name="ring", bufs=3))
         psum = ctx.enter_context(tc.psum_pool(name="psum", bufs=1))
 
         offsets = held.tile([P, J // 16], U16, name="offsets")
         nc.sync.dma_start(offsets[:], offs)
 
-        table_scales = held.tile([P, T], U8, name="table_scales", tag="scales_then_wd", align_bytes=64)
-        nc.vector.memset(table_scales[:].bitcast(I32), 0)
-        table = held.tile([P, T], I32, name="table")
-        nc.sync.dma_start(table[:], tab_words[0].rearrange("p t b -> p (t b)").bitcast(I32))
+        table_scales = shared.tile([P, T], U8, name="table_scales", offset=512, align_bytes=64)
+        nc.gpsimd.memset(table_scales[:].bitcast(I32), 0)
         scale_rows = tab_scales.rearrange("a (q r) t -> r q a t", r=4)
         for r in range(4):
             nc.sync.dma_start(table_scales[r:P:16, :].bitcast(I32), scale_rows[r].bitcast(I32))
 
+        table = held.tile([P, T], I32, name="table")
+        nc.sync.dma_start(table[:], tab_words[0].rearrange("p t b -> p (t b)").bitcast(I32))
+        wg_rows = wg.rearrange("(a p i) r -> a p i r", a=2, i=4)
+        wg_raw = [held.tile([P, 4, R], F32, name="wg_raw%d" % a, tag="wg_raw%d" % a) for a in range(2)]
+        nc.sync.dma_start(wg_raw[0][:], wg_rows[0])
         wu_w = held.tile([P, 2, 2 * R], U8, name="wu_w", align_bytes=64)
         nc.sync.dma_start(wu_w[:].bitcast(I32), wu_words.rearrange("a p b -> p a b").bitcast(I32))
-        wg_rows = wg.rearrange("(a p i) (c r) -> a c p i r", a=2, i=4, c=2)
-        wg_raw = []
-        for a in range(2):
-            raw = held.tile([P, 2, 4, R // 2], F32, name="wg_raw%d" % a, tag="wg_raw%d" % a)
-            for c in range(2):
-                nc.sync.dma_start(raw[:, c], wg_rows[a, c])
-            wg_raw.append(raw)
+        nc.sync.dma_start(wg_raw[1][:], wg_rows[1])
 
         wu_s = held.tile([P, 2, R], U8, name="wu_s", align_bytes=64)
         nc.vector.memset(wu_s[:].bitcast(I32), 0)
+        wd_s = held.tile([P, N], U8, name="wd_s", align_bytes=64)
+        nc.vector.memset(wd_s[:].bitcast(I32), 0)
         for q in range(4):
-            nc.scalar.dma_start(
+            nc.gpsimd.dma_start(
                 wu_s[32 * q : 32 * q + 4, :, :].bitcast(I32),
                 wu_scales[:, 4 * q : 4 * q + 4, :].rearrange("a r n -> r a n").bitcast(I32),
             )
         identity = held.tile([P, P], F32, name="identity")
         make_identity(nc, identity[:])
+        for q in range(4):
+            nc.gpsimd.dma_start(
+                wd_s[32 * q : 32 * q + 4, :].bitcast(I32), wd_scales[0, 4 * q : 4 * q + 4, :].bitcast(I32)
+            )
 
         picked_s1 = held.tile([P, J], U8, name="picked_s1", align_bytes=64)
         nc.vector.memset(picked_s1[:].bitcast(I32), 0)
         picked_s0 = held.tile([P, J], U8, name="picked_s0", align_bytes=64)
         nc.vector.tensor_copy(picked_s0[:], table_scales[:].indirect(offsets[:]))
-        for q in range(4):
-            nc.sync.dma_start(
-                picked_s1[32 * q : 32 * q + 4, :].bitcast(I32), picked_s0[32 * q + 16 : 32 * q + 20, :].bitcast(I32)
-            )
+        nc.scalar.dma_start(picked_s1[0 : P - 16, :].bitcast(I32), picked_s0[16:P, :].bitcast(I32))
         picked_s = [picked_s0, picked_s1]
 
-        windows = [held.tile([P, T], F32, name="window%d" % w) for w in range(WINDOWS)]
-        for w in range(WINDOWS):
+        windows = [held.tile([P, T], F32, name="window%d" % w) for w in range(2)]
+        for w in range(2):
             for c in range(2):
                 nc.vector.memset(windows[w][:, c * (T // 2) : (c + 1) * (T // 2)].bitcast(I32), 0)
 
         parted = {}
 
-        def pick_words(j0, j1, tag):
-            pairs = held.tile([P, j1 - j0], U32, name="pairs%d" % j0, tag=tag, align_bytes=64)
+        def pick_words(j0, j1, pairs):
             nc.vector.tensor_copy(pairs[:], table[:].bitcast(U32).indirect(offsets[:, j0 // 16 : j1 // 16]))
             apart = held.tile([P, 2, 2 * (j1 - j0)], U8, name="apart%d" % j0, align_bytes=64)
             nc.vector.tensor_copy(apart[:].bitcast(U16), pairs[:].bitcast(U16).rearrange("p (j d) -> p d j", d=2))
@@ -93,125 +94,120 @@ def tile_list_modp_gsilu_none_kernel(
         wg_q = held.tile([P, 2, R], U32, name="wg_q", align_bytes=64)
         wg_s = held.tile([P, 2, R], U8, name="wg_s", align_bytes=64)
 
-        def round_wg(copy, raw, width, name):
-            grouped = held.tile([P, width, 4], BF16, name=name, tag=name, align_bytes=64)
-            copy(grouped[:].rearrange("p (c e) i -> p c i e", e=4), raw.rearrange("p i (c e) -> p c i e", e=4))
-            return grouped
+        def round_wg(copy, grouped, a, c0, c1):
+            copy(
+                grouped[:, c0:c1, :].rearrange("p (c e) i -> p c i e", e=4),
+                wg_raw[a][:, :, c0:c1].rearrange("p i (c e) -> p c i e", e=4),
+            )
 
-        def quantize_wg(grouped, a, r0, width):
+        def quantize_wg(grouped, a):
             nc.vector.quantize_mx(
-                out=wg_q[:, a, r0 : r0 + width].bitcast(FP8X4),
-                scales=wg_s[:, a, r0 : r0 + width],
-                in_=grouped[:].rearrange("p c i -> p (c i)"),
+                out=wg_q[:, a, :].bitcast(FP8X4), scales=wg_s[:, a, :], in_=grouped[:].rearrange("p c i -> p (c i)")
             )
 
-        pick_words(0, GROUP, "scales_then_wd")
-        pick_words(2 * GROUP, J, "scales_then_wd")
-        wd_w = held.tile([P, 4 * N], U8, name="wd_w", tag="scales_then_wd", align_bytes=64)
+        for c in range(2):
+            pairs = shared.tile([P, 384], U32, name="pairs%d" % c, offset=1536 * c, align_bytes=64)
+            pick_words(GROUP + 384 * c, GROUP + 384 * (c + 1), pairs)
+        wd_w = shared.tile([P, 4 * N], U8, name="wd_w", offset=0, align_bytes=64)
         nc.sync.dma_start(wd_w[:].bitcast(I32), wd_words[0].rearrange("p n i -> p (n i)").bitcast(I32))
-        for a in range(2):
-            for c in range(2):
-                grouped = round_wg(nc.scalar.copy, wg_raw[a][:, c], R // 2, "wg_bf%d%d" % (a, c))
-                quantize_wg(grouped, a, c * (R // 2), R // 2)
-        pick_words(GROUP, 2 * GROUP, "wg_bf11")
 
-        wd_s = held.tile([P, N], U8, name="wd_s", tag="wg_bf00", align_bytes=64)
-        nc.vector.memset(wd_s[:].bitcast(I32), 0)
-        for q in range(4):
-            nc.sync.dma_start(
-                wd_s[32 * q : 32 * q + 4, :].bitcast(I32), wd_scales[0, 4 * q : 4 * q + 4, :].bitcast(I32)
-            )
+        wg_bf = [held.tile([P, R, 4], BF16, name="wg_bf%d" % a, tag="wg_bf%d" % a, align_bytes=64) for a in range(2)]
+        round_wg(nc.scalar.copy, wg_bf[0], 0, 0, R)
+        quantize_wg(wg_bf[0], 0)
+        round_wg(nc.scalar.copy, wg_bf[1], 1, 0, SCALAR_COLS)
+        round_wg(nc.vector.tensor_copy, wg_bf[1], 1, SCALAR_COLS, R)
+        quantize_wg(wg_bf[1], 1)
+        pairs = held.tile([P, 256], U32, name="pairs2", tag="wg_bf1", align_bytes=64)
+        pick_words(0, GROUP, pairs)
 
         router = held.tile([P, J], F32, name="router", tag="wg_raw0")
         nc.sync.dma_start(router[:], wgo)
 
-        h_grouped = [held.tile([P, GROUP, 4], BF16, name="h_grouped%d" % g, tag="h_then_window%d" % g, align_bytes=64) for g in range(GROUPS)]
+        h_codes = held.tile([P, J], U32, name="h_codes", align_bytes=64)
+        h_scales = held.tile([P, J], U8, name="h_scales", align_bytes=64)
         y = [held.tile([P, J], F32, name="y%d" % n) for n in range(N_TILES)]
-        stage = {}
 
-        def products(b):
+        def product(b, acc, words, scales, dtype):
             apart, j = parted[b]
-            up = psum.tile([P, R], F32, name="up", bufs=3)
-            gate = psum.tile([P, R], F32, name="gate", bufs=3)
-            for acc, is_gate in ((up, False), (gate, True)):
-                for a in range(2):
-                    nc.tensor.matmul_mx(
-                        out=acc[:],
-                        lhsT=apart[:, a, 2 * j : 2 * (j + BLOCK)].bitcast(FP4X4),
-                        lhsT_scale=picked_s[a][:, b * BLOCK : (b + 1) * BLOCK],
-                        rhs=wg_q[:, a, :].bitcast(FP8X4) if is_gate else wu_w[:, a, :].bitcast(FP4X4),
-                        rhs_scale=wg_s[:, a, :] if is_gate else wu_s[:, a, :],
-                        start=(a == 0),
-                        stop=(a == 1),
-                    )
+            for a in range(2):
+                nc.tensor.matmul_mx(
+                    out=acc[:],
+                    lhsT=apart[:, a, 2 * j : 2 * (j + BLOCK)].bitcast(FP4X4),
+                    lhsT_scale=picked_s[a][:, b * BLOCK : (b + 1) * BLOCK],
+                    rhs=words[:, a, :].bitcast(dtype),
+                    rhs_scale=scales[:, a, :],
+                    start=(a == 0),
+                    stop=(a == 1),
+                )
+
+        def by_word_half(ap):
+            return ap.rearrange("t (p u e) -> t u p e", u=2, e=2)
+
+        def as_laid(ap):
+            return ap.rearrange("t (u p e) -> t u p e", u=2, e=2)
+
+        def hidden(b, turned):
+            up = psum.tile([P, R], F32, name="up", bufs=4)
+            product(b, up, wu_w, wu_s, FP4X4)
+            gate = psum.tile([P, R], F32, name="gate", bufs=2)
+            product(b, gate, wg_q, wg_s, FP8X4)
             act = ring.tile([P, R], F32, name="act")
-            nc.scalar.activation(act[:], gate[:], SILU)
-            stage[b] = (up, act)
-
-        def hidden(b):
-            up, act = stage[b]
+            nc.scalar.activation(as_laid(act[:]), by_word_half(gate[:]), SILU)
             h = ring.tile([P, R], BF16, name="h")
-            nc.vector.tensor_tensor(h[:], up[:], act[:], MULT)
-            turned = psum.tile([P, 2, BLOCK], F32, name="turned", tag="bank%d" % (b % 2))
+            nc.vector.tensor_tensor(as_laid(h[:]), by_word_half(up[:]), as_laid(act[:]), MULT)
             words = h[:].bitcast(F32)
+            j = b * BLOCK % GROUP
             for u in range(2):
-                nc.tensor.transpose(turned[:, u, :], words[:, u : R // 2 : 2], identity[:])
-            g, j = divmod(b * BLOCK, GROUP)
-            nc.scalar.copy(
-                h_grouped[g][:, j : j + BLOCK, :].bitcast(F32), turned[:].rearrange("p u j -> p j u")
-            )
-
-        h_mx = {}
+                nc.tensor.transpose(turned[:, u, j : j + BLOCK], words[:, u * P : (u + 1) * P], identity[:])
 
         def quantize_h(g):
-            codes = held.tile([P, GROUP], U32, name="h_codes%d" % g, align_bytes=64)
-            scales = held.tile([P, GROUP], U8, name="h_scales%d" % g, align_bytes=64)
+            turned = psum.tile([P, 2, GROUP], F32, name="turned", tag="bank0")
+            hidden(2 * g, turned)
+            hidden(2 * g + 1, turned)
+            grouped = ring.tile([P, GROUP, 4], BF16, name="h_grouped", align_bytes=64)
+            nc.scalar.copy(grouped[:].bitcast(F32), turned[:].rearrange("p u j -> p j u"))
             nc.vector.quantize_mx(
-                out=codes[:].bitcast(FP8X4), scales=scales[:], in_=h_grouped[g][:].rearrange("p j i -> p (j i)")
+                out=h_codes[:, g * GROUP : (g + 1) * GROUP].bitcast(FP8X4),
+                scales=h_scales[:, g * GROUP : (g + 1) * GROUP],
+                in_=grouped[:].rearrange("p j i -> p (j i)"),
             )
-            h_mx[g] = (codes, scales)
 
-        def down(n, g):
-            codes, scales = h_mx[g]
-            acc = psum.tile([P, GROUP], F32, name="acc", tag="bank%d" % (n % 2))
+        def down(n, j0, j1, bank):
+            acc = psum.tile([P, j1 - j0], F32, name="acc", tag="bank%d" % bank)
             nc.tensor.matmul_mx(
                 out=acc[:],
                 lhsT=wd_w[:, 4 * P * n : 4 * P * (n + 1)].bitcast(FP8X4),
                 lhsT_scale=wd_s[:, P * n : P * (n + 1)],
-                rhs=codes[:].bitcast(FP8X4),
-                rhs_scale=scales[:],
+                rhs=h_codes[:, j0:j1].bitcast(FP8X4),
+                rhs_scale=h_scales[:, j0:j1],
                 start=True,
                 stop=True,
             )
-            nc.scalar.copy(y[n][:, g * GROUP : (g + 1) * GROUP], acc[:])
+            nc.scalar.copy(y[n][:, j0:j1], acc[:])
 
         def place(n, j0, j1):
-            window = windows[n % WINDOWS]
+            window = windows[n % 2]
             nc.vector.tensor_tensor(
                 window[:].indirect(offsets[:, j0 // 16 : j1 // 16]), y[n][:, j0:j1], router[:, j0:j1], MULT
             )
-            if j1 == J:
-                nc.sync.dma_start(out[n * P : (n + 1) * P, :], window[:])
 
-        def down_and_place(n, g):
-            down(n, g)
-            place(n, g * GROUP, (g + 1) * GROUP)
+        def store(n):
+            nc.sync.dma_start(out[n * P : (n + 1) * P, :], windows[n % 2][:])
 
-        for b in range(3):
-            products(b)
-        for g in range(GROUPS):
-            hidden(2 * g)
-            hidden(2 * g + 1)
+        for g in (1, 2, 3, 0):
             quantize_h(g)
-            if g > 0:
-                down_and_place(1, g - 1)
-            down_and_place(0, g)
-            for b in range(2 * g + 3, min(2 * g + 5, J // BLOCK)):
-                products(b)
-            if g > 0:
-                down_and_place(2, g - 1)
-                down(3, g - 1)
-        down_and_place(1, GROUPS - 1)
-        down_and_place(2, GROUPS - 1)
-        down(3, GROUPS - 1)
-        place(3, 0, J)
+            if g == 0:
+                down(1, J - GROUP, J, 0)
+                place(1, J - GROUP, J)
+            down(0, g * GROUP, (g + 1) * GROUP, 1)
+            place(0, g * GROUP, (g + 1) * GROUP)
+        store(0)
+        down(1, GROUP, J - GROUP, 0)
+        down(1, 0, GROUP, 1)
+        place(1, 0, J - GROUP)
+        store(1)
+        for n in range(2, N_TILES):
+            for c in range(2):
+                down(n, c * HALF, (c + 1) * HALF, c)
+            place(n, 0, J)
+            store(n)

@@ -23,7 +23,6 @@ GROUP = 256
 GROUPS = J // GROUP
 N_TILES = N // P
 HALF = 512
-SCALAR_COLS = 192
 
 
 def tile_list_modp_gsilu_none_kernel(
@@ -40,24 +39,29 @@ def tile_list_modp_gsilu_none_kernel(
         nc.sync.dma_start(offsets[:], offs)
 
         table_scales = shared.tile([P, T], U8, name="table_scales", offset=512, align_bytes=64)
-        nc.gpsimd.memset(table_scales[:].bitcast(I32), 0)
-        scale_rows = tab_scales.rearrange("a (q r) t -> r q a t", r=4)
-        for r in range(4):
-            nc.sync.dma_start(table_scales[r:P:16, :].bitcast(I32), scale_rows[r].bitcast(I32))
+        scale_rows = tab_scales.rearrange("a (q r) t -> q a r t", r=4)
+        for q in range(4):
+            nc.sync.dma_start(table_scales[32 * q + 24 : 32 * q + 32, :].bitcast(I32), scale_rows[q].bitcast(I32))
+            nc.vector.memset(table_scales[32 * q : 32 * q + 24, :].bitcast(I32), 0)
 
         table = held.tile([P, T], I32, name="table")
         nc.sync.dma_start(table[:], tab_words[0].rearrange("p t b -> p (t b)").bitcast(I32))
         wg_rows = wg.rearrange("(a p i) r -> a p i r", a=2, i=4)
-        wg_raw = [held.tile([P, 4, R], F32, name="wg_raw%d" % a, tag="wg_raw%d" % a) for a in range(2)]
-        nc.sync.dma_start(wg_raw[0][:], wg_rows[0])
+        wg_raw = {}
+
+        def load_wg(a):
+            for c in range(2):
+                raw = held.tile([P, 4, R // 2], F32, name="wg_raw", tag="stage%d%d" % (a, c))
+                nc.sync.dma_start(raw[:], wg_rows[a][:, :, c * (R // 2) : (c + 1) * (R // 2)])
+                wg_raw[a, c] = raw
+
+        load_wg(0)
         wu_w = held.tile([P, 2, 2 * R], U8, name="wu_w", align_bytes=64)
         nc.sync.dma_start(wu_w[:].bitcast(I32), wu_words.rearrange("a p b -> p a b").bitcast(I32))
-        nc.sync.dma_start(wg_raw[1][:], wg_rows[1])
+        load_wg(1)
 
         wu_s = held.tile([P, 2, R], U8, name="wu_s", align_bytes=64)
-        nc.vector.memset(wu_s[:].bitcast(I32), 0)
-        wd_s = held.tile([P, N], U8, name="wd_s", align_bytes=64)
-        nc.vector.memset(wd_s[:].bitcast(I32), 0)
+        nc.gpsimd.memset(wu_s[:].bitcast(I32), 0)
         for q in range(4):
             nc.gpsimd.dma_start(
                 wu_s[32 * q : 32 * q + 4, :, :].bitcast(I32),
@@ -65,22 +69,22 @@ def tile_list_modp_gsilu_none_kernel(
             )
         identity = held.tile([P, P], F32, name="identity")
         make_identity(nc, identity[:])
-        for q in range(4):
-            nc.gpsimd.dma_start(
-                wd_s[32 * q : 32 * q + 4, :].bitcast(I32), wd_scales[0, 4 * q : 4 * q + 4, :].bitcast(I32)
-            )
 
-        picked_s1 = held.tile([P, J], U8, name="picked_s1", align_bytes=64)
-        nc.vector.memset(picked_s1[:].bitcast(I32), 0)
-        picked_s0 = held.tile([P, J], U8, name="picked_s0", align_bytes=64)
-        nc.vector.tensor_copy(picked_s0[:], table_scales[:].indirect(offsets[:]))
-        nc.scalar.dma_start(picked_s1[0 : P - 16, :].bitcast(I32), picked_s0[16:P, :].bitcast(I32))
-        picked_s = [picked_s0, picked_s1]
+        planes = held.tile([P, 2, J], U8, name="planes", align_bytes=64)
+        nc.gpsimd.memset(planes[96:P].bitcast(I32), 0)
+        picked = held.tile([P, J], U8, name="picked", align_bytes=64)
+        nc.vector.tensor_copy(picked[:], table_scales[:].indirect(offsets[:]))
+        for a in range(2):
+            shift = 24 + 4 * a
+            nc.gpsimd.dma_start(planes[0 : P - shift, a, :].bitcast(I32), picked[shift:P, :].bitcast(I32))
 
-        windows = [held.tile([P, T], F32, name="window%d" % w) for w in range(2)]
-        for w in range(2):
-            for c in range(2):
-                nc.vector.memset(windows[w][:, c * (T // 2) : (c + 1) * (T // 2)].bitcast(I32), 0)
+        def zeroed_window(tag):
+            window = held.tile([P, T], F32, name="window", tag=tag)
+            for c in range(4):
+                nc.vector.memset(window[:, c * (T // 4) : (c + 1) * (T // 4)].bitcast(I32), 0)
+            return window
+
+        windows = [zeroed_window("window0")]
 
         parted = {}
 
@@ -94,33 +98,35 @@ def tile_list_modp_gsilu_none_kernel(
         wg_q = held.tile([P, 2, R], U32, name="wg_q", align_bytes=64)
         wg_s = held.tile([P, 2, R], U8, name="wg_s", align_bytes=64)
 
-        def round_wg(copy, grouped, a, c0, c1):
-            copy(
-                grouped[:, c0:c1, :].rearrange("p (c e) i -> p c i e", e=4),
-                wg_raw[a][:, :, c0:c1].rearrange("p i (c e) -> p c i e", e=4),
-            )
+        def round_wg(copy, grouped, raw):
+            copy(grouped.rearrange("p (c e) i -> p c i e", e=4), raw.rearrange("p i (c e) -> p c i e", e=4))
 
-        def quantize_wg(grouped, a):
+        def quantize_wg(grouped, a, c0, c1):
             nc.vector.quantize_mx(
-                out=wg_q[:, a, :].bitcast(FP8X4), scales=wg_s[:, a, :], in_=grouped[:].rearrange("p c i -> p (c i)")
+                out=wg_q[:, a, c0:c1].bitcast(FP8X4), scales=wg_s[:, a, c0:c1], in_=grouped.rearrange("p c i -> p (c i)")
             )
 
-        for c in range(2):
-            pairs = shared.tile([P, 384], U32, name="pairs%d" % c, offset=1536 * c, align_bytes=64)
-            pick_words(GROUP + 384 * c, GROUP + 384 * (c + 1), pairs)
+        for j0, j1 in ((0, 384), (384, J)):
+            pairs = shared.tile([P, j1 - j0], U32, name="pairs%d" % j0, offset=4 * j0, align_bytes=64)
+            pick_words(j0, j1, pairs)
         wd_w = shared.tile([P, 4 * N], U8, name="wd_w", offset=0, align_bytes=64)
         nc.sync.dma_start(wd_w[:].bitcast(I32), wd_words[0].rearrange("p n i -> p (n i)").bitcast(I32))
 
-        wg_bf = [held.tile([P, R, 4], BF16, name="wg_bf%d" % a, tag="wg_bf%d" % a, align_bytes=64) for a in range(2)]
-        round_wg(nc.scalar.copy, wg_bf[0], 0, 0, R)
-        quantize_wg(wg_bf[0], 0)
-        round_wg(nc.scalar.copy, wg_bf[1], 1, 0, SCALAR_COLS)
-        round_wg(nc.vector.tensor_copy, wg_bf[1], 1, SCALAR_COLS, R)
-        quantize_wg(wg_bf[1], 1)
-        pairs = held.tile([P, 256], U32, name="pairs2", tag="wg_bf1", align_bytes=64)
-        pick_words(0, GROUP, pairs)
+        for a in range(2):
+            for c in range(2):
+                copy = nc.vector.tensor_copy if (a, c) == (1, 1) else nc.scalar.copy
+                grouped = held.tile([P, R // 2, 4], BF16, name="wg_bf", tag="wg_bf%d%d" % (a, c), align_bytes=64)
+                round_wg(copy, grouped[:], wg_raw[a, c][:])
+                quantize_wg(grouped[:], a, c * (R // 2), (c + 1) * (R // 2))
 
-        router = held.tile([P, J], F32, name="router", tag="wg_raw0")
+        wd_s = held.tile([P, N], U8, name="wd_s", tag="wg_bf00", align_bytes=64)
+        nc.vector.memset(wd_s[:].bitcast(I32), 0)
+        for q in range(4):
+            nc.sync.dma_start(
+                wd_s[32 * q : 32 * q + 4, :].bitcast(I32), wd_scales[0, 4 * q : 4 * q + 4, :].bitcast(I32)
+            )
+
+        router = held.tile([P, J], F32, name="router", tag="stage01")
         nc.sync.dma_start(router[:], wgo)
 
         h_codes = held.tile([P, J], U32, name="h_codes", align_bytes=64)
@@ -133,7 +139,7 @@ def tile_list_modp_gsilu_none_kernel(
                 nc.tensor.matmul_mx(
                     out=acc[:],
                     lhsT=apart[:, a, 2 * j : 2 * (j + BLOCK)].bitcast(FP4X4),
-                    lhsT_scale=picked_s[a][:, b * BLOCK : (b + 1) * BLOCK],
+                    lhsT_scale=planes[:, a, b * BLOCK : (b + 1) * BLOCK],
                     rhs=words[:, a, :].bitcast(dtype),
                     rhs_scale=scales[:, a, :],
                     start=(a == 0),
@@ -186,28 +192,30 @@ def tile_list_modp_gsilu_none_kernel(
             nc.scalar.copy(y[n][:, j0:j1], acc[:])
 
         def place(n, j0, j1):
-            window = windows[n % 2]
+            window = windows[n % 3]
             nc.vector.tensor_tensor(
                 window[:].indirect(offsets[:, j0 // 16 : j1 // 16]), y[n][:, j0:j1], router[:, j0:j1], MULT
             )
 
         def store(n):
-            nc.sync.dma_start(out[n * P : (n + 1) * P, :], windows[n % 2][:])
+            nc.sync.dma_start(out[n * P : (n + 1) * P, :], windows[n % 3][:])
 
-        for g in (1, 2, 3, 0):
+        for g in range(GROUPS):
             quantize_h(g)
-            if g == 0:
-                down(1, J - GROUP, J, 0)
-                place(1, J - GROUP, J)
+            if g == 1:
+                windows.append(zeroed_window("stage10"))
+            if g > 0:
+                down(1, (g - 1) * GROUP, g * GROUP, 0)
+                place(1, (g - 1) * GROUP, g * GROUP)
             down(0, g * GROUP, (g + 1) * GROUP, 1)
             place(0, g * GROUP, (g + 1) * GROUP)
         store(0)
-        down(1, GROUP, J - GROUP, 0)
-        down(1, 0, GROUP, 1)
-        place(1, 0, J - GROUP)
+        down(1, J - GROUP, J, 0)
+        place(1, J - GROUP, J)
         store(1)
+        windows.append(zeroed_window("stage11"))
         for n in range(2, N_TILES):
             for c in range(2):
-                down(n, c * HALF, (c + 1) * HALF, c)
+                down(n, c * HALF, (c + 1) * HALF, 1 - c)
             place(n, 0, J)
             store(n)

@@ -76,7 +76,7 @@ def tile_list_modp_gsilu_none_kernel(
         nc.vector.tensor_copy(picked[:], table_scales[:].indirect(offsets[:]))
         for a in range(2):
             shift = 24 + 4 * a
-            nc.gpsimd.dma_start(planes[0 : P - shift, a, :].bitcast(I32), picked[shift:P, :].bitcast(I32))
+            nc.scalar.dma_start(planes[0 : P - shift, a, :].bitcast(I32), picked[shift:P, :].bitcast(I32))
 
         def zeroed_window(tag):
             window = held.tile([P, T], F32, name="window", tag=tag)
@@ -153,10 +153,10 @@ def tile_list_modp_gsilu_none_kernel(
             return ap.rearrange("t (u p e) -> t u p e", u=2, e=2)
 
         def hidden(b, turned):
-            up = psum.tile([P, R], F32, name="up", bufs=4)
-            product(b, up, wu_w, wu_s, FP4X4)
-            gate = psum.tile([P, R], F32, name="gate", bufs=2)
+            gate = psum.tile([P, R], F32, name="gate", bufs=3)
             product(b, gate, wg_q, wg_s, FP8X4)
+            up = psum.tile([P, R], F32, name="up", bufs=3)
+            product(b, up, wu_w, wu_s, FP4X4)
             act = ring.tile([P, R], F32, name="act")
             nc.scalar.activation(as_laid(act[:]), by_word_half(gate[:]), SILU)
             h = ring.tile([P, R], BF16, name="h")

@@ -39,11 +39,10 @@ def tile_list_modp_gsilu_none_kernel(
         nc.sync.dma_start(offsets[:], offs)
 
         table_scales = shared.tile([P, T], U8, name="table_scales", offset=512, align_bytes=64)
-        scale_rows = tab_scales.rearrange("a (q r) t -> q a r t", r=4)
-        for q in range(4):
-            nc.sync.dma_start(table_scales[32 * q + 24 : 32 * q + 32, :].bitcast(I32), scale_rows[q].bitcast(I32))
-            nc.vector.memset(table_scales[32 * q : 32 * q + 24, :].bitcast(I32), 0)
+        nc.sync.dma_start(table_scales[96:P, :].bitcast(I32), tab_scales.rearrange("a s t -> s a t").bitcast(I32))
 
+        wu_w = held.tile([P, 2, 2 * R], U8, name="wu_w", align_bytes=64)
+        nc.sync.dma_start(wu_w[:].bitcast(I32), wu_words.rearrange("a p b -> p a b").bitcast(I32))
         table = held.tile([P, T], I32, name="table")
         nc.sync.dma_start(table[:], tab_words[0].rearrange("p t b -> p (t b)").bitcast(I32))
         wg_rows = wg.rearrange("(a p i) r -> a p i r", a=2, i=4)
@@ -56,10 +55,13 @@ def tile_list_modp_gsilu_none_kernel(
                 wg_raw[a, c] = raw
 
         load_wg(0)
-        wu_w = held.tile([P, 2, 2 * R], U8, name="wu_w", align_bytes=64)
-        nc.sync.dma_start(wu_w[:].bitcast(I32), wu_words.rearrange("a p b -> p a b").bitcast(I32))
         load_wg(1)
 
+        warm = held.tile([P, 2, 8], F32, name="warm")
+        nc.gpsimd.memset(warm[:, 0, :], 0.0)
+        nc.scalar.activation(warm[:, 1, :], warm[:, 0, :], SILU)
+        identity = held.tile([P, P], F32, name="identity")
+        make_identity(nc, identity[:])
         wu_s = held.tile([P, 2, R], U8, name="wu_s", align_bytes=64)
         nc.gpsimd.memset(wu_s[:].bitcast(I32), 0)
         for q in range(4):
@@ -67,22 +69,22 @@ def tile_list_modp_gsilu_none_kernel(
                 wu_s[32 * q : 32 * q + 4, :, :].bitcast(I32),
                 wu_scales[:, 4 * q : 4 * q + 4, :].rearrange("a r n -> r a n").bitcast(I32),
             )
-        identity = held.tile([P, P], F32, name="identity")
-        make_identity(nc, identity[:])
-
-        planes = held.tile([P, 2, J], U8, name="planes", align_bytes=64)
-        nc.gpsimd.memset(planes[96:P].bitcast(I32), 0)
-        picked = held.tile([P, J], U8, name="picked", align_bytes=64)
-        nc.vector.tensor_copy(picked[:], table_scales[:].indirect(offsets[:]))
-        for a in range(2):
-            shift = 24 + 4 * a
-            nc.scalar.dma_start(planes[0 : P - shift, a, :].bitcast(I32), picked[shift:P, :].bitcast(I32))
 
         def zeroed_window(tag):
             window = held.tile([P, T], F32, name="window", tag=tag)
             for c in range(4):
                 nc.vector.memset(window[:, c * (T // 4) : (c + 1) * (T // 4)].bitcast(I32), 0)
             return window
+
+        nc.vector.memset(table_scales[0:96, :].bitcast(I32), 0)
+        planes = held.tile([P, 2, J], U8, name="planes", align_bytes=64)
+        nc.vector.memset(planes[:].bitcast(I32), 0)
+        picked = held.tile([P, J], U8, name="picked", align_bytes=64)
+        nc.vector.tensor_copy(picked[:], table_scales[:].indirect(offsets[:]))
+        for q in range(4):
+            nc.scalar.dma_start(
+                planes[32 * q : 32 * q + 4].bitcast(I32), picked[96 + 8 * q : 96 + 8 * q + 8, :].bitcast(I32)
+            )
 
         windows = [zeroed_window("window0")]
 

@@ -23,6 +23,8 @@ GROUP = 256
 GROUPS = J // GROUP
 N_TILES = N // P
 HALF = 512
+WIDE = R // 2
+LEAD = 0
 
 
 def tile_list_modp_gsilu_none_kernel(
@@ -41,20 +43,19 @@ def tile_list_modp_gsilu_none_kernel(
         table_scales = shared.tile([P, T], U8, name="table_scales", offset=512, align_bytes=64)
         nc.sync.dma_start(table_scales[96:P, :].bitcast(I32), tab_scales.rearrange("a s t -> s a t").bitcast(I32))
 
-        wu_w = held.tile([P, 2, 2 * R], U8, name="wu_w", align_bytes=64)
-        nc.sync.dma_start(wu_w[:].bitcast(I32), wu_words.rearrange("a p b -> p a b").bitcast(I32))
         table = held.tile([P, T], I32, name="table")
         nc.sync.dma_start(table[:], tab_words[0].rearrange("p t b -> p (t b)").bitcast(I32))
         wg_rows = wg.rearrange("(a p i) r -> a p i r", a=2, i=4)
-        wg_raw = {}
+        wg_raw = []
 
         def load_wg(a):
-            for c in range(2):
-                raw = held.tile([P, 4, R // 2], F32, name="wg_raw", tag="stage%d%d" % (a, c))
-                nc.sync.dma_start(raw[:], wg_rows[a][:, :, c * (R // 2) : (c + 1) * (R // 2)])
-                wg_raw[a, c] = raw
+            raw = held.tile([P, 4, R], F32, name="wg_raw", tag="stage%d" % a, align_bytes=64)
+            nc.sync.dma_start(raw[:], wg_rows[a])
+            wg_raw.append(raw)
 
         load_wg(0)
+        wu_w = held.tile([P, 2, 2 * R], U8, name="wu_w", align_bytes=64)
+        nc.sync.dma_start(wu_w[:].bitcast(I32), wu_words.rearrange("a p b -> p a b").bitcast(I32))
         load_wg(1)
 
         warm = held.tile([P, 2, 8], F32, name="warm")
@@ -62,6 +63,7 @@ def tile_list_modp_gsilu_none_kernel(
         nc.scalar.activation(warm[:, 1, :], warm[:, 0, :], SILU)
         identity = held.tile([P, P], F32, name="identity")
         make_identity(nc, identity[:])
+        planes = held.tile([P, 2, J], U8, name="planes", align_bytes=64)
         wu_s = held.tile([P, 2, R], U8, name="wu_s", align_bytes=64)
         nc.gpsimd.memset(wu_s[:].bitcast(I32), 0)
         for q in range(4):
@@ -71,13 +73,12 @@ def tile_list_modp_gsilu_none_kernel(
             )
 
         def zeroed_window(tag):
-            window = held.tile([P, T], F32, name="window", tag=tag)
+            window = held.tile([P, T], F32, name="window", tag=tag, align_bytes=64)
             for c in range(4):
                 nc.vector.memset(window[:, c * (T // 4) : (c + 1) * (T // 4)].bitcast(I32), 0)
             return window
 
         nc.vector.memset(table_scales[0:96, :].bitcast(I32), 0)
-        planes = held.tile([P, 2, J], U8, name="planes", align_bytes=64)
         nc.vector.memset(planes[:].bitcast(I32), 0)
         picked = held.tile([P, J], U8, name="picked", align_bytes=64)
         nc.vector.tensor_copy(picked[:], table_scales[:].indirect(offsets[:]))
@@ -100,14 +101,6 @@ def tile_list_modp_gsilu_none_kernel(
         wg_q = held.tile([P, 2, R], U32, name="wg_q", align_bytes=64)
         wg_s = held.tile([P, 2, R], U8, name="wg_s", align_bytes=64)
 
-        def round_wg(copy, grouped, raw):
-            copy(grouped.rearrange("p (c e) i -> p c i e", e=4), raw.rearrange("p i (c e) -> p c i e", e=4))
-
-        def quantize_wg(grouped, a, c0, c1):
-            nc.vector.quantize_mx(
-                out=wg_q[:, a, c0:c1].bitcast(FP8X4), scales=wg_s[:, a, c0:c1], in_=grouped.rearrange("p c i -> p (c i)")
-            )
-
         for j0, j1 in ((0, 384), (384, J)):
             pairs = shared.tile([P, j1 - j0], U32, name="pairs%d" % j0, offset=4 * j0, align_bytes=64)
             pick_words(j0, j1, pairs)
@@ -115,11 +108,18 @@ def tile_list_modp_gsilu_none_kernel(
         nc.sync.dma_start(wd_w[:].bitcast(I32), wd_words[0].rearrange("p n i -> p (n i)").bitcast(I32))
 
         for a in range(2):
-            for c in range(2):
+            for c in (a, 1 - a):
                 copy = nc.vector.tensor_copy if (a, c) == (1, 1) else nc.scalar.copy
-                grouped = held.tile([P, R // 2, 4], BF16, name="wg_bf", tag="wg_bf%d%d" % (a, c), align_bytes=64)
-                round_wg(copy, grouped[:], wg_raw[a, c][:])
-                quantize_wg(grouped[:], a, c * (R // 2), (c + 1) * (R // 2))
+                grouped = held.tile([P, WIDE, 4], BF16, name="wg_bf", tag="wg_bf%d%d" % (a, c), align_bytes=64)
+                copy(
+                    grouped[:].rearrange("p (c e) i -> p c i e", e=4),
+                    wg_raw[a][:, :, c * WIDE : (c + 1) * WIDE].rearrange("p i (c e) -> p c i e", e=4),
+                )
+                nc.vector.quantize_mx(
+                    out=wg_q[:, a, c * WIDE : (c + 1) * WIDE].bitcast(FP8X4),
+                    scales=wg_s[:, a, c * WIDE : (c + 1) * WIDE],
+                    in_=grouped[:].rearrange("p c i -> p (c i)"),
+                )
 
         wd_s = held.tile([P, N], U8, name="wd_s", tag="wg_bf00", align_bytes=64)
         nc.vector.memset(wd_s[:].bitcast(I32), 0)
@@ -128,22 +128,22 @@ def tile_list_modp_gsilu_none_kernel(
                 wd_s[32 * q : 32 * q + 4, :].bitcast(I32), wd_scales[0, 4 * q : 4 * q + 4, :].bitcast(I32)
             )
 
-        router = held.tile([P, J], F32, name="router", tag="stage01")
+        router = held.tile([P, J], F32, name="router", tag="stage0", align_bytes=64)
         nc.sync.dma_start(router[:], wgo)
 
         h_codes = held.tile([P, J], U32, name="h_codes", align_bytes=64)
         h_scales = held.tile([P, J], U8, name="h_scales", align_bytes=64)
         y = [held.tile([P, J], F32, name="y%d" % n) for n in range(N_TILES)]
 
-        def product(b, acc, words, scales, dtype):
+        def product(b, acc, codes, scales):
             apart, j = parted[b]
             for a in range(2):
                 nc.tensor.matmul_mx(
-                    out=acc[:],
+                    out=acc,
                     lhsT=apart[:, a, 2 * j : 2 * (j + BLOCK)].bitcast(FP4X4),
                     lhsT_scale=planes[:, a, b * BLOCK : (b + 1) * BLOCK],
-                    rhs=words[:, a, :].bitcast(dtype),
-                    rhs_scale=scales[:, a, :],
+                    rhs=codes[:, a],
+                    rhs_scale=scales[:, a],
                     start=(a == 0),
                     stop=(a == 1),
                 )
@@ -154,29 +154,36 @@ def tile_list_modp_gsilu_none_kernel(
         def as_laid(ap):
             return ap.rearrange("t (u p e) -> t u p e", u=2, e=2)
 
-        def hidden(b, turned):
+        def block_tiles():
             gate = psum.tile([P, R], F32, name="gate", bufs=3)
-            product(b, gate, wg_q, wg_s, FP8X4)
             up = psum.tile([P, R], F32, name="up", bufs=3)
-            product(b, up, wu_w, wu_s, FP4X4)
             act = ring.tile([P, R], F32, name="act")
-            nc.scalar.activation(as_laid(act[:]), by_word_half(gate[:]), SILU)
             h = ring.tile([P, R], BF16, name="h")
-            nc.vector.tensor_tensor(as_laid(h[:]), by_word_half(up[:]), as_laid(act[:]), MULT)
-            words = h[:].bitcast(F32)
-            j = b * BLOCK % GROUP
-            for u in range(2):
-                nc.tensor.transpose(turned[:, u, j : j + BLOCK], words[:, u * P : (u + 1) * P], identity[:])
+            return gate, up, act, h
 
-        def quantize_h(g):
-            turned = psum.tile([P, 2, GROUP], F32, name="turned", tag="bank0")
-            hidden(2 * g, turned)
-            hidden(2 * g + 1, turned)
-            grouped = ring.tile([P, GROUP, 4], BF16, name="h_grouped", align_bytes=64)
+        def hidden(b, tiles, r0, r1, width):
+            gate, up, act, h = tiles
+            for r in range(r0, r1, width):
+                product(b, gate[:, r : r + width], wg_q[:, :, r : r + width].bitcast(FP8X4), wg_s[:, :, r : r + width])
+            if r0 == 0:
+                product(b, up[:], wu_w[:].bitcast(FP4X4), wu_s[:])
+            part = slice(r0 // 4, r1 // 4)
+            nc.scalar.activation(as_laid(act[:])[:, :, part], by_word_half(gate[:])[:, :, part], SILU)
+            nc.vector.tensor_tensor(
+                as_laid(h[:])[:, :, part], by_word_half(up[:])[:, :, part], as_laid(act[:])[:, :, part], MULT
+            )
+
+        def turn(h, turned):
+            words = h[:].bitcast(F32)
+            for u in range(2):
+                nc.tensor.transpose(turned[:, u], words[:, u * P : (u + 1) * P], identity[:])
+
+        def quantize_h(turned, j0, j1):
+            grouped = ring.tile([P, j1 - j0, 4], BF16, name="h_grouped", align_bytes=64)
             nc.scalar.copy(grouped[:].bitcast(F32), turned[:].rearrange("p u j -> p j u"))
             nc.vector.quantize_mx(
-                out=h_codes[:, g * GROUP : (g + 1) * GROUP].bitcast(FP8X4),
-                scales=h_scales[:, g * GROUP : (g + 1) * GROUP],
+                out=h_codes[:, j0:j1].bitcast(FP8X4),
+                scales=h_scales[:, j0:j1],
                 in_=grouped[:].rearrange("p j i -> p (j i)"),
             )
 
@@ -202,20 +209,40 @@ def tile_list_modp_gsilu_none_kernel(
         def store(n):
             nc.sync.dma_start(out[n * P : (n + 1) * P, :], windows[n % 3][:])
 
+        lead = [block_tiles() for b in range(LEAD)]
+        for b in range(LEAD):
+            hidden(b, lead[b], 0, WIDE, BLOCK)
         for g in range(GROUPS):
-            quantize_h(g)
-            if g == 1:
-                windows.append(zeroed_window("stage10"))
+            blocks = (2 * g, 2 * g + 1)
             if g > 0:
+                turned = psum.tile([P, 2, GROUP], F32, name="turned", tag="bank0")
+            for b in blocks:
+                if b < LEAD:
+                    tiles = lead[b]
+                    hidden(b, tiles, WIDE, R, BLOCK)
+                else:
+                    tiles = block_tiles()
+                    hidden(b, tiles, 0, R, R)
+                if g == 0:
+                    turned = psum.tile([P, 2, BLOCK], F32, name="turned", tag="bank0")
+                    turn(tiles[3], turned)
+                    quantize_h(turned, b * BLOCK, (b + 1) * BLOCK)
+                    down(0, b * BLOCK, (b + 1) * BLOCK, 1)
+                else:
+                    turn(tiles[3], turned[:, :, b % 2 * BLOCK : (b % 2 + 1) * BLOCK])
+            if g > 0:
+                quantize_h(turned, g * GROUP, (g + 1) * GROUP)
+                if g == 1:
+                    windows.append(zeroed_window("wg_bf11"))
                 down(1, (g - 1) * GROUP, g * GROUP, 0)
                 place(1, (g - 1) * GROUP, g * GROUP)
-            down(0, g * GROUP, (g + 1) * GROUP, 1)
+                down(0, g * GROUP, (g + 1) * GROUP, 1)
             place(0, g * GROUP, (g + 1) * GROUP)
         store(0)
         down(1, J - GROUP, J, 0)
         place(1, J - GROUP, J)
         store(1)
-        windows.append(zeroed_window("stage11"))
+        windows.append(zeroed_window("stage1"))
         for n in range(2, N_TILES):
             for c in range(2):
                 down(n, c * HALF, (c + 1) * HALF, 1 - c)

@@ -24,7 +24,7 @@ GROUPS = J // GROUP
 N_TILES = N // P
 HALF = 512
 WIDE = R // 2
-LEAD = 0
+SCALAR_SHARE = 192
 
 
 def tile_list_modp_gsilu_none_kernel(
@@ -43,6 +43,8 @@ def tile_list_modp_gsilu_none_kernel(
         table_scales = shared.tile([P, T], U8, name="table_scales", offset=512, align_bytes=64)
         nc.sync.dma_start(table_scales[96:P, :].bitcast(I32), tab_scales.rearrange("a s t -> s a t").bitcast(I32))
 
+        wu_w = held.tile([P, 2, 2 * R], U8, name="wu_w", align_bytes=64)
+        nc.sync.dma_start(wu_w[:].bitcast(I32), wu_words.rearrange("a p b -> p a b").bitcast(I32))
         table = held.tile([P, T], I32, name="table")
         nc.sync.dma_start(table[:], tab_words[0].rearrange("p t b -> p (t b)").bitcast(I32))
         wg_rows = wg.rearrange("(a p i) r -> a p i r", a=2, i=4)
@@ -54,23 +56,19 @@ def tile_list_modp_gsilu_none_kernel(
             wg_raw.append(raw)
 
         load_wg(0)
-        wu_w = held.tile([P, 2, 2 * R], U8, name="wu_w", align_bytes=64)
-        nc.sync.dma_start(wu_w[:].bitcast(I32), wu_words.rearrange("a p b -> p a b").bitcast(I32))
-        load_wg(1)
 
+        wu_s = held.tile([P, 2, R], U8, name="wu_s", align_bytes=64)
+        nc.gpsimd.memset(wu_s[:].bitcast(I32), 0)
+        for q in range(4):
+            nc.scalar.dma_start(
+                wu_s[32 * q : 32 * q + 4, :, :].bitcast(I32),
+                wu_scales[:, 4 * q : 4 * q + 4, :].rearrange("a r n -> r a n").bitcast(I32),
+            )
         warm = held.tile([P, 2, 8], F32, name="warm")
         nc.gpsimd.memset(warm[:, 0, :], 0.0)
         nc.scalar.activation(warm[:, 1, :], warm[:, 0, :], SILU)
         identity = held.tile([P, P], F32, name="identity")
         make_identity(nc, identity[:])
-        planes = held.tile([P, 2, J], U8, name="planes", align_bytes=64)
-        wu_s = held.tile([P, 2, R], U8, name="wu_s", align_bytes=64)
-        nc.gpsimd.memset(wu_s[:].bitcast(I32), 0)
-        for q in range(4):
-            nc.gpsimd.dma_start(
-                wu_s[32 * q : 32 * q + 4, :, :].bitcast(I32),
-                wu_scales[:, 4 * q : 4 * q + 4, :].rearrange("a r n -> r a n").bitcast(I32),
-            )
 
         def zeroed_window(tag):
             window = held.tile([P, T], F32, name="window", tag=tag, align_bytes=64)
@@ -79,13 +77,22 @@ def tile_list_modp_gsilu_none_kernel(
             return window
 
         nc.vector.memset(table_scales[0:96, :].bitcast(I32), 0)
-        nc.vector.memset(planes[:].bitcast(I32), 0)
-        picked = held.tile([P, J], U8, name="picked", align_bytes=64)
-        nc.vector.tensor_copy(picked[:], table_scales[:].indirect(offsets[:]))
-        for q in range(4):
-            nc.scalar.dma_start(
-                planes[32 * q : 32 * q + 4].bitcast(I32), picked[96 + 8 * q : 96 + 8 * q + 8, :].bitcast(I32)
-            )
+        planes = []
+
+        def pick_scales(j0):
+            plane = held.tile([P, 2, HALF], U8, name="plane%d" % j0, align_bytes=64)
+            nc.vector.memset(plane[:].bitcast(I32), 0)
+            picked = held.tile([P, HALF], U8, name="picked%d" % j0, align_bytes=64)
+            nc.vector.tensor_copy(picked[:], table_scales[:].indirect(offsets[:, j0 // 16 : (j0 + HALF) // 16]))
+            for q in range(4):
+                nc.sync.dma_start(
+                    plane[32 * q : 32 * q + 4].bitcast(I32), picked[96 + 8 * q : 96 + 8 * q + 8, :].bitcast(I32)
+                )
+            planes.append(plane)
+
+        pick_scales(0)
+        load_wg(1)
+        pick_scales(HALF)
 
         windows = [zeroed_window("window0")]
 
@@ -107,19 +114,33 @@ def tile_list_modp_gsilu_none_kernel(
         wd_w = shared.tile([P, 4 * N], U8, name="wd_w", offset=0, align_bytes=64)
         nc.sync.dma_start(wd_w[:].bitcast(I32), wd_words[0].rearrange("p n i -> p (n i)").bitcast(I32))
 
-        for a in range(2):
-            for c in (a, 1 - a):
-                copy = nc.vector.tensor_copy if (a, c) == (1, 1) else nc.scalar.copy
-                grouped = held.tile([P, WIDE, 4], BF16, name="wg_bf", tag="wg_bf%d%d" % (a, c), align_bytes=64)
-                copy(
-                    grouped[:].rearrange("p (c e) i -> p c i e", e=4),
-                    wg_raw[a][:, :, c * WIDE : (c + 1) * WIDE].rearrange("p i (c e) -> p c i e", e=4),
-                )
-                nc.vector.quantize_mx(
-                    out=wg_q[:, a, c * WIDE : (c + 1) * WIDE].bitcast(FP8X4),
-                    scales=wg_s[:, a, c * WIDE : (c + 1) * WIDE],
-                    in_=grouped[:].rearrange("p c i -> p (c i)"),
-                )
+        wg_bf = {
+            (a, c): held.tile([P, WIDE, 4], BF16, name="wg_bf", tag="wg_bf%d%d" % (a, c), align_bytes=64)
+            for a in range(2)
+            for c in range(2)
+        }
+
+        def round_wg(copy, a, r0, r1):
+            copy(
+                wg_bf[a, r0 // WIDE][:, r0 % WIDE : (r1 - 1) % WIDE + 1].rearrange("p (c e) i -> p c i e", e=4),
+                wg_raw[a][:, :, r0:r1].rearrange("p i (c e) -> p c i e", e=4),
+            )
+
+        def quantize_wg(a, c):
+            nc.vector.quantize_mx(
+                out=wg_q[:, a, c * WIDE : (c + 1) * WIDE].bitcast(FP8X4),
+                scales=wg_s[:, a, c * WIDE : (c + 1) * WIDE],
+                in_=wg_bf[a, c][:].rearrange("p c i -> p (c i)"),
+            )
+
+        for c in range(2):
+            round_wg(nc.scalar.copy, 0, c * WIDE, (c + 1) * WIDE)
+            quantize_wg(0, c)
+        round_wg(nc.scalar.copy, 1, 0, SCALAR_SHARE)
+        round_wg(nc.vector.tensor_copy, 1, WIDE, R)
+        round_wg(nc.vector.tensor_copy, 1, SCALAR_SHARE, WIDE)
+        quantize_wg(1, 1)
+        quantize_wg(1, 0)
 
         wd_s = held.tile([P, N], U8, name="wd_s", tag="wg_bf00", align_bytes=64)
         nc.vector.memset(wd_s[:].bitcast(I32), 0)
@@ -141,7 +162,7 @@ def tile_list_modp_gsilu_none_kernel(
                 nc.tensor.matmul_mx(
                     out=acc,
                     lhsT=apart[:, a, 2 * j : 2 * (j + BLOCK)].bitcast(FP4X4),
-                    lhsT_scale=planes[:, a, b * BLOCK : (b + 1) * BLOCK],
+                    lhsT_scale=planes[b * BLOCK // HALF][:, a, b * BLOCK % HALF : b * BLOCK % HALF + BLOCK],
                     rhs=codes[:, a],
                     rhs_scale=scales[:, a],
                     start=(a == 0),
@@ -154,24 +175,31 @@ def tile_list_modp_gsilu_none_kernel(
         def as_laid(ap):
             return ap.rearrange("t (u p e) -> t u p e", u=2, e=2)
 
-        def block_tiles():
-            gate = psum.tile([P, R], F32, name="gate", bufs=3)
+        def up_product(b):
             up = psum.tile([P, R], F32, name="up", bufs=3)
-            act = ring.tile([P, R], F32, name="act")
-            h = ring.tile([P, R], BF16, name="h")
+            product(b, up[:], wu_w[:].bitcast(FP4X4), wu_s[:])
+            return up
+
+        early = [up_product(b) for b in range(3)]
+
+        def block_tiles(b):
+            gate = psum.tile([P, R], F32, name="gate", bufs=3)
+            product(b, gate[:], wg_q[:].bitcast(FP8X4), wg_s[:])
+            up = early[b] if b < len(early) else up_product(b)
+            act = held.tile([P, R], F32, name="act", tag="second_h") if b == 3 else ring.tile([P, R], F32, name="act")
+            h = held.tile([P, R], BF16, name="h", tag="second_h") if b == 1 else ring.tile([P, R], BF16, name="h")
             return gate, up, act, h
 
-        def hidden(b, tiles, r0, r1, width):
+        def hidden(b, tiles, pieces):
             gate, up, act, h = tiles
-            for r in range(r0, r1, width):
-                product(b, gate[:, r : r + width], wg_q[:, :, r : r + width].bitcast(FP8X4), wg_s[:, :, r : r + width])
-            if r0 == 0:
-                product(b, up[:], wu_w[:].bitcast(FP4X4), wu_s[:])
-            part = slice(r0 // 4, r1 // 4)
-            nc.scalar.activation(as_laid(act[:])[:, :, part], by_word_half(gate[:])[:, :, part], SILU)
-            nc.vector.tensor_tensor(
-                as_laid(h[:])[:, :, part], by_word_half(up[:])[:, :, part], as_laid(act[:])[:, :, part], MULT
-            )
+            halves = (slice(0, 1), slice(1, 2))
+            whole = (slice(0, 2),)
+            for part in halves if b < 5 else whole:
+                nc.scalar.activation(as_laid(act[:])[:, part], by_word_half(gate[:])[:, part], SILU)
+            for part in halves if pieces == 2 else whole:
+                nc.vector.tensor_tensor(
+                    as_laid(h[:])[:, part], by_word_half(up[:])[:, part], as_laid(act[:])[:, part], MULT
+                )
 
         def turn(h, turned):
             words = h[:].bitcast(F32)
@@ -209,31 +237,24 @@ def tile_list_modp_gsilu_none_kernel(
         def store(n):
             nc.sync.dma_start(out[n * P : (n + 1) * P, :], windows[n % 3][:])
 
-        lead = [block_tiles() for b in range(LEAD)]
-        for b in range(LEAD):
-            hidden(b, lead[b], 0, WIDE, BLOCK)
         for g in range(GROUPS):
             blocks = (2 * g, 2 * g + 1)
             if g > 0:
                 turned = psum.tile([P, 2, GROUP], F32, name="turned", tag="bank0")
             for b in blocks:
-                if b < LEAD:
-                    tiles = lead[b]
-                    hidden(b, tiles, WIDE, R, BLOCK)
-                else:
-                    tiles = block_tiles()
-                    hidden(b, tiles, 0, R, R)
+                tiles = block_tiles(b)
+                hidden(b, tiles, 2 if g == 0 else 1)
                 if g == 0:
-                    turned = psum.tile([P, 2, BLOCK], F32, name="turned", tag="bank0")
+                    turned = psum.tile([P, 2, BLOCK], F32, name="turned", tag="bank%d" % b)
                     turn(tiles[3], turned)
                     quantize_h(turned, b * BLOCK, (b + 1) * BLOCK)
-                    down(0, b * BLOCK, (b + 1) * BLOCK, 1)
+                    down(0, b * BLOCK, (b + 1) * BLOCK, b)
                 else:
                     turn(tiles[3], turned[:, :, b % 2 * BLOCK : (b % 2 + 1) * BLOCK])
             if g > 0:
                 quantize_h(turned, g * GROUP, (g + 1) * GROUP)
                 if g == 1:
-                    windows.append(zeroed_window("wg_bf11"))
+                    windows.append(zeroed_window("wg_bf10"))
                 down(1, (g - 1) * GROUP, g * GROUP, 0)
                 place(1, (g - 1) * GROUP, g * GROUP)
                 down(0, g * GROUP, (g + 1) * GROUP, 1)

@@ -40,7 +40,7 @@ def tile_list_modp_gsilu_none_kernel(
         offsets = held.tile([P, J // 16], U16, name="offsets")
         nc.sync.dma_start(offsets[:], offs)
 
-        table_scales = shared.tile([P, T], U8, name="table_scales", offset=512, align_bytes=64)
+        table_scales = shared.tile([P, T], U8, name="table_scales", offset=3584, align_bytes=64)
         nc.sync.dma_start(table_scales[96:P, :].bitcast(I32), tab_scales.rearrange("a s t -> s a t").bitcast(I32))
 
         wu_w = held.tile([P, 2, 2 * R], U8, name="wu_w", align_bytes=64)
@@ -51,7 +51,10 @@ def tile_list_modp_gsilu_none_kernel(
         wg_raw = []
 
         def load_wg(a):
-            raw = held.tile([P, 4, R], F32, name="wg_raw", tag="stage%d" % a, align_bytes=64)
+            if a == 0:
+                raw = held.tile([P, 4, R], F32, name="wg_raw", tag="stage0", align_bytes=64)
+            else:
+                raw = shared.tile([P, 4, R], F32, name="wg_last", offset=4096, align_bytes=64)
             nc.sync.dma_start(raw[:], wg_rows[a])
             wg_raw.append(raw)
 
@@ -64,19 +67,17 @@ def tile_list_modp_gsilu_none_kernel(
                 wu_s[32 * q : 32 * q + 4, :, :].bitcast(I32),
                 wu_scales[:, 4 * q : 4 * q + 4, :].rearrange("a r n -> r a n").bitcast(I32),
             )
-        warm = held.tile([P, 2, 8], F32, name="warm")
-        nc.gpsimd.memset(warm[:, 0, :], 0.0)
-        nc.scalar.activation(warm[:, 1, :], warm[:, 0, :], SILU)
         identity = held.tile([P, P], F32, name="identity")
         make_identity(nc, identity[:])
 
-        def zeroed_window(tag):
-            window = held.tile([P, T], F32, name="window", tag=tag, align_bytes=64)
+        def zeroed(window):
             for c in range(4):
                 nc.vector.memset(window[:, c * (T // 4) : (c + 1) * (T // 4)].bitcast(I32), 0)
             return window
 
         nc.vector.memset(table_scales[0:96, :].bitcast(I32), 0)
+        wd_s = held.tile([P, N], U8, name="wd_s", align_bytes=64)
+        nc.vector.memset(wd_s[:].bitcast(I32), 0)
         planes = []
 
         def pick_scales(j0):
@@ -84,17 +85,21 @@ def tile_list_modp_gsilu_none_kernel(
             nc.vector.memset(plane[:].bitcast(I32), 0)
             picked = held.tile([P, HALF], U8, name="picked%d" % j0, align_bytes=64)
             nc.vector.tensor_copy(picked[:], table_scales[:].indirect(offsets[:, j0 // 16 : (j0 + HALF) // 16]))
+            planes.append(plane)
+            return plane, picked
+
+        def move_scales(plane, picked):
             for q in range(4):
                 nc.sync.dma_start(
                     plane[32 * q : 32 * q + 4].bitcast(I32), picked[96 + 8 * q : 96 + 8 * q + 8, :].bitcast(I32)
                 )
-            planes.append(plane)
 
-        pick_scales(0)
+        move_scales(*pick_scales(0))
+        late = pick_scales(HALF)
         load_wg(1)
-        pick_scales(HALF)
+        move_scales(*late)
 
-        windows = [zeroed_window("window0")]
+        windows = [zeroed(held.tile([P, T], F32, name="window0"))]
 
         parted = {}
 
@@ -109,9 +114,9 @@ def tile_list_modp_gsilu_none_kernel(
         wg_s = held.tile([P, 2, R], U8, name="wg_s", align_bytes=64)
 
         for j0, j1 in ((0, 384), (384, J)):
-            pairs = shared.tile([P, j1 - j0], U32, name="pairs%d" % j0, offset=4 * j0, align_bytes=64)
+            pairs = shared.tile([P, j1 - j0], U32, name="pairs%d" % j0, offset=4096 - 4 * (j1 - j0), align_bytes=64)
             pick_words(j0, j1, pairs)
-        wd_w = shared.tile([P, 4 * N], U8, name="wd_w", offset=0, align_bytes=64)
+        wd_w = shared.tile([P, 4 * N], U8, name="wd_w", offset=2048, align_bytes=64)
         nc.sync.dma_start(wd_w[:].bitcast(I32), wd_words[0].rearrange("p n i -> p (n i)").bitcast(I32))
 
         wg_bf = {
@@ -142,8 +147,6 @@ def tile_list_modp_gsilu_none_kernel(
         quantize_wg(1, 1)
         quantize_wg(1, 0)
 
-        wd_s = held.tile([P, N], U8, name="wd_s", tag="wg_bf00", align_bytes=64)
-        nc.vector.memset(wd_s[:].bitcast(I32), 0)
         for q in range(4):
             nc.sync.dma_start(
                 wd_s[32 * q : 32 * q + 4, :].bitcast(I32), wd_scales[0, 4 * q : 4 * q + 4, :].bitcast(I32)
@@ -254,7 +257,7 @@ def tile_list_modp_gsilu_none_kernel(
             if g > 0:
                 quantize_h(turned, g * GROUP, (g + 1) * GROUP)
                 if g == 1:
-                    windows.append(zeroed_window("wg_bf10"))
+                    windows.append(zeroed(held.tile([P, T], F32, name="window1", tag="wg_bf10", align_bytes=64)))
                 down(1, (g - 1) * GROUP, g * GROUP, 0)
                 place(1, (g - 1) * GROUP, g * GROUP)
                 down(0, g * GROUP, (g + 1) * GROUP, 1)
@@ -263,7 +266,7 @@ def tile_list_modp_gsilu_none_kernel(
         down(1, J - GROUP, J, 0)
         place(1, J - GROUP, J)
         store(1)
-        windows.append(zeroed_window("stage1"))
+        windows.append(zeroed(shared.tile([P, T], F32, name="window2", offset=4096, align_bytes=64)))
         for n in range(2, N_TILES):
             for c in range(2):
                 down(n, c * HALF, (c + 1) * HALF, 1 - c)

@@ -210,7 +210,10 @@ def tile_list_modp_gsilu_none_kernel(
                 nc.tensor.transpose(turned[:, u], words[:, u * P : (u + 1) * P], identity[:])
 
         def quantize_h(turned, j0, j1):
-            grouped = ring.tile([P, j1 - j0, 4], BF16, name="h_grouped", align_bytes=64)
+            if j1 == J:
+                grouped = held.tile([P, j1 - j0, 4], BF16, name="h_grouped", tag="last_h", align_bytes=64)
+            else:
+                grouped = ring.tile([P, j1 - j0, 4], BF16, name="h_grouped", align_bytes=64)
             nc.scalar.copy(grouped[:].bitcast(F32), turned[:].rearrange("p u j -> p j u"))
             nc.vector.quantize_mx(
                 out=h_codes[:, j0:j1].bitcast(FP8X4),
@@ -266,7 +269,9 @@ def tile_list_modp_gsilu_none_kernel(
         down(1, J - GROUP, J, 0)
         place(1, J - GROUP, J)
         store(1)
-        windows.append(zeroed(shared.tile([P, T], F32, name="window2", offset=4096, align_bytes=64)))
+        third = held.tile([P, T], F32, name="window2", tag="last_h", align_bytes=64)
+        nc.gpsimd.memset(third[:].bitcast(I32), 0)
+        windows.append(third)
         for n in range(2, N_TILES):
             for c in range(2):
                 down(n, c * HALF, (c + 1) * HALF, 1 - c)

@@ -24,7 +24,7 @@ GROUPS = J // GROUP
 N_TILES = N // P
 HALF = 512
 WIDE = R // 2
-SCALAR_SHARE = 192
+SCALAR_SHARE = 128
 
 
 def tile_list_modp_gsilu_none_kernel(
@@ -44,9 +44,9 @@ def tile_list_modp_gsilu_none_kernel(
         nc.sync.dma_start(table_scales[96:P, :].bitcast(I32), tab_scales.rearrange("a s t -> s a t").bitcast(I32))
 
         wu_w = held.tile([P, 2, 2 * R], U8, name="wu_w", align_bytes=64)
-        nc.sync.dma_start(wu_w[:].bitcast(I32), wu_words.rearrange("a p b -> p a b").bitcast(I32))
         table = held.tile([P, T], I32, name="table")
         nc.sync.dma_start(table[:], tab_words[0].rearrange("p t b -> p (t b)").bitcast(I32))
+        nc.sync.dma_start(wu_w[:].bitcast(I32), wu_words.rearrange("a p b -> p a b").bitcast(I32))
         wg_rows = wg.rearrange("(a p i) r -> a p i r", a=2, i=4)
         wg_raw = []
 

@@ -16,15 +16,17 @@ FP8X4 = mybir.dt.float8_e4m3fn_x4
 FP4X4 = mybir.dt.float4_e2m1fn_x4
 MULT = mybir.AluOpType.mult
 SILU = mybir.ActivationFunctionType.Silu
+COPY = mybir.ActivationFunctionType.Copy
 
 P = 128
 BLOCK = 128
 GROUP = 256
-GROUPS = J // GROUP
-N_TILES = N // P
 HALF = 512
 WIDE = R // 2
-SCALAR_SHARE = 128
+SCALAR_SHARE = 64
+FIRST_PICK = 384
+ZERO_PIECE = 512
+VECTOR_ZERO = 688
 
 
 def tile_list_modp_gsilu_none_kernel(
@@ -33,32 +35,24 @@ def tile_list_modp_gsilu_none_kernel(
     nc = tc.nc
     with ExitStack() as ctx:
         held = ctx.enter_context(tc.tile_pool(name="held", bufs=1))
-        shared = ctx.enter_context(tc.tile_pool(name="shared", bufs=1))
+        laid = ctx.enter_context(tc.tile_pool(name="laid", bufs=1))
         ring = ctx.enter_context(tc.tile_pool(name="ring", bufs=3))
         psum = ctx.enter_context(tc.psum_pool(name="psum", bufs=1))
 
         offsets = held.tile([P, J // 16], U16, name="offsets")
         nc.sync.dma_start(offsets[:], offs)
 
-        table_scales = shared.tile([P, T], U8, name="table_scales", offset=3584, align_bytes=64)
-        nc.sync.dma_start(table_scales[96:P, :].bitcast(I32), tab_scales.rearrange("a s t -> s a t").bitcast(I32))
+        table_scales = laid.tile([P, T], U8, name="table_scales", offset=2048, align_bytes=64)
+        nc.scalar.dma_start(table_scales[96:P, :].bitcast(I32), tab_scales.rearrange("a s t -> s a t").bitcast(I32))
+        nc.gpsimd.memset(table_scales[0:96, :].bitcast(I32), 0)
 
-        wu_w = held.tile([P, 2, 2 * R], U8, name="wu_w", align_bytes=64)
         table = held.tile([P, T], I32, name="table")
         nc.sync.dma_start(table[:], tab_words[0].rearrange("p t b -> p (t b)").bitcast(I32))
+        wu_w = held.tile([P, 2, 2 * R], U8, name="wu_w", align_bytes=64)
         nc.sync.dma_start(wu_w[:].bitcast(I32), wu_words.rearrange("a p b -> p a b").bitcast(I32))
         wg_rows = wg.rearrange("(a p i) r -> a p i r", a=2, i=4)
-        wg_raw = []
-
-        def load_wg(a):
-            if a == 0:
-                raw = held.tile([P, 4, R], F32, name="wg_raw", tag="stage0", align_bytes=64)
-            else:
-                raw = shared.tile([P, 4, R], F32, name="wg_last", offset=4096, align_bytes=64)
-            nc.sync.dma_start(raw[:], wg_rows[a])
-            wg_raw.append(raw)
-
-        load_wg(0)
+        wg_raw = [laid.tile([P, 4, R], F32, name="wg_first", offset=16384, align_bytes=64)]
+        nc.sync.dma_start(wg_raw[0][:], wg_rows[0])
 
         wu_s = held.tile([P, 2, R], U8, name="wu_s", align_bytes=64)
         nc.gpsimd.memset(wu_s[:].bitcast(I32), 0)
@@ -67,164 +61,185 @@ def tile_list_modp_gsilu_none_kernel(
                 wu_s[32 * q : 32 * q + 4, :, :].bitcast(I32),
                 wu_scales[:, 4 * q : 4 * q + 4, :].rearrange("a r n -> r a n").bitcast(I32),
             )
+        wu_dealt = held.tile([P, 2, 2 * R], U8, name="wu_dealt", align_bytes=64)
+        nc.scalar.copy(
+            wu_dealt[:].bitcast(U16).rearrange("p a (t m) -> p a t m", t=4),
+            wu_w[:].bitcast(U16).rearrange("p a (m t) -> p a t m", t=4),
+        )
+        planes = []
+        for half in range(2):
+            plane = held.tile([P, 2, HALF], U8, name="plane%d" % half, align_bytes=64)
+            nc.gpsimd.memset(plane[:].bitcast(I32), 0)
+            planes.append(plane)
         identity = held.tile([P, P], F32, name="identity")
         make_identity(nc, identity[:])
 
-        def zeroed(window):
-            for c in range(4):
-                nc.vector.memset(window[:, c * (T // 4) : (c + 1) * (T // 4)].bitcast(I32), 0)
-            return window
+        windows = [held.tile([P, T], F32, name="window0")]
+        nc.vector.memset(windows[0][:, 0 : T // 2 + 1].bitcast(I32), 0)
+        nc.vector.memset(windows[0][:, T // 2 + 1 : T].bitcast(I32), 0)
 
-        nc.vector.memset(table_scales[0:96, :].bitcast(I32), 0)
-        wd_s = held.tile([P, N], U8, name="wd_s", align_bytes=64)
-        nc.vector.memset(wd_s[:].bitcast(I32), 0)
-        planes = []
+        def zeroed(window, start):
+            for c in range(start, T, ZERO_PIECE):
+                nc.gpsimd.memset(window[:, c : min(c + ZERO_PIECE, T)].bitcast(I32), 0)
+            windows.append(window)
 
-        def pick_scales(j0):
-            plane = held.tile([P, 2, HALF], U8, name="plane%d" % j0, align_bytes=64)
-            nc.vector.memset(plane[:].bitcast(I32), 0)
-            picked = held.tile([P, HALF], U8, name="picked%d" % j0, align_bytes=64)
-            nc.vector.tensor_copy(picked[:], table_scales[:].indirect(offsets[:, j0 // 16 : (j0 + HALF) // 16]))
-            planes.append(plane)
-            return plane, picked
+        def entries(j0, j1):
+            return offsets[:, j0 // 16 : j1 // 16]
 
-        def move_scales(plane, picked):
+        picked = []
+        for half in range(2):
+            rows = held.tile([P, HALF], U8, name="picked%d" % half, align_bytes=64)
+            nc.vector.tensor_copy(rows[:], table_scales[:].indirect(entries(half * HALF, (half + 1) * HALF)))
+            picked.append(rows)
+
+        wu_s_dealt = held.tile([P, 2, R], U8, name="wu_s_dealt", align_bytes=64)
+        nc.vector.tensor_copy(
+            wu_s_dealt[:].rearrange("p a (t m) -> p a t m", t=4), wu_s[:].rearrange("p a (m t) -> p a t m", t=4)
+        )
+
+        def move_scales(half):
             for q in range(4):
                 nc.sync.dma_start(
-                    plane[32 * q : 32 * q + 4].bitcast(I32), picked[96 + 8 * q : 96 + 8 * q + 8, :].bitcast(I32)
+                    planes[half][32 * q : 32 * q + 4].bitcast(I32),
+                    picked[half][96 + 8 * q : 96 + 8 * q + 8, :].bitcast(I32),
                 )
 
-        move_scales(*pick_scales(0))
-        late = pick_scales(HALF)
-        load_wg(1)
-        move_scales(*late)
-
-        windows = [zeroed(held.tile([P, T], F32, name="window0"))]
+        move_scales(0)
+        wg_raw.append(laid.tile([P, 4, R], F32, name="wg_last", offset=4032, align_bytes=64))
+        nc.sync.dma_start(wg_raw[1][:], wg_rows[1])
+        move_scales(1)
 
         parted = {}
-
-        def pick_words(j0, j1, pairs):
-            nc.vector.tensor_copy(pairs[:], table[:].bitcast(U32).indirect(offsets[:, j0 // 16 : j1 // 16]))
+        for j0, j1, offset in ((0, FIRST_PICK, 12288), (FIRST_PICK, J, 13760)):
+            pairs = laid.tile([P, j1 - j0], U32, name="pairs%d" % j0, offset=offset, align_bytes=64)
+            nc.vector.tensor_copy(pairs[:], table[:].bitcast(U32).indirect(entries(j0, j1)))
             apart = held.tile([P, 2, 2 * (j1 - j0)], U8, name="apart%d" % j0, align_bytes=64)
             nc.vector.tensor_copy(apart[:].bitcast(U16), pairs[:].bitcast(U16).rearrange("p (j d) -> p d j", d=2))
             for j in range(j0, j1, BLOCK):
                 parted[j // BLOCK] = (apart, j - j0)
 
+        wd_w = laid.tile([P, 4 * N], U8, name="wd_w", offset=13824, align_bytes=64)
+        nc.sync.dma_start(wd_w[:].bitcast(I32), wd_words[0].rearrange("p n i -> p (n i)").bitcast(I32))
+        wd_s = laid.tile([P, N], U8, name="wd_s", offset=12288, align_bytes=64)
+        nc.gpsimd.memset(wd_s[:].bitcast(I32), 0)
+        for q in range(4):
+            nc.sync.dma_start(
+                wd_s[32 * q : 32 * q + 4, :].bitcast(I32), wd_scales[0, 4 * q : 4 * q + 4, :].bitcast(I32)
+            )
+
         wg_q = held.tile([P, 2, R], U32, name="wg_q", align_bytes=64)
         wg_s = held.tile([P, 2, R], U8, name="wg_s", align_bytes=64)
-
-        for j0, j1 in ((0, 384), (384, J)):
-            pairs = shared.tile([P, j1 - j0], U32, name="pairs%d" % j0, offset=4096 - 4 * (j1 - j0), align_bytes=64)
-            pick_words(j0, j1, pairs)
-        wd_w = shared.tile([P, 4 * N], U8, name="wd_w", offset=2048, align_bytes=64)
-        nc.sync.dma_start(wd_w[:].bitcast(I32), wd_words[0].rearrange("p n i -> p (n i)").bitcast(I32))
-
         wg_bf = {
-            (a, c): held.tile([P, WIDE, 4], BF16, name="wg_bf", tag="wg_bf%d%d" % (a, c), align_bytes=64)
+            (a, c): held.tile([P, 2, P, 4], BF16, name="wg_bf", tag="wg_bf%d%d" % (a, c), align_bytes=64)
             for a in range(2)
             for c in range(2)
         }
 
-        def round_wg(copy, a, r0, r1):
+        def round_wg(copy, a, c, m0, m1):
             copy(
-                wg_bf[a, r0 // WIDE][:, r0 % WIDE : (r1 - 1) % WIDE + 1].rearrange("p (c e) i -> p c i e", e=4),
-                wg_raw[a][:, :, r0:r1].rearrange("p i (c e) -> p c i e", e=4),
+                wg_bf[a, c][:, :, m0:m1].rearrange("p t m i -> p m i t"),
+                wg_raw[a][:].rearrange("p i (m t) -> p m i t", t=4)[:, m0:m1, :, 2 * c : 2 * c + 2],
             )
 
         def quantize_wg(a, c):
             nc.vector.quantize_mx(
                 out=wg_q[:, a, c * WIDE : (c + 1) * WIDE].bitcast(FP8X4),
                 scales=wg_s[:, a, c * WIDE : (c + 1) * WIDE],
-                in_=wg_bf[a, c][:].rearrange("p c i -> p (c i)"),
+                in_=wg_bf[a, c][:].rearrange("p t m i -> p (t m i)"),
             )
 
         for c in range(2):
-            round_wg(nc.scalar.copy, 0, c * WIDE, (c + 1) * WIDE)
+            round_wg(nc.scalar.copy, 0, c, 0, P)
             quantize_wg(0, c)
-        round_wg(nc.scalar.copy, 1, 0, SCALAR_SHARE)
-        round_wg(nc.vector.tensor_copy, 1, WIDE, R)
-        round_wg(nc.vector.tensor_copy, 1, SCALAR_SHARE, WIDE)
-        quantize_wg(1, 1)
+        round_wg(nc.scalar.copy, 1, 1, 0, SCALAR_SHARE)
+        round_wg(nc.vector.tensor_copy, 1, 0, 0, P)
+        round_wg(nc.vector.tensor_copy, 1, 1, SCALAR_SHARE, P)
         quantize_wg(1, 0)
+        quantize_wg(1, 1)
+        second = held.tile([P, T], F32, name="window1", tag="wg_bf11", align_bytes=64)
+        zeroed(second, VECTOR_ZERO)
+        nc.vector.memset(second[:, 0 : VECTOR_ZERO // 2 - 1].bitcast(I32), 0)
+        nc.vector.memset(second[:, VECTOR_ZERO // 2 - 1 : VECTOR_ZERO].bitcast(I32), 0)
 
-        for q in range(4):
-            nc.sync.dma_start(
-                wd_s[32 * q : 32 * q + 4, :].bitcast(I32), wd_scales[0, 4 * q : 4 * q + 4, :].bitcast(I32)
-            )
-
-        router = held.tile([P, J], F32, name="router", tag="stage0", align_bytes=64)
-        nc.sync.dma_start(router[:], wgo)
+        router_first = laid.tile([P, GROUP], F32, name="router_first", offset=16384, align_bytes=64)
+        nc.sync.dma_start(router_first[:], wgo[:, 0:GROUP])
+        router_turned = laid.tile([P, 2], F32, name="router_turned", offset=17408, align_bytes=64)
+        with nc.allow_non_contiguous_dma(reason="one router weight for each partition"):
+            nc.sync.dma_start(router_turned[:], wgo[0, GROUP:HALF].rearrange("(c p) -> p c", p=P))
+        router_last = laid.tile([P, HALF], F32, name="router_last", offset=17472, align_bytes=64)
+        nc.sync.dma_start(router_last[:], wgo[:, HALF:J])
 
         h_codes = held.tile([P, J], U32, name="h_codes", align_bytes=64)
         h_scales = held.tile([P, J], U8, name="h_scales", align_bytes=64)
-        y = [held.tile([P, J], F32, name="y%d" % n) for n in range(N_TILES)]
 
-        def product(b, acc, codes, scales):
+        def first_pass(b, acc, codes, width, dtype, scales, a):
             apart, j = parted[b]
-            for a in range(2):
+            for t in range(4):
                 nc.tensor.matmul_mx(
-                    out=acc,
-                    lhsT=apart[:, a, 2 * j : 2 * (j + BLOCK)].bitcast(FP4X4),
-                    lhsT_scale=planes[b * BLOCK // HALF][:, a, b * BLOCK % HALF : b * BLOCK % HALF + BLOCK],
-                    rhs=codes[:, a],
-                    rhs_scale=scales[:, a],
-                    start=(a == 0),
-                    stop=(a == 1),
+                    out=acc[:, t],
+                    lhsT=codes[:, a, width * P * t : width * P * (t + 1)].bitcast(dtype),
+                    lhsT_scale=scales[:, a, P * t : P * (t + 1)],
+                    rhs=apart[:, a, 2 * j : 2 * (j + BLOCK)].bitcast(FP4X4),
+                    rhs_scale=planes[b * BLOCK // HALF][:, a, b * BLOCK % HALF : b * BLOCK % HALF + BLOCK],
+                    start=(a == 0 and t == 0),
+                    stop=(a == 1 and t == 3),
                 )
 
-        def by_word_half(ap):
-            return ap.rearrange("t (p u e) -> t u p e", u=2, e=2)
+        gates = {}
+        ups = {}
 
-        def as_laid(ap):
-            return ap.rearrange("t (u p e) -> t u p e", u=2, e=2)
+        def gate_pass(b, a):
+            if a == 0:
+                gates[b] = psum.tile([P, 4, BLOCK], F32, name="gate", bufs=3)
+            first_pass(b, gates[b], wg_q, 1, FP8X4, wg_s, a)
 
         def up_product(b):
-            up = psum.tile([P, R], F32, name="up", bufs=3)
-            product(b, up[:], wu_w[:].bitcast(FP4X4), wu_s[:])
-            return up
+            ups[b] = psum.tile([P, 4, BLOCK], F32, name="up", bufs=2)
+            for a in range(2):
+                first_pass(b, ups[b], wu_dealt, 2, FP4X4, wu_s_dealt, a)
 
-        early = [up_product(b) for b in range(3)]
+        def by_token(acc):
+            return acc[:].rearrange("p t j -> p j t")
 
-        def block_tiles(b):
-            gate = psum.tile([P, R], F32, name="gate", bufs=3)
-            product(b, gate[:], wg_q[:].bitcast(FP8X4), wg_s[:])
-            up = early[b] if b < len(early) else up_product(b)
-            act = held.tile([P, R], F32, name="act", tag="second_h") if b == 3 else ring.tile([P, R], F32, name="act")
-            h = held.tile([P, R], BF16, name="h", tag="second_h") if b == 1 else ring.tile([P, R], BF16, name="h")
-            return gate, up, act, h
+        halves = (slice(0, BLOCK // 2), slice(BLOCK // 2, BLOCK))
+        whole = (slice(0, BLOCK),)
 
-        def hidden(b, tiles, pieces):
-            gate, up, act, h = tiles
-            halves = (slice(0, 1), slice(1, 2))
-            whole = (slice(0, 2),)
-            for part in halves if b < 5 else whole:
-                nc.scalar.activation(as_laid(act[:])[:, part], by_word_half(gate[:])[:, part], SILU)
-            for part in halves if pieces == 2 else whole:
-                nc.vector.tensor_tensor(
-                    as_laid(h[:])[:, part], by_word_half(up[:])[:, part], as_laid(act[:])[:, part], MULT
-                )
-
-        def turn(h, turned):
-            words = h[:].bitcast(F32)
-            for u in range(2):
-                nc.tensor.transpose(turned[:, u], words[:, u * P : (u + 1) * P], identity[:])
-
-        def quantize_h(turned, j0, j1):
-            if j1 == J:
-                grouped = held.tile([P, j1 - j0, 4], BF16, name="h_grouped", tag="last_h", align_bytes=64)
+        def silu(b, parts):
+            if b == 3:
+                act = laid.tile([P, BLOCK, 4], F32, name="act3", offset=24576, align_bytes=64)
             else:
-                grouped = ring.tile([P, j1 - j0, 4], BF16, name="h_grouped", align_bytes=64)
-            nc.scalar.copy(grouped[:].bitcast(F32), turned[:].rearrange("p u j -> p j u"))
+                act = held.tile([P, BLOCK, 4], F32, name="act", tag="act%d" % b, align_bytes=64)
+            for part in parts:
+                nc.scalar.activation(act[:, part], by_token(gates[b])[:, part], SILU)
+            return act
+
+        def hidden_on_vector(b, parts, h):
+            act = silu(b, parts)
+            for part in parts:
+                nc.vector.tensor_tensor(h[:, part], by_token(ups[b])[:, part], act[:, part], MULT)
+
+        def hidden_on_gpsimd(b, h):
+            act = silu(b, whole)
+            up = held.tile([P, BLOCK, 4], F32, name="up_out%d" % b)
+            nc.scalar.copy(up[:], by_token(ups[b]))
+            nc.gpsimd.tensor_tensor(h, up[:], act[:], MULT)
+
+        def bank(name, shape):
+            return psum.tile(shape, F32, name="acc", tag=name)
+
+        def hidden_tile(j0, j1, tag):
+            return held.tile([P, j1 - j0, 4], BF16, name="h", tag=tag, align_bytes=64)
+
+        def quantize_h(h, j0, j1):
             nc.vector.quantize_mx(
                 out=h_codes[:, j0:j1].bitcast(FP8X4),
                 scales=h_scales[:, j0:j1],
-                in_=grouped[:].rearrange("p j i -> p (j i)"),
+                in_=h[:].rearrange("p j i -> p (j i)"),
             )
 
-        def down(n, j0, j1, bank):
-            acc = psum.tile([P, j1 - j0], F32, name="acc", tag="bank%d" % bank)
+        def down(acc, n, j0, j1):
             nc.tensor.matmul_mx(
-                out=acc[:],
+                out=acc,
                 lhsT=wd_w[:, 4 * P * n : 4 * P * (n + 1)].bitcast(FP8X4),
                 lhsT_scale=wd_s[:, P * n : P * (n + 1)],
                 rhs=h_codes[:, j0:j1].bitcast(FP8X4),
@@ -232,48 +247,98 @@ def tile_list_modp_gsilu_none_kernel(
                 start=True,
                 stop=True,
             )
-            nc.scalar.copy(y[n][:, j0:j1], acc[:])
 
-        def place(n, j0, j1):
-            window = windows[n % 3]
-            nc.vector.tensor_tensor(
-                window[:].indirect(offsets[:, j0 // 16 : j1 // 16]), y[n][:, j0:j1], router[:, j0:j1], MULT
+        def place(n, j0, j1, y, router):
+            nc.vector.tensor_tensor(windows[n][:].indirect(entries(j0, j1)), y, router, MULT)
+
+        def put(n, j0, j1, y):
+            nc.vector.tensor_copy(windows[n][:].indirect(entries(j0, j1)), y)
+
+        for b in range(2):
+            up_product(b)
+        for a in range(2):
+            for b in range(3):
+                gate_pass(b, a)
+
+        y_first = held.tile([P, GROUP], F32, name="y_first")
+        for b, name in ((0, "a"), (1, "b")):
+            h = hidden_tile(b * BLOCK, (b + 1) * BLOCK, "h%d" % b)
+            hidden_on_vector(b, halves, h)
+            quantize_h(h, b * BLOCK, (b + 1) * BLOCK)
+            acc = bank(name, [P, BLOCK])
+            down(acc[:], 0, b * BLOCK, (b + 1) * BLOCK)
+            nc.scalar.copy(y_first[:, b * BLOCK : (b + 1) * BLOCK], acc[:])
+
+        def products(b):
+            if b > 2:
+                for a in range(2):
+                    gate_pass(b, a)
+            up_product(b)
+
+        h = laid.tile([P, GROUP, 4], BF16, name="h_second", offset=40960, align_bytes=64)
+        for b in (2, 3):
+            products(b)
+            hidden_on_vector(b, whole, h[:, b % 2 * BLOCK : (b % 2 + 1) * BLOCK])
+        quantize_h(h, GROUP, HALF)
+        for n, offset in ((2, 42944), (3, 32832)):
+            zeroed(laid.tile([P, T], F32, name="window%d" % n, offset=offset, align_bytes=64), 0)
+        place(0, 0, GROUP, y_first[:], router_first[:])
+
+        acc = bank("a", [P, 2, GROUP])
+        for n in (1, 2):
+            down(acc[:, n - 1], n, 0, GROUP)
+        y_next = laid.tile([P, 2, GROUP], F32, name="y_next", offset=24576, align_bytes=64)
+        nc.scalar.copy(y_next[:], acc[:])
+        for n in (1, 2):
+            place(n, 0, GROUP, y_next[:, n - 1], router_first[:])
+
+        weighted = []
+        for b, name in ((2, "b"), (3, "c")):
+            acc = bank(name, [P, N])
+            nc.tensor.matmul_mx(
+                out=acc[:],
+                lhsT=h_codes[:, b * BLOCK : (b + 1) * BLOCK].bitcast(FP8X4),
+                lhsT_scale=h_scales[:, b * BLOCK : (b + 1) * BLOCK],
+                rhs=wd_w[:].bitcast(FP8X4),
+                rhs_scale=wd_s[:],
+                start=True,
+                stop=True,
             )
+            rows = held.tile([P, N], F32, name="weighted%d" % b)
+            nc.scalar.activation(rows[:], acc[:], COPY, scale=router_turned[:, b - 2 : b - 1])
+            weighted.append(rows)
 
-        def store(n):
-            nc.sync.dma_start(out[n * P : (n + 1) * P, :], windows[n % 3][:])
+        def turn_back(name, tiles):
+            back = bank(name, [P, len(tiles), GROUP])
+            for m, n in enumerate(tiles):
+                for c in range(2):
+                    nc.tensor.transpose(
+                        back[:, m, c * BLOCK : (c + 1) * BLOCK], weighted[c][:, n * P : (n + 1) * P], identity[:]
+                    )
+            y = held.tile([P, len(tiles), GROUP], F32, name="y_back%d" % tiles[0])
+            nc.scalar.copy(y[:], back[:])
+            for m, n in enumerate(tiles):
+                put(n, GROUP, HALF, y[:, m])
 
-        for g in range(GROUPS):
-            blocks = (2 * g, 2 * g + 1)
-            if g > 0:
-                turned = psum.tile([P, 2, GROUP], F32, name="turned", tag="bank0")
-            for b in blocks:
-                tiles = block_tiles(b)
-                hidden(b, tiles, 2 if g == 0 else 1)
-                if g == 0:
-                    turned = psum.tile([P, 2, BLOCK], F32, name="turned", tag="bank%d" % b)
-                    turn(tiles[3], turned)
-                    quantize_h(turned, b * BLOCK, (b + 1) * BLOCK)
-                    down(0, b * BLOCK, (b + 1) * BLOCK, b)
-                else:
-                    turn(tiles[3], turned[:, :, b % 2 * BLOCK : (b % 2 + 1) * BLOCK])
-            if g > 0:
-                quantize_h(turned, g * GROUP, (g + 1) * GROUP)
-                if g == 1:
-                    windows.append(zeroed(held.tile([P, T], F32, name="window1", tag="wg_bf10", align_bytes=64)))
-                down(1, (g - 1) * GROUP, g * GROUP, 0)
-                place(1, (g - 1) * GROUP, g * GROUP)
-                down(0, g * GROUP, (g + 1) * GROUP, 1)
-            place(0, g * GROUP, (g + 1) * GROUP)
-        store(0)
-        down(1, J - GROUP, J, 0)
-        place(1, J - GROUP, J)
-        store(1)
-        third = held.tile([P, T], F32, name="window2", tag="last_h", align_bytes=64)
-        nc.gpsimd.memset(third[:].bitcast(I32), 0)
-        windows.append(third)
-        for n in range(2, N_TILES):
-            for c in range(2):
-                down(n, c * HALF, (c + 1) * HALF, 1 - c)
-            place(n, 0, J)
-            store(n)
+        turn_back("b", (0, 1))
+        turn_back("c", (2, 3))
+
+        h = laid.tile([P, HALF, 4], BF16, name="h_late", offset=25600, align_bytes=64)
+        for b in range(4, 8):
+            products(b)
+            hidden_on_gpsimd(b, h[:, (b - 4) * BLOCK : (b - 3) * BLOCK])
+        quantize_h(h, HALF, J)
+
+        acc = bank("a", [P, GROUP])
+        down(acc[:], 3, 0, GROUP)
+        y_rest = held.tile([P, GROUP], F32, name="y_rest", tag="act7", align_bytes=64)
+        nc.scalar.copy(y_rest[:], acc[:])
+        place(3, 0, GROUP, y_rest[:], router_first[:])
+
+        for n in range(N // P):
+            acc = bank("bc"[n % 2 : n % 2 + 1], [P, HALF])
+            down(acc[:], n, HALF, J)
+            y = held.tile([P, HALF], F32, name="y_last%d" % n)
+            nc.scalar.copy(y[:], acc[:])
+            place(n, HALF, J, y[:], router_last[:])
+            nc.sync.dma_start(out[n * P : (n + 1) * P, :], windows[n][:])

@@ -26,6 +26,8 @@ WIDE = R // 2
 SCALAR_SHARE = 64
 FIRST_PICK = 384
 ZERO_PIECE = 512
+GATE_BANK = (3, 4, 5, 3, 7, 0, 7, 0)
+UP_BANK = (0, 1, 2, 0, 6, 1, 6, 1)
 VECTOR_ZERO = 688
 
 
@@ -185,16 +187,19 @@ def tile_list_modp_gsilu_none_kernel(
                     stop=(a == 1 and t == 3),
                 )
 
+        def bank(number, shape):
+            return psum.tile(shape, F32, name="acc", tag="bank%d" % number)
+
         gates = {}
         ups = {}
 
         def gate_pass(b, a):
             if a == 0:
-                gates[b] = psum.tile([P, 4, BLOCK], F32, name="gate", bufs=3)
+                gates[b] = bank(GATE_BANK[b], [P, 4, BLOCK])
             first_pass(b, gates[b], wg_q, 1, FP8X4, wg_s, a)
 
         def up_product(b):
-            ups[b] = psum.tile([P, 4, BLOCK], F32, name="up", bufs=2)
+            ups[b] = bank(UP_BANK[b], [P, 4, BLOCK])
             for a in range(2):
                 first_pass(b, ups[b], wu_dealt, 2, FP4X4, wu_s_dealt, a)
 
@@ -223,9 +228,6 @@ def tile_list_modp_gsilu_none_kernel(
             up = held.tile([P, BLOCK, 4], F32, name="up_out%d" % b)
             nc.scalar.copy(up[:], by_token(ups[b]))
             nc.gpsimd.tensor_tensor(h, up[:], act[:], MULT)
-
-        def bank(name, shape):
-            return psum.tile(shape, F32, name="acc", tag=name)
 
         def hidden_tile(j0, j1, tag):
             return held.tile([P, j1 - j0, 4], BF16, name="h", tag=tag, align_bytes=64)
@@ -257,11 +259,14 @@ def tile_list_modp_gsilu_none_kernel(
         for b in range(2):
             up_product(b)
         for a in range(2):
-            for b in range(3):
+            for b in range(2):
                 gate_pass(b, a)
+        up_product(2)
+        for a in range(2):
+            gate_pass(2, a)
 
         y_first = held.tile([P, GROUP], F32, name="y_first")
-        for b, name in ((0, "a"), (1, "b")):
+        for b, name in ((0, 6), (1, 7)):
             h = hidden_tile(b * BLOCK, (b + 1) * BLOCK, "h%d" % b)
             hidden_on_vector(b, halves, h)
             quantize_h(h, b * BLOCK, (b + 1) * BLOCK)
@@ -269,22 +274,18 @@ def tile_list_modp_gsilu_none_kernel(
             down(acc[:], 0, b * BLOCK, (b + 1) * BLOCK)
             nc.scalar.copy(y_first[:, b * BLOCK : (b + 1) * BLOCK], acc[:])
 
-        def products(b):
-            if b > 2:
-                for a in range(2):
-                    gate_pass(b, a)
-            up_product(b)
-
         h = laid.tile([P, GROUP, 4], BF16, name="h_second", offset=40960, align_bytes=64)
+        for a in range(2):
+            gate_pass(3, a)
+        up_product(3)
         for b in (2, 3):
-            products(b)
             hidden_on_vector(b, whole, h[:, b % 2 * BLOCK : (b % 2 + 1) * BLOCK])
         quantize_h(h, GROUP, HALF)
         for n, offset in ((2, 42944), (3, 32832)):
             zeroed(laid.tile([P, T], F32, name="window%d" % n, offset=offset, align_bytes=64), 0)
         place(0, 0, GROUP, y_first[:], router_first[:])
 
-        acc = bank("a", [P, 2, GROUP])
+        acc = bank(0, [P, 2, GROUP])
         for n in (1, 2):
             down(acc[:, n - 1], n, 0, GROUP)
         y_next = laid.tile([P, 2, GROUP], F32, name="y_next", offset=24576, align_bytes=64)
@@ -293,7 +294,7 @@ def tile_list_modp_gsilu_none_kernel(
             place(n, 0, GROUP, y_next[:, n - 1], router_first[:])
 
         weighted = []
-        for b, name in ((2, "b"), (3, "c")):
+        for b, name in ((2, 1), (3, 2)):
             acc = bank(name, [P, N])
             nc.tensor.matmul_mx(
                 out=acc[:],
@@ -320,23 +321,25 @@ def tile_list_modp_gsilu_none_kernel(
             for m, n in enumerate(tiles):
                 put(n, GROUP, HALF, y[:, m])
 
-        turn_back("b", (0, 1))
-        turn_back("c", (2, 3))
+        turn_back(4, (0, 1))
+        turn_back(5, (2, 3))
 
         h = laid.tile([P, HALF, 4], BF16, name="h_late", offset=25600, align_bytes=64)
         for b in range(4, 8):
-            products(b)
+            for a in range(2):
+                gate_pass(b, a)
+            up_product(b)
             hidden_on_gpsimd(b, h[:, (b - 4) * BLOCK : (b - 3) * BLOCK])
         quantize_h(h, HALF, J)
 
-        acc = bank("a", [P, GROUP])
+        acc = bank(2, [P, GROUP])
         down(acc[:], 3, 0, GROUP)
         y_rest = held.tile([P, GROUP], F32, name="y_rest", tag="act7", align_bytes=64)
         nc.scalar.copy(y_rest[:], acc[:])
         place(3, 0, GROUP, y_rest[:], router_first[:])
 
         for n in range(N // P):
-            acc = bank("bc"[n % 2 : n % 2 + 1], [P, HALF])
+            acc = bank(3 + n % 3, [P, HALF])
             down(acc[:], n, HALF, J)
             y = held.tile([P, HALF], F32, name="y_last%d" % n)
             nc.scalar.copy(y[:], acc[:])

@@ -23,7 +23,7 @@ BLOCK = 128
 GROUP = 256
 HALF = 512
 WIDE = R // 2
-SCALAR_SHARE = 64
+SCALAR_SHARE = 32
 FIRST_PICK = 384
 ZERO_PIECE = 512
 GATE_BANK = (3, 4, 5, 3, 7, 0, 7, 0)
@@ -131,34 +131,30 @@ def tile_list_modp_gsilu_none_kernel(
 
         wg_q = held.tile([P, 2, R], U32, name="wg_q", align_bytes=64)
         wg_s = held.tile([P, 2, R], U8, name="wg_s", align_bytes=64)
-        wg_bf = {
-            (a, c): held.tile([P, 2, P, 4], BF16, name="wg_bf", tag="wg_bf%d%d" % (a, c), align_bytes=64)
-            for a in range(2)
-            for c in range(2)
-        }
+        wg_bf = [held.tile([P, 4, P, 4], BF16, name="wg_bf", tag="wg_bf%d" % a, align_bytes=64) for a in range(2)]
 
-        def round_wg(copy, a, c, m0, m1):
+        def round_wg(copy, a, m0, m1):
             copy(
-                wg_bf[a, c][:, :, m0:m1].rearrange("p t m i -> p m i t"),
-                wg_raw[a][:].rearrange("p i (m t) -> p m i t", t=4)[:, m0:m1, :, 2 * c : 2 * c + 2],
+                wg_bf[a][:, :, m0:m1].rearrange("p t m i -> p m i t"),
+                wg_raw[a][:].rearrange("p i (m t) -> p m i t", t=4)[:, m0:m1],
             )
 
-        def quantize_wg(a, c):
+        def quantize_wg(a, r0, r1):
             nc.vector.quantize_mx(
-                out=wg_q[:, a, c * WIDE : (c + 1) * WIDE].bitcast(FP8X4),
-                scales=wg_s[:, a, c * WIDE : (c + 1) * WIDE],
-                in_=wg_bf[a, c][:].rearrange("p t m i -> p (t m i)"),
+                out=wg_q[:, a, r0:r1].bitcast(FP8X4),
+                scales=wg_s[:, a, r0:r1],
+                in_=wg_bf[a][:].rearrange("p t m i -> p (t m i)")[:, 4 * r0 : 4 * r1],
             )
 
-        for c in range(2):
-            round_wg(nc.scalar.copy, 0, c, 0, P)
-            quantize_wg(0, c)
-        round_wg(nc.scalar.copy, 1, 1, 0, SCALAR_SHARE)
-        round_wg(nc.vector.tensor_copy, 1, 0, 0, P)
-        round_wg(nc.vector.tensor_copy, 1, 1, SCALAR_SHARE, P)
-        quantize_wg(1, 0)
-        quantize_wg(1, 1)
-        second = held.tile([P, T], F32, name="window1", tag="wg_bf11", align_bytes=64)
+        for m0 in (0, P // 2):
+            round_wg(nc.scalar.copy, 0, m0, m0 + P // 2)
+            for t in range(4):
+                quantize_wg(0, t * P + m0, t * P + m0 + P // 2)
+        round_wg(nc.scalar.copy, 1, 0, SCALAR_SHARE)
+        round_wg(nc.vector.tensor_copy, 1, SCALAR_SHARE, P)
+        quantize_wg(1, 0, WIDE)
+        quantize_wg(1, WIDE, R)
+        second = held.tile([P, T], F32, name="window1", tag="wg_bf1", align_bytes=64)
         zeroed(second, VECTOR_ZERO)
         nc.vector.memset(second[:, 0 : VECTOR_ZERO // 2 - 1].bitcast(I32), 0)
         nc.vector.memset(second[:, VECTOR_ZERO // 2 - 1 : VECTOR_ZERO].bitcast(I32), 0)

@@ -28,7 +28,7 @@ FIRST_PICK = 384
 ZERO_PIECE = 512
 GATE_BANK = (3, 4, 5, 3, 7, 0, 7, 0)
 UP_BANK = (0, 1, 2, 0, 6, 1, 6, 1)
-VECTOR_ZERO = 688
+VECTOR_ZERO = 1024
 
 
 def tile_list_modp_gsilu_none_kernel(
@@ -334,10 +334,12 @@ def tile_list_modp_gsilu_none_kernel(
         nc.scalar.copy(y_rest[:], acc[:])
         place(3, 0, GROUP, y_rest[:], router_first[:])
 
-        for n in range(N // P):
-            acc = bank(3 + n % 3, [P, HALF])
-            down(acc[:], n, HALF, J)
-            y = held.tile([P, HALF], F32, name="y_last%d" % n)
-            nc.scalar.copy(y[:], acc[:])
-            place(n, HALF, J, y[:], router_last[:])
-            nc.sync.dma_start(out[n * P : (n + 1) * P, :], windows[n][:])
+        y_last = [held.tile([P, HALF], F32, name="y_last%d" % n) for n in range(N // P)]
+        pieces = ((0, 0, GROUP), (1, 0, HALF), (0, GROUP, HALF), (2, 0, HALF), (3, 0, HALF))
+        for turn, (n, c0, c1) in enumerate(pieces):
+            acc = bank(3 + turn % 2, [P, c1 - c0])
+            down(acc[:], n, HALF + c0, HALF + c1)
+            nc.scalar.copy(y_last[n][:, c0:c1], acc[:])
+            place(n, HALF + c0, HALF + c1, y_last[n][:, c0:c1], router_last[:, c0:c1])
+            if c1 == HALF:
+                nc.sync.dma_start(out[n * P : (n + 1) * P, :], windows[n][:])

@@ -26,8 +26,8 @@ WIDE = R // 2
 SCALAR_SHARE = 32
 FIRST_PICK = 384
 ZERO_PIECE = 512
-GATE_BANK = (3, 4, 5, 3, 7, 0, 7, 0)
-UP_BANK = (0, 1, 2, 0, 6, 1, 6, 1)
+GATE_BANK = (3, 4, 5, 3, 7, 1, 7, 1)
+UP_BANK = (0, 1, 2, 0, 6, 0, 6, 0)
 VECTOR_ZERO = 1024
 
 
@@ -167,8 +167,11 @@ def tile_list_modp_gsilu_none_kernel(
         router_last = laid.tile([P, HALF], F32, name="router_last", offset=17472, align_bytes=64)
         nc.sync.dma_start(router_last[:], wgo[:, HALF:J])
 
-        h_codes = held.tile([P, J], U32, name="h_codes", align_bytes=64)
+        h_codes = [held.tile([P, HALF], U32, name="h_codes", align_bytes=64)]
         h_scales = held.tile([P, J], U8, name="h_scales", align_bytes=64)
+
+        def codes_of(j0, j1):
+            return h_codes[j0 // HALF][:, j0 % HALF : (j1 - 1) % HALF + 1].bitcast(FP8X4)
 
         def first_pass(b, acc, codes, width, dtype, scales, a):
             apart, j = parted[b]
@@ -221,7 +224,7 @@ def tile_list_modp_gsilu_none_kernel(
 
         def hidden_on_gpsimd(b, h):
             act = silu(b, whole)
-            up = held.tile([P, BLOCK, 4], F32, name="up_out%d" % b)
+            up = held.tile([P, BLOCK, 4], F32, name="up_out", tag="up_out%d" % b, align_bytes=64)
             nc.scalar.copy(up[:], by_token(ups[b]))
             nc.gpsimd.tensor_tensor(h, up[:], act[:], MULT)
 
@@ -230,9 +233,9 @@ def tile_list_modp_gsilu_none_kernel(
 
         def quantize_h(h, j0, j1):
             nc.vector.quantize_mx(
-                out=h_codes[:, j0:j1].bitcast(FP8X4),
+                out=codes_of(j0, j1),
                 scales=h_scales[:, j0:j1],
-                in_=h[:].rearrange("p j i -> p (j i)"),
+                in_=h.rearrange("p j i -> p (j i)"),
             )
 
         def down(acc, n, j0, j1):
@@ -240,7 +243,7 @@ def tile_list_modp_gsilu_none_kernel(
                 out=acc,
                 lhsT=wd_w[:, 4 * P * n : 4 * P * (n + 1)].bitcast(FP8X4),
                 lhsT_scale=wd_s[:, P * n : P * (n + 1)],
-                rhs=h_codes[:, j0:j1].bitcast(FP8X4),
+                rhs=codes_of(j0, j1),
                 rhs_scale=h_scales[:, j0:j1],
                 start=True,
                 stop=True,
@@ -265,7 +268,7 @@ def tile_list_modp_gsilu_none_kernel(
         for b, name in ((0, 6), (1, 7)):
             h = hidden_tile(b * BLOCK, (b + 1) * BLOCK, "h%d" % b)
             hidden_on_vector(b, halves, h)
-            quantize_h(h, b * BLOCK, (b + 1) * BLOCK)
+            quantize_h(h[:], b * BLOCK, (b + 1) * BLOCK)
             acc = bank(name, [P, BLOCK])
             down(acc[:], 0, b * BLOCK, (b + 1) * BLOCK)
             nc.scalar.copy(y_first[:, b * BLOCK : (b + 1) * BLOCK], acc[:])
@@ -275,13 +278,13 @@ def tile_list_modp_gsilu_none_kernel(
             gate_pass(3, a)
         up_product(3)
         for b in (2, 3):
-            hidden_on_vector(b, whole, h[:, b % 2 * BLOCK : (b % 2 + 1) * BLOCK])
-        quantize_h(h, GROUP, HALF)
+            hidden_on_vector(b, halves, h[:, b % 2 * BLOCK : (b % 2 + 1) * BLOCK])
+        quantize_h(h[:], GROUP, HALF)
         for n, offset in ((2, 42944), (3, 32832)):
             zeroed(laid.tile([P, T], F32, name="window%d" % n, offset=offset, align_bytes=64), 0)
         place(0, 0, GROUP, y_first[:], router_first[:])
 
-        acc = bank(0, [P, 2, GROUP])
+        acc = bank(1, [P, 2, GROUP])
         for n in (1, 2):
             down(acc[:, n - 1], n, 0, GROUP)
         y_next = laid.tile([P, 2, GROUP], F32, name="y_next", offset=24576, align_bytes=64)
@@ -290,11 +293,11 @@ def tile_list_modp_gsilu_none_kernel(
             place(n, 0, GROUP, y_next[:, n - 1], router_first[:])
 
         weighted = []
-        for b, name in ((2, 1), (3, 2)):
+        for b, name in ((2, 0), (3, 2)):
             acc = bank(name, [P, N])
             nc.tensor.matmul_mx(
                 out=acc[:],
-                lhsT=h_codes[:, b * BLOCK : (b + 1) * BLOCK].bitcast(FP8X4),
+                lhsT=codes_of(b * BLOCK, (b + 1) * BLOCK),
                 lhsT_scale=h_scales[:, b * BLOCK : (b + 1) * BLOCK],
                 rhs=wd_w[:].bitcast(FP8X4),
                 rhs_scale=wd_s[:],
@@ -326,7 +329,9 @@ def tile_list_modp_gsilu_none_kernel(
                 gate_pass(b, a)
             up_product(b)
             hidden_on_gpsimd(b, h[:, (b - 4) * BLOCK : (b - 3) * BLOCK])
-        quantize_h(h, HALF, J)
+        h_codes.append(held.tile([P, HALF], U32, name="late_codes", tag="up_out7", align_bytes=64))
+        for j0 in (HALF, HALF + GROUP):
+            quantize_h(h[:, j0 - HALF : j0 - HALF + GROUP], j0, j0 + GROUP)
 
         acc = bank(2, [P, GROUP])
         down(acc[:], 3, 0, GROUP)

@@ -23,8 +23,10 @@ BLOCK = 128
 GROUP = 256
 HALF = 512
 WIDE = R // 2
-SCALAR_SHARE = 32
+SCALAR_SHARE = 40
+VECTOR_SHARE = 24
 FIRST_PICK = 384
+SECOND_PICK = 640
 ZERO_PIECE = 512
 GATE_BANK = (3, 4, 5, 3, 7, 1, 7, 1)
 UP_BANK = (0, 1, 2, 0, 6, 0, 6, 0)
@@ -112,7 +114,7 @@ def tile_list_modp_gsilu_none_kernel(
         move_scales(1)
 
         parted = {}
-        for j0, j1, offset in ((0, FIRST_PICK, 12288), (FIRST_PICK, J, 13760)):
+        for j0, j1, offset in ((0, FIRST_PICK, 12288), (FIRST_PICK, SECOND_PICK, 0), (SECOND_PICK, J, 13760)):
             pairs = laid.tile([P, j1 - j0], U32, name="pairs%d" % j0, offset=offset, align_bytes=64)
             nc.vector.tensor_copy(pairs[:], table[:].bitcast(U32).indirect(entries(j0, j1)))
             apart = held.tile([P, 2, 2 * (j1 - j0)], U8, name="apart%d" % j0, align_bytes=64)
@@ -146,8 +148,10 @@ def tile_list_modp_gsilu_none_kernel(
                 in_=wg_bf[a][:].rearrange("p t m i -> p (t m i)")[:, 4 * r0 : 4 * r1],
             )
 
+        round_wg(nc.scalar.copy, 0, 0, P // 2)
+        round_wg(nc.scalar.copy, 0, P // 2, P - VECTOR_SHARE)
+        round_wg(nc.vector.tensor_copy, 0, P - VECTOR_SHARE, P)
         for m0 in (0, P // 2):
-            round_wg(nc.scalar.copy, 0, m0, m0 + P // 2)
             for t in range(4):
                 quantize_wg(0, t * P + m0, t * P + m0 + P // 2)
         round_wg(nc.scalar.copy, 1, 0, SCALAR_SHARE)

@@ -23,14 +23,8 @@ BLOCK = 128
 GROUP = 256
 HALF = 512
 WIDE = R // 2
-SCALAR_SHARE = 40
-VECTOR_SHARE = 24
-FIRST_PICK = 384
-SECOND_PICK = 640
+SCALAR_SHARE = (50, 20)
 ZERO_PIECE = 512
-GATE_BANK = (3, 4, 5, 3, 7, 1, 7, 1)
-UP_BANK = (0, 1, 2, 0, 6, 0, 6, 0)
-VECTOR_ZERO = 1024
 
 
 def tile_list_modp_gsilu_none_kernel(
@@ -40,66 +34,81 @@ def tile_list_modp_gsilu_none_kernel(
     with ExitStack() as ctx:
         held = ctx.enter_context(tc.tile_pool(name="held", bufs=1))
         laid = ctx.enter_context(tc.tile_pool(name="laid", bufs=1))
-        ring = ctx.enter_context(tc.tile_pool(name="ring", bufs=3))
         psum = ctx.enter_context(tc.psum_pool(name="psum", bufs=1))
+
+        def lay(shape, dtype, name, offset):
+            return laid.tile(shape, dtype, name=name, offset=offset, align_bytes=64)
+
+        def keep(shape, dtype, name, tag=None):
+            return held.tile(shape, dtype, name=name, tag=tag or name, align_bytes=64)
+
+        def bank(number, shape):
+            return psum.tile(shape, F32, name="acc", tag="bank%d" % number)
 
         offsets = held.tile([P, J // 16], U16, name="offsets")
         nc.sync.dma_start(offsets[:], offs)
 
-        table_scales = laid.tile([P, T], U8, name="table_scales", offset=2048, align_bytes=64)
-        nc.scalar.dma_start(table_scales[96:P, :].bitcast(I32), tab_scales.rearrange("a s t -> s a t").bitcast(I32))
-        nc.gpsimd.memset(table_scales[0:96, :].bitcast(I32), 0)
-
-        table = held.tile([P, T], I32, name="table")
-        nc.sync.dma_start(table[:], tab_words[0].rearrange("p t b -> p (t b)").bitcast(I32))
-        wu_w = held.tile([P, 2, 2 * R], U8, name="wu_w", align_bytes=64)
-        nc.sync.dma_start(wu_w[:].bitcast(I32), wu_words.rearrange("a p b -> p a b").bitcast(I32))
-        wg_rows = wg.rearrange("(a p i) r -> a p i r", a=2, i=4)
-        wg_raw = [laid.tile([P, 4, R], F32, name="wg_first", offset=16384, align_bytes=64)]
-        nc.sync.dma_start(wg_raw[0][:], wg_rows[0])
-
-        wu_s = held.tile([P, 2, R], U8, name="wu_s", align_bytes=64)
+        wu_s = keep([P, 2, R], U8, "wu_s")
         nc.gpsimd.memset(wu_s[:].bitcast(I32), 0)
-        for q in range(4):
-            nc.scalar.dma_start(
+
+        def load_wu_scales(queue, q):
+            queue.dma_start(
                 wu_s[32 * q : 32 * q + 4, :, :].bitcast(I32),
                 wu_scales[:, 4 * q : 4 * q + 4, :].rearrange("a r n -> r a n").bitcast(I32),
             )
-        wu_dealt = held.tile([P, 2, 2 * R], U8, name="wu_dealt", align_bytes=64)
-        nc.scalar.copy(
-            wu_dealt[:].bitcast(U16).rearrange("p a (t m) -> p a t m", t=4),
-            wu_w[:].bitcast(U16).rearrange("p a (m t) -> p a t m", t=4),
-        )
+
+        table_scales = lay([P, T], U8, "table_scales", 4096)
+        nc.scalar.dma_start(table_scales[96:P, :].bitcast(I32), tab_scales.rearrange("a s t -> s a t").bitcast(I32))
+        nc.gpsimd.memset(table_scales[0:96, :].bitcast(I32), 0)
+
+        table = keep([P, T], I32, "table")
+        nc.sync.dma_start(table[:], tab_words[0].rearrange("p t b -> p (t b)").bitcast(I32))
+        wu_w = keep([P, 2, 2 * R], U8, "wu_w")
+        nc.sync.dma_start(wu_w[:].bitcast(I32), wu_words.rearrange("a p b -> p a b").bitcast(I32))
+        load_wu_scales(nc.sync, 0)
+        for q in range(1, 4):
+            load_wu_scales(nc.scalar, q)
+        wg_rows = wg.rearrange("(a p i) r -> a p i r", a=2, i=4)
+        wg_first = lay([P, 4, R], F32, "wg_first", 16384)
+        nc.sync.dma_start(wg_first[:], wg_rows[0])
+
+        wu_dealt = keep([P, 2, 2 * R], U8, "wu_dealt")
+        for a in range(2):
+            nc.scalar.copy(
+                wu_dealt[:, a].bitcast(U16).rearrange("p (t m) -> p t m", t=4),
+                wu_w[:, a].bitcast(U16).rearrange("p (m t) -> p t m", t=4),
+            )
         planes = []
         for half in range(2):
-            plane = held.tile([P, 2, HALF], U8, name="plane%d" % half, align_bytes=64)
+            plane = keep([P, 2, HALF], U8, "plane%d" % half)
             nc.gpsimd.memset(plane[:].bitcast(I32), 0)
             planes.append(plane)
-        identity = held.tile([P, P], F32, name="identity")
+        identity = keep([P, P], F32, "identity")
         make_identity(nc, identity[:])
 
-        windows = [held.tile([P, T], F32, name="window0")]
+        windows = [keep([P, T], F32, "window0")]
         nc.vector.memset(windows[0][:, 0 : T // 2 + 1].bitcast(I32), 0)
         nc.vector.memset(windows[0][:, T // 2 + 1 : T].bitcast(I32), 0)
 
-        def zeroed(window, start):
-            for c in range(start, T, ZERO_PIECE):
-                nc.gpsimd.memset(window[:, c : min(c + ZERO_PIECE, T)].bitcast(I32), 0)
+        def zeroed(window):
+            for c in range(0, T, ZERO_PIECE):
+                nc.gpsimd.memset(window[:, c : c + ZERO_PIECE].bitcast(I32), 0)
             windows.append(window)
+
+        zeroed(keep([P, T], F32, "window1"))
+        wu_s_dealt = keep([P, 2, R], U8, "wu_s_dealt")
+        nc.gpsimd.tensor_copy(
+            wu_s_dealt[:].rearrange("p a (t m) -> p a t m", t=4), wu_s[:].rearrange("p a (m t) -> p a t m", t=4)
+        )
 
         def entries(j0, j1):
             return offsets[:, j0 // 16 : j1 // 16]
 
         picked = []
         for half in range(2):
-            rows = held.tile([P, HALF], U8, name="picked%d" % half, align_bytes=64)
+            rows = keep([P, HALF], U8, "picked%d" % half)
             nc.vector.tensor_copy(rows[:], table_scales[:].indirect(entries(half * HALF, (half + 1) * HALF)))
             picked.append(rows)
-
-        wu_s_dealt = held.tile([P, 2, R], U8, name="wu_s_dealt", align_bytes=64)
-        nc.vector.tensor_copy(
-            wu_s_dealt[:].rearrange("p a (t m) -> p a t m", t=4), wu_s[:].rearrange("p a (m t) -> p a t m", t=4)
-        )
 
         def move_scales(half):
             for q in range(4):
@@ -109,131 +118,129 @@ def tile_list_modp_gsilu_none_kernel(
                 )
 
         move_scales(0)
-        wg_raw.append(laid.tile([P, 4, R], F32, name="wg_last", offset=4032, align_bytes=64))
-        nc.sync.dma_start(wg_raw[1][:], wg_rows[1])
+        wg_last = []
+        for half, offset in enumerate((6080, 64)):
+            raw = lay([P, 4, WIDE], F32, "wg_last%d" % half, offset)
+            nc.sync.dma_start(raw[:], wg_rows[1][:, :, half * WIDE : (half + 1) * WIDE])
+            wg_last.append(raw)
         move_scales(1)
 
         parted = {}
-        for j0, j1, offset in ((0, FIRST_PICK, 12288), (FIRST_PICK, SECOND_PICK, 0), (SECOND_PICK, J, 13760)):
-            pairs = laid.tile([P, j1 - j0], U32, name="pairs%d" % j0, offset=offset, align_bytes=64)
+
+        def pick_words(pairs, j0, j1):
             nc.vector.tensor_copy(pairs[:], table[:].bitcast(U32).indirect(entries(j0, j1)))
-            apart = held.tile([P, 2, 2 * (j1 - j0)], U8, name="apart%d" % j0, align_bytes=64)
+
+        def part_words(pairs, j0, j1):
+            apart = keep([P, 2, 2 * (j1 - j0)], U8, "apart%d" % j0)
             nc.vector.tensor_copy(apart[:].bitcast(U16), pairs[:].bitcast(U16).rearrange("p (j d) -> p d j", d=2))
             for j in range(j0, j1, BLOCK):
                 parted[j // BLOCK] = (apart, j - j0)
 
-        wd_w = laid.tile([P, 4 * N], U8, name="wd_w", offset=13824, align_bytes=64)
+        early = [
+            (lay([P, GROUP], U32, "pairs_first", 12288), 0, GROUP),
+            (lay([P, HALF], U32, "pairs_next", 14336), GROUP, HALF + GROUP),
+        ]
+        for piece in early:
+            pick_words(*piece)
+        for piece in early:
+            part_words(*piece)
+
+        wd_w = lay([P, 4 * N], U8, "wd_w", 14336)
         nc.sync.dma_start(wd_w[:].bitcast(I32), wd_words[0].rearrange("p n i -> p (n i)").bitcast(I32))
-        wd_s = laid.tile([P, N], U8, name="wd_s", offset=12288, align_bytes=64)
+        wd_s = lay([P, N], U8, "wd_s", 12288)
         nc.gpsimd.memset(wd_s[:].bitcast(I32), 0)
         for q in range(4):
             nc.sync.dma_start(
                 wd_s[32 * q : 32 * q + 4, :].bitcast(I32), wd_scales[0, 4 * q : 4 * q + 4, :].bitcast(I32)
             )
 
-        wg_q = held.tile([P, 2, R], U32, name="wg_q", align_bytes=64)
-        wg_s = held.tile([P, 2, R], U8, name="wg_s", align_bytes=64)
-        wg_bf = [held.tile([P, 4, P, 4], BF16, name="wg_bf", tag="wg_bf%d" % a, align_bytes=64) for a in range(2)]
+        wg_q = keep([P, 2, R], U32, "wg_q")
+        wg_s = keep([P, 2, R], U8, "wg_s", tag="wu_s")
+        rounded = [keep([P, 4, P, 4], BF16, "wg_bf%d" % a) for a in range(2)]
 
-        def round_wg(copy, a, m0, m1):
+        def round_wg(copy, a, raw, base, m0, m1, t0, t1):
             copy(
-                wg_bf[a][:, :, m0:m1].rearrange("p t m i -> p m i t"),
-                wg_raw[a][:].rearrange("p i (m t) -> p m i t", t=4)[:, m0:m1],
+                rounded[a][:, t0:t1, base + m0 : base + m1].rearrange("p t m i -> p m i t"),
+                raw[:].rearrange("p i (m t) -> p m i t", t=4)[:, m0:m1, :, t0:t1],
             )
 
         def quantize_wg(a, r0, r1):
             nc.vector.quantize_mx(
                 out=wg_q[:, a, r0:r1].bitcast(FP8X4),
                 scales=wg_s[:, a, r0:r1],
-                in_=wg_bf[a][:].rearrange("p t m i -> p (t m i)")[:, 4 * r0 : 4 * r1],
+                in_=rounded[a][:].rearrange("p t m i -> p (t m i)")[:, 4 * r0 : 4 * r1],
             )
 
-        round_wg(nc.scalar.copy, 0, 0, P // 2)
-        round_wg(nc.scalar.copy, 0, P // 2, P - VECTOR_SHARE)
-        round_wg(nc.vector.tensor_copy, 0, P - VECTOR_SHARE, P)
-        for m0 in (0, P // 2):
-            for t in range(4):
-                quantize_wg(0, t * P + m0, t * P + m0 + P // 2)
-        round_wg(nc.scalar.copy, 1, 0, SCALAR_SHARE)
-        round_wg(nc.vector.tensor_copy, 1, SCALAR_SHARE, P)
-        quantize_wg(1, 0, WIDE)
-        quantize_wg(1, WIDE, R)
-        second = held.tile([P, T], F32, name="window1", tag="wg_bf1", align_bytes=64)
-        zeroed(second, VECTOR_ZERO)
-        nc.vector.memset(second[:, 0 : VECTOR_ZERO // 2 - 1].bitcast(I32), 0)
-        nc.vector.memset(second[:, VECTOR_ZERO // 2 - 1 : VECTOR_ZERO].bitcast(I32), 0)
+        middle = P // 2
+        round_wg(nc.scalar.copy, 0, wg_first, 0, 0, SCALAR_SHARE[0], 0, 4)
+        round_wg(nc.vector.tensor_copy, 0, wg_first, 0, SCALAR_SHARE[0], P, 0, 4)
+        for r0 in (0, WIDE):
+            quantize_wg(0, r0, r0 + WIDE)
+        round_wg(nc.scalar.copy, 1, wg_last[0], 0, 0, SCALAR_SHARE[1], 0, 4)
+        round_wg(nc.vector.tensor_copy, 1, wg_last[0], 0, SCALAR_SHARE[1], middle, 0, 4)
+        for t in range(4):
+            quantize_wg(1, t * P, t * P + middle)
+        for t0 in (0, 2):
+            round_wg(nc.vector.tensor_copy, 1, wg_last[1], middle, 0, middle, t0, t0 + 2)
+        for t in range(4):
+            quantize_wg(1, t * P + middle, (t + 1) * P)
 
-        router_first = laid.tile([P, GROUP], F32, name="router_first", offset=16384, align_bytes=64)
+        late = (keep([P, GROUP], U32, "pairs_last", tag="wg_bf1"), HALF + GROUP, J)
+        pick_words(*late)
+        part_words(*late)
+
+        router_first = lay([P, GROUP], F32, "router_first", 16384)
         nc.sync.dma_start(router_first[:], wgo[:, 0:GROUP])
-        router_turned = laid.tile([P, 2], F32, name="router_turned", offset=17408, align_bytes=64)
+        router_turned = lay([P, 2], F32, "router_turned", 17408)
         with nc.allow_non_contiguous_dma(reason="one router weight for each partition"):
             nc.sync.dma_start(router_turned[:], wgo[0, GROUP:HALF].rearrange("(c p) -> p c", p=P))
-        router_last = laid.tile([P, HALF], F32, name="router_last", offset=17472, align_bytes=64)
+        router_last = lay([P, HALF], F32, "router_last", 17472)
         nc.sync.dma_start(router_last[:], wgo[:, HALF:J])
 
-        h_codes = [held.tile([P, HALF], U32, name="h_codes", align_bytes=64)]
-        h_scales = held.tile([P, J], U8, name="h_scales", align_bytes=64)
+        h_codes = [keep([P, HALF], U32, "h_codes")]
+        h_scales = keep([P, J], U8, "h_scales")
 
         def codes_of(j0, j1):
             return h_codes[j0 // HALF][:, j0 % HALF : (j1 - 1) % HALF + 1].bitcast(FP8X4)
 
-        def first_pass(b, acc, codes, width, dtype, scales, a):
+        def first_stage(acc, b, tokens, slices, passes, codes, width, dtype, scales):
             apart, j = parted[b]
-            for t in range(4):
+            c = b * BLOCK % HALF
+            steps = [(a, t) for a in passes for t in slices]
+            for a, t in steps:
                 nc.tensor.matmul_mx(
-                    out=acc[:, t],
+                    out=acc[:, t - slices[0]],
                     lhsT=codes[:, a, width * P * t : width * P * (t + 1)].bitcast(dtype),
                     lhsT_scale=scales[:, a, P * t : P * (t + 1)],
-                    rhs=apart[:, a, 2 * j : 2 * (j + BLOCK)].bitcast(FP4X4),
-                    rhs_scale=planes[b * BLOCK // HALF][:, a, b * BLOCK % HALF : b * BLOCK % HALF + BLOCK],
-                    start=(a == 0 and t == 0),
-                    stop=(a == 1 and t == 3),
+                    rhs=apart[:, a, 2 * j : 2 * (j + tokens)].bitcast(FP4X4),
+                    rhs_scale=planes[b * BLOCK // HALF][:, a, c : c + tokens],
+                    start=(a, t) == steps[0],
+                    stop=(a, t) == steps[-1],
                 )
+            return acc
 
-        def bank(number, shape):
-            return psum.tile(shape, F32, name="acc", tag="bank%d" % number)
+        def up_sums(number, b):
+            return first_stage(bank(number, [P, 4, BLOCK]), b, BLOCK, range(4), (0, 1), wu_dealt, 2, FP4X4, wu_s_dealt)
 
-        gates = {}
-        ups = {}
+        def gate_sums(number, b):
+            return first_stage(bank(number, [P, 4, BLOCK]), b, BLOCK, range(4), (0, 1), wg_q, 1, FP8X4, wg_s)
 
-        def gate_pass(b, a):
-            if a == 0:
-                gates[b] = bank(GATE_BANK[b], [P, 4, BLOCK])
-            first_pass(b, gates[b], wg_q, 1, FP8X4, wg_s, a)
+        def gate_pair(number, g, u, passes):
+            acc = bank(number, [P, 2, GROUP])
+            return first_stage(acc, 2 * g, GROUP, range(2 * u, 2 * u + 2), passes, wg_q, 1, FP8X4, wg_s)
 
-        def up_product(b):
-            ups[b] = bank(UP_BANK[b], [P, 4, BLOCK])
-            for a in range(2):
-                first_pass(b, ups[b], wu_dealt, 2, FP4X4, wu_s_dealt, a)
+        def silu_pair(act, gates, c, u, j0, j1):
+            nc.scalar.activation(
+                act[:, u, j0:j1], gates[u][:, :, c * BLOCK + j0 : c * BLOCK + j1].rearrange("p e j -> p j e"), SILU
+            )
 
-        def by_token(acc):
-            return acc[:].rearrange("p t j -> p j t")
-
-        halves = (slice(0, BLOCK // 2), slice(BLOCK // 2, BLOCK))
-        whole = (slice(0, BLOCK),)
-
-        def silu(b, parts):
-            if b == 3:
-                act = laid.tile([P, BLOCK, 4], F32, name="act3", offset=24576, align_bytes=64)
-            else:
-                act = held.tile([P, BLOCK, 4], F32, name="act", tag="act%d" % b, align_bytes=64)
-            for part in parts:
-                nc.scalar.activation(act[:, part], by_token(gates[b])[:, part], SILU)
-            return act
-
-        def hidden_on_vector(b, parts, h):
-            act = silu(b, parts)
-            for part in parts:
-                nc.vector.tensor_tensor(h[:, part], by_token(ups[b])[:, part], act[:, part], MULT)
-
-        def hidden_on_gpsimd(b, h):
-            act = silu(b, whole)
-            up = held.tile([P, BLOCK, 4], F32, name="up_out", tag="up_out%d" % b, align_bytes=64)
-            nc.scalar.copy(up[:], by_token(ups[b]))
-            nc.gpsimd.tensor_tensor(h, up[:], act[:], MULT)
-
-        def hidden_tile(j0, j1, tag):
-            return held.tile([P, j1 - j0, 4], BF16, name="h", tag=tag, align_bytes=64)
+        def product(h, c, up, act, j0, j1):
+            nc.vector.tensor_tensor(
+                h[:, c * BLOCK + j0 : c * BLOCK + j1].rearrange("p j (u e) -> p j u e", u=2),
+                up[:, :, j0:j1].rearrange("p (u e) j -> p j u e", u=2),
+                act[:, :, j0:j1].rearrange("p u j e -> p j u e"),
+                MULT,
+            )
 
         def quantize_h(h, j0, j1):
             nc.vector.quantize_mx(
@@ -259,94 +266,105 @@ def tile_list_modp_gsilu_none_kernel(
         def put(n, j0, j1, y):
             nc.vector.tensor_copy(windows[n][:].indirect(entries(j0, j1)), y)
 
-        for b in range(2):
-            up_product(b)
-        for a in range(2):
-            for b in range(2):
-                gate_pass(b, a)
-        up_product(2)
-        for a in range(2):
-            gate_pass(2, a)
+        ups = [up_sums(b, b) for b in range(2)]
+        gates = [[gate_pair(2 + u, 0, u, (0, 1)) for u in range(2)]]
+        gates.append([gate_pair(4 + u, 1, u, (1, 0)) for u in range(2)])
+        acts = [keep([P, 2, BLOCK, 2], F32, "act%d" % b) for b in range(3)]
+        acts.append(lay([P, 2, BLOCK, 2], F32, "act3", 24576))
+        h_first = lay([P, GROUP, 4], BF16, "h_first", 30720)
+        h_second = lay([P, GROUP, 4], BF16, "h_second", 40960)
 
-        y_first = held.tile([P, GROUP], F32, name="y_first")
-        for b, name in ((0, 6), (1, 7)):
-            h = hidden_tile(b * BLOCK, (b + 1) * BLOCK, "h%d" % b)
-            hidden_on_vector(b, halves, h)
-            quantize_h(h[:], b * BLOCK, (b + 1) * BLOCK)
-            acc = bank(name, [P, BLOCK])
-            down(acc[:], 0, b * BLOCK, (b + 1) * BLOCK)
-            nc.scalar.copy(y_first[:, b * BLOCK : (b + 1) * BLOCK], acc[:])
+        y_first = keep([P, GROUP], F32, "y_first")
+        for c in range(2):
+            silu_pair(acts[c], gates[0], c, 0, 0, BLOCK)
+            for j0, j1 in ((0, middle), (middle, BLOCK)):
+                silu_pair(acts[c], gates[0], c, 1, j0, j1)
+                product(h_first, c, ups[c], acts[c], j0, j1)
+            j0, j1 = c * BLOCK, (c + 1) * BLOCK
+            quantize_h(h_first[:, j0:j1], j0, j1)
+            acc = bank(6 + c, [P, BLOCK])
+            down(acc[:], 0, j0, j1)
+            nc.scalar.copy(y_first[:, j0:j1], acc[:])
 
-        h = laid.tile([P, GROUP, 4], BF16, name="h_second", offset=40960, align_bytes=64)
-        for a in range(2):
-            gate_pass(3, a)
-        up_product(3)
-        for b in (2, 3):
-            hidden_on_vector(b, halves, h[:, b % 2 * BLOCK : (b % 2 + 1) * BLOCK])
-        quantize_h(h[:], GROUP, HALF)
-        for n, offset in ((2, 42944), (3, 32832)):
-            zeroed(laid.tile([P, T], F32, name="window%d" % n, offset=offset, align_bytes=64), 0)
-        place(0, 0, GROUP, y_first[:], router_first[:])
+        ups.extend(up_sums(2 + c, 2 + c) for c in range(2))
+        for c in range(2):
+            for u in range(2):
+                silu_pair(acts[2 + c], gates[1], c, u, 0, BLOCK)
+        zeroed(lay([P, T], F32, "window2", 32704))
+        for c in range(2):
+            for j0, j1 in ((0, middle), (middle, BLOCK)):
+                product(h_second, c, ups[2 + c], acts[2 + c], j0, j1)
+            if c == 1:
+                place(0, 0, GROUP, y_first[:], router_first[:])
+            j0, j1 = c * BLOCK, (c + 1) * BLOCK
+            quantize_h(h_second[:, j0:j1], GROUP + j0, GROUP + j1)
+        zeroed(lay([P, T], F32, "window3", 42944))
 
-        acc = bank(1, [P, 2, GROUP])
+        acc = bank(0, [P, 2, GROUP])
         for n in (1, 2):
             down(acc[:, n - 1], n, 0, GROUP)
-        y_next = laid.tile([P, 2, GROUP], F32, name="y_next", offset=24576, align_bytes=64)
+        y_next = lay([P, 2, GROUP], F32, "y_next", 24576)
         nc.scalar.copy(y_next[:], acc[:])
         for n in (1, 2):
             place(n, 0, GROUP, y_next[:, n - 1], router_first[:])
 
         weighted = []
-        for b, name in ((2, 0), (3, 2)):
-            acc = bank(name, [P, N])
-            nc.tensor.matmul_mx(
-                out=acc[:],
-                lhsT=codes_of(b * BLOCK, (b + 1) * BLOCK),
-                lhsT_scale=h_scales[:, b * BLOCK : (b + 1) * BLOCK],
-                rhs=wd_w[:].bitcast(FP8X4),
-                rhs_scale=wd_s[:],
-                start=True,
-                stop=True,
-            )
-            rows = held.tile([P, N], F32, name="weighted%d" % b)
-            nc.scalar.activation(rows[:], acc[:], COPY, scale=router_turned[:, b - 2 : b - 1])
+        for c in range(2):
+            j0, j1 = GROUP + c * BLOCK, GROUP + (c + 1) * BLOCK
+            rows = keep([P, N], F32, "weighted%d" % c)
+            acc = bank((1, 4)[c], [P, N])
+            for n0 in (0, N // 2):
+                n1 = n0 + N // 2
+                nc.tensor.matmul_mx(
+                    out=acc[:, n0:n1],
+                    lhsT=codes_of(j0, j1),
+                    lhsT_scale=h_scales[:, j0:j1],
+                    rhs=wd_w[:, 4 * n0 : 4 * n1].bitcast(FP8X4),
+                    rhs_scale=wd_s[:, n0:n1],
+                    start=True,
+                    stop=True,
+                )
+            for n0 in (0, N // 2):
+                n1 = n0 + N // 2
+                nc.scalar.activation(rows[:, n0:n1], acc[:, n0:n1], COPY, scale=router_turned[:, c : c + 1])
             weighted.append(rows)
 
-        def turn_back(name, tiles):
-            back = bank(name, [P, len(tiles), GROUP])
-            for m, n in enumerate(tiles):
-                for c in range(2):
-                    nc.tensor.transpose(
-                        back[:, m, c * BLOCK : (c + 1) * BLOCK], weighted[c][:, n * P : (n + 1) * P], identity[:]
-                    )
-            y = held.tile([P, len(tiles), GROUP], F32, name="y_back%d" % tiles[0])
+        for n in range(N // P):
+            back = bank(2 + n % 2, [P, GROUP])
+            for c in range(2):
+                nc.tensor.transpose(
+                    back[:, c * BLOCK : (c + 1) * BLOCK], weighted[c][:, n * P : (n + 1) * P], identity[:]
+                )
+            y = keep([P, GROUP], F32, "y_back%d" % n)
             nc.scalar.copy(y[:], back[:])
-            for m, n in enumerate(tiles):
-                put(n, GROUP, HALF, y[:, m])
+            put(n, GROUP, HALF, y[:])
 
-        turn_back(4, (0, 1))
-        turn_back(5, (2, 3))
+        def by_token(acc):
+            return acc[:].rearrange("p t j -> p j t")
 
-        h = laid.tile([P, HALF, 4], BF16, name="h_late", offset=25600, align_bytes=64)
+        h_late = lay([P, HALF, 4], BF16, "h_late", 25600)
         for b in range(4, 8):
-            for a in range(2):
-                gate_pass(b, a)
-            up_product(b)
-            hidden_on_gpsimd(b, h[:, (b - 4) * BLOCK : (b - 3) * BLOCK])
-        h_codes.append(held.tile([P, HALF], U32, name="late_codes", tag="up_out7", align_bytes=64))
+            gate = gate_sums((7, 0)[b % 2], b)
+            up = up_sums((6, 1)[b % 2], b)
+            act = keep([P, BLOCK, 4], F32, "act%d" % b)
+            nc.scalar.activation(act[:], by_token(gate), SILU)
+            up_out = keep([P, BLOCK, 4], F32, "up_out%d" % b)
+            nc.scalar.copy(up_out[:], by_token(up))
+            nc.gpsimd.tensor_tensor(h_late[:, (b - 4) * BLOCK : (b - 3) * BLOCK], up_out[:], act[:], MULT)
+        h_codes.append(keep([P, HALF], U32, "late_codes", tag="up_out7"))
         for j0 in (HALF, HALF + GROUP):
-            quantize_h(h[:, j0 - HALF : j0 - HALF + GROUP], j0, j0 + GROUP)
+            quantize_h(h_late[:, j0 - HALF : j0 - HALF + GROUP], j0, j0 + GROUP)
 
         acc = bank(2, [P, GROUP])
         down(acc[:], 3, 0, GROUP)
-        y_rest = held.tile([P, GROUP], F32, name="y_rest", tag="act7", align_bytes=64)
+        y_rest = keep([P, GROUP], F32, "y_rest", tag="act7")
         nc.scalar.copy(y_rest[:], acc[:])
         place(3, 0, GROUP, y_rest[:], router_first[:])
 
-        y_last = [held.tile([P, HALF], F32, name="y_last%d" % n) for n in range(N // P)]
+        y_last = [keep([P, HALF], F32, "y_last%d" % n) for n in range(N // P)]
         pieces = ((0, 0, GROUP), (1, 0, HALF), (0, GROUP, HALF), (2, 0, HALF), (3, 0, HALF))
         for turn, (n, c0, c1) in enumerate(pieces):
-            acc = bank(3 + turn % 2, [P, c1 - c0])
+            acc = bank(4 + turn % 2, [P, c1 - c0])
             down(acc[:], n, HALF + c0, HALF + c1)
             nc.scalar.copy(y_last[n][:, c0:c1], acc[:])
             place(n, HALF + c0, HALF + c1, y_last[n][:, c0:c1], router_last[:, c0:c1])

@@ -271,7 +271,7 @@ def tile_list_modp_gsilu_none_kernel(
         gates.append([gate_pair(4 + u, 1, u, (1, 0)) for u in range(2)])
         acts = [keep([P, 2, BLOCK, 2], F32, "act%d" % b) for b in range(3)]
         acts.append(lay([P, 2, BLOCK, 2], F32, "act3", 24576))
-        h_first = lay([P, GROUP, 4], BF16, "h_first", 30720)
+        h_first = keep([P, GROUP, 4], BF16, "h_first")
         h_second = lay([P, GROUP, 4], BF16, "h_second", 40960)
 
         y_first = keep([P, GROUP], F32, "y_first")
@@ -290,7 +290,6 @@ def tile_list_modp_gsilu_none_kernel(
         for c in range(2):
             for u in range(2):
                 silu_pair(acts[2 + c], gates[1], c, u, 0, BLOCK)
-        zeroed(lay([P, T], F32, "window2", 32704))
         for c in range(2):
             for j0, j1 in ((0, middle), (middle, BLOCK)):
                 product(h_second, c, ups[2 + c], acts[2 + c], j0, j1)
@@ -298,7 +297,8 @@ def tile_list_modp_gsilu_none_kernel(
                 place(0, 0, GROUP, y_first[:], router_first[:])
             j0, j1 = c * BLOCK, (c + 1) * BLOCK
             quantize_h(h_second[:, j0:j1], GROUP + j0, GROUP + j1)
-        zeroed(lay([P, T], F32, "window3", 42944))
+        for n, offset in ((2, 32832), (3, 42944)):
+            zeroed(lay([P, T], F32, "window%d" % n, offset))
 
         acc = bank(0, [P, 2, GROUP])
         for n in (1, 2):

@@ -23,7 +23,8 @@ BLOCK = 128
 GROUP = 256
 HALF = 512
 WIDE = R // 2
-SCALAR_SHARE = (50, 20)
+LEAD = 3 * R // 4
+SCALAR_SHARE = (56, 36, 20)
 ZERO_PIECE = 512
 
 
@@ -58,19 +59,22 @@ def tile_list_modp_gsilu_none_kernel(
             )
 
         table_scales = lay([P, T], U8, "table_scales", 4096)
-        nc.scalar.dma_start(table_scales[96:P, :].bitcast(I32), tab_scales.rearrange("a s t -> s a t").bitcast(I32))
+        nc.sync.dma_start(table_scales[96:P, :].bitcast(I32), tab_scales.rearrange("a s t -> s a t").bitcast(I32))
         nc.gpsimd.memset(table_scales[0:96, :].bitcast(I32), 0)
 
         table = keep([P, T], I32, "table")
         nc.sync.dma_start(table[:], tab_words[0].rearrange("p t b -> p (t b)").bitcast(I32))
+        for q in range(4):
+            load_wu_scales((nc.sync, nc.scalar)[q % 2], q)
         wu_w = keep([P, 2, 2 * R], U8, "wu_w")
         nc.sync.dma_start(wu_w[:].bitcast(I32), wu_words.rearrange("a p b -> p a b").bitcast(I32))
-        load_wu_scales(nc.sync, 0)
-        for q in range(1, 4):
-            load_wu_scales(nc.scalar, q)
         wg_rows = wg.rearrange("(a p i) r -> a p i r", a=2, i=4)
-        wg_first = lay([P, 4, R], F32, "wg_first", 16384)
-        nc.sync.dma_start(wg_first[:], wg_rows[0])
+        wg_first = lay([P, 4, LEAD], F32, "wg_first", 16384)
+        nc.sync.dma_start(wg_first[:], wg_rows[0][:, :, 0:LEAD])
+
+        warm = keep([P, 2], F32, "warm")
+        nc.gpsimd.memset(warm[:, 0:1], 0.0)
+        nc.scalar.activation(warm[:, 1:2], warm[:, 0:1], SILU)
 
         wu_dealt = keep([P, 2, 2 * R], U8, "wu_dealt")
         for a in range(2):
@@ -118,11 +122,13 @@ def tile_list_modp_gsilu_none_kernel(
                 )
 
         move_scales(0)
+        wg_next = lay([P, 4, R - LEAD], F32, "wg_next", 2112)
+        nc.sync.dma_start(wg_next[:], wg_rows[0][:, :, LEAD:R])
+        wg_halves = lay([P, 2, 4, WIDE], F32, "wg_halves", 6080)
         wg_last = []
-        for half, offset in enumerate((6080, 64)):
-            raw = lay([P, 4, WIDE], F32, "wg_last%d" % half, offset)
-            nc.sync.dma_start(raw[:], wg_rows[1][:, :, half * WIDE : (half + 1) * WIDE])
-            wg_last.append(raw)
+        for half in range(2):
+            nc.sync.dma_start(wg_halves[:, half], wg_rows[1][:, :, half * WIDE : (half + 1) * WIDE])
+            wg_last.append(wg_halves[:, half])
         move_scales(1)
 
         parted = {}
@@ -137,8 +143,8 @@ def tile_list_modp_gsilu_none_kernel(
                 parted[j // BLOCK] = (apart, j - j0)
 
         early = [
-            (lay([P, GROUP], U32, "pairs_first", 12288), 0, GROUP),
-            (lay([P, HALF], U32, "pairs_next", 14336), GROUP, HALF + GROUP),
+            (lay([P, GROUP], U32, "pairs_first", 59264), 0, GROUP),
+            (lay([P, GROUP + BLOCK], U32, "pairs_next", 14336), GROUP, HALF + BLOCK),
         ]
         for piece in early:
             pick_words(*piece)
@@ -147,7 +153,7 @@ def tile_list_modp_gsilu_none_kernel(
 
         wd_w = lay([P, 4 * N], U8, "wd_w", 14336)
         nc.sync.dma_start(wd_w[:].bitcast(I32), wd_words[0].rearrange("p n i -> p (n i)").bitcast(I32))
-        wd_s = lay([P, N], U8, "wd_s", 12288)
+        wd_s = lay([P, N], U8, "wd_s", 59264)
         nc.gpsimd.memset(wd_s[:].bitcast(I32), 0)
         for q in range(4):
             nc.sync.dma_start(
@@ -173,21 +179,29 @@ def tile_list_modp_gsilu_none_kernel(
 
         middle = P // 2
         round_wg(nc.scalar.copy, 0, wg_first, 0, 0, SCALAR_SHARE[0], 0, 4)
-        round_wg(nc.vector.tensor_copy, 0, wg_first, 0, SCALAR_SHARE[0], P, 0, 4)
+        round_wg(nc.vector.tensor_copy, 0, wg_first, 0, SCALAR_SHARE[0], LEAD // 4, 0, 4)
+        round_wg(nc.vector.tensor_copy, 0, wg_next, LEAD // 4, 0, P - LEAD // 4, 0, 4)
         for r0 in (0, WIDE):
             quantize_wg(0, r0, r0 + WIDE)
         round_wg(nc.scalar.copy, 1, wg_last[0], 0, 0, SCALAR_SHARE[1], 0, 4)
         round_wg(nc.vector.tensor_copy, 1, wg_last[0], 0, SCALAR_SHARE[1], middle, 0, 4)
         for t in range(4):
             quantize_wg(1, t * P, t * P + middle)
+        round_wg(nc.scalar.copy, 1, wg_last[1], middle, 0, SCALAR_SHARE[2], 0, 4)
         for t0 in (0, 2):
-            round_wg(nc.vector.tensor_copy, 1, wg_last[1], middle, 0, middle, t0, t0 + 2)
+            round_wg(nc.vector.tensor_copy, 1, wg_last[1], middle, SCALAR_SHARE[2], middle, t0, t0 + 2)
         for t in range(4):
             quantize_wg(1, t * P + middle, (t + 1) * P)
 
-        late = (keep([P, GROUP], U32, "pairs_last", tag="wg_bf1"), HALF + GROUP, J)
-        pick_words(*late)
-        part_words(*late)
+        pairs_last = keep([P, J - HALF - BLOCK], U32, "pairs_last", tag="wg_bf1")
+        late = [
+            (pairs_last[:, 0:GROUP], HALF + BLOCK, J - BLOCK),
+            (pairs_last[:, GROUP : GROUP + BLOCK], J - BLOCK, J),
+        ]
+        for piece in late:
+            pick_words(*piece)
+        for piece in late:
+            part_words(*piece)
 
         router_first = lay([P, GROUP], F32, "router_first", 16384)
         nc.sync.dma_start(router_first[:], wgo[:, 0:GROUP])

@@ -24,7 +24,7 @@ GROUP = 256
 HALF = 512
 WIDE = R // 2
 LEAD = 3 * R // 4
-SCALAR_SHARE = (56, 36, 20)
+SCALAR_SHARE = (60, 38, 20)
 ZERO_PIECE = 512
 
 
@@ -143,7 +143,7 @@ def tile_list_modp_gsilu_none_kernel(
                 parted[j // BLOCK] = (apart, j - j0)
 
         early = [
-            (lay([P, GROUP], U32, "pairs_first", 59264), 0, GROUP),
+            (keep([P, GROUP], U32, "pairs_first"), 0, GROUP),
             (lay([P, GROUP + BLOCK], U32, "pairs_next", 14336), GROUP, HALF + BLOCK),
         ]
         for piece in early:
@@ -153,7 +153,7 @@ def tile_list_modp_gsilu_none_kernel(
 
         wd_w = lay([P, 4 * N], U8, "wd_w", 14336)
         nc.sync.dma_start(wd_w[:].bitcast(I32), wd_words[0].rearrange("p n i -> p (n i)").bitcast(I32))
-        wd_s = lay([P, N], U8, "wd_s", 59264)
+        wd_s = lay([P, N], U8, "wd_s", 4608)
         nc.gpsimd.memset(wd_s[:].bitcast(I32), 0)
         for q in range(4):
             nc.sync.dma_start(
@@ -294,6 +294,7 @@ def tile_list_modp_gsilu_none_kernel(
             for j0, j1 in ((0, middle), (middle, BLOCK)):
                 silu_pair(acts[c], gates[0], c, 1, j0, j1)
                 product(h_first, c, ups[c], acts[c], j0, j1)
+        for c in range(2):
             j0, j1 = c * BLOCK, (c + 1) * BLOCK
             quantize_h(h_first[:, j0:j1], j0, j1)
             acc = bank(6 + c, [P, BLOCK])

@@ -136,20 +136,23 @@ def tile_list_modp_gsilu_none_kernel(
         def pick_words(pairs, j0, j1):
             nc.vector.tensor_copy(pairs[:], table[:].bitcast(U32).indirect(entries(j0, j1)))
 
-        def part_words(pairs, j0, j1):
-            apart = keep([P, 2, 2 * (j1 - j0)], U8, "apart%d" % j0)
+        def part_words(pairs, j0, j1, apart=None):
+            if apart is None:
+                apart = keep([P, 2, 2 * (j1 - j0)], U8, "apart%d" % j0)
             nc.vector.tensor_copy(apart[:].bitcast(U16), pairs[:].bitcast(U16).rearrange("p (j d) -> p d j", d=2))
             for j in range(j0, j1, BLOCK):
                 parted[j // BLOCK] = (apart, j - j0)
 
         early = [
-            (keep([P, GROUP], U32, "pairs_first"), 0, GROUP),
+            (lay([P, GROUP], U32, "pairs_first", 59264), 0, GROUP),
             (lay([P, GROUP + BLOCK], U32, "pairs_next", 14336), GROUP, HALF + BLOCK),
         ]
         for piece in early:
             pick_words(*piece)
         for piece in early:
             part_words(*piece)
+        last = (lay([P, BLOCK], U32, "pairs_last", 59264), J - BLOCK, J)
+        pick_words(*last)
 
         wd_w = lay([P, 4 * N], U8, "wd_w", 14336)
         nc.sync.dma_start(wd_w[:].bitcast(I32), wd_words[0].rearrange("p n i -> p (n i)").bitcast(I32))
@@ -193,15 +196,10 @@ def tile_list_modp_gsilu_none_kernel(
         for t in range(4):
             quantize_wg(1, t * P + middle, (t + 1) * P)
 
-        pairs_last = keep([P, J - HALF - BLOCK], U32, "pairs_last", tag="wg_bf1")
-        late = [
-            (pairs_last[:, 0:GROUP], HALF + BLOCK, J - BLOCK),
-            (pairs_last[:, GROUP : GROUP + BLOCK], J - BLOCK, J),
-        ]
-        for piece in late:
-            pick_words(*piece)
-        for piece in late:
-            part_words(*piece)
+        late = (lay([P, GROUP], U32, "pairs_late", 8192), HALF + BLOCK, J - BLOCK)
+        pick_words(*late)
+        part_words(*last, lay([P, 2, 2 * BLOCK], U8, "apart_last", 10240))
+        part_words(*late)
 
         router_first = lay([P, GROUP], F32, "router_first", 16384)
         nc.sync.dma_start(router_first[:], wgo[:, 0:GROUP])
@@ -239,9 +237,9 @@ def tile_list_modp_gsilu_none_kernel(
         def gate_sums(number, b):
             return first_stage(bank(number, [P, 4, BLOCK]), b, BLOCK, range(4), (0, 1), wg_q, 1, FP8X4, wg_s)
 
-        def gate_pair(number, g, u, passes):
-            acc = bank(number, [P, 2, GROUP])
-            return first_stage(acc, 2 * g, GROUP, range(2 * u, 2 * u + 2), passes, wg_q, 1, FP8X4, wg_s)
+        def gate_pair(number, b, tokens, u, passes):
+            acc = bank(number, [P, 2, tokens])
+            return first_stage(acc, b, tokens, range(2 * u, 2 * u + 2), passes, wg_q, 1, FP8X4, wg_s)
 
         def silu_pair(act, gates, c, u, j0, j1):
             nc.scalar.activation(
@@ -281,8 +279,8 @@ def tile_list_modp_gsilu_none_kernel(
             nc.vector.tensor_copy(windows[n][:].indirect(entries(j0, j1)), y)
 
         ups = [up_sums(b, b) for b in range(2)]
-        gates = [[gate_pair(2 + u, 0, u, (0, 1)) for u in range(2)]]
-        gates.append([gate_pair(4 + u, 1, u, (1, 0)) for u in range(2)])
+        gates = [[gate_pair(first + u, b, BLOCK, u, (0, 1)) for u in range(2)] for b, first in enumerate((2, 6))]
+        gates.append([gate_pair(4 + u, 2, GROUP, u, (1, 0)) for u in range(2)])
         acts = [keep([P, 2, BLOCK, 2], F32, "act%d" % b) for b in range(3)]
         acts.append(lay([P, 2, BLOCK, 2], F32, "act3", 24576))
         h_first = keep([P, GROUP, 4], BF16, "h_first")
@@ -290,9 +288,9 @@ def tile_list_modp_gsilu_none_kernel(
 
         y_first = keep([P, GROUP], F32, "y_first")
         for c in range(2):
-            silu_pair(acts[c], gates[0], c, 0, 0, BLOCK)
+            silu_pair(acts[c], gates[c], 0, 0, 0, BLOCK)
             for j0, j1 in ((0, middle), (middle, BLOCK)):
-                silu_pair(acts[c], gates[0], c, 1, j0, j1)
+                silu_pair(acts[c], gates[c], 0, 1, j0, j1)
                 product(h_first, c, ups[c], acts[c], j0, j1)
         for c in range(2):
             j0, j1 = c * BLOCK, (c + 1) * BLOCK
@@ -304,14 +302,14 @@ def tile_list_modp_gsilu_none_kernel(
         ups.extend(up_sums(2 + c, 2 + c) for c in range(2))
         for c in range(2):
             for u in range(2):
-                silu_pair(acts[2 + c], gates[1], c, u, 0, BLOCK)
+                silu_pair(acts[2 + c], gates[2], c, u, 0, BLOCK)
         for c in range(2):
             for j0, j1 in ((0, middle), (middle, BLOCK)):
                 product(h_second, c, ups[2 + c], acts[2 + c], j0, j1)
-            if c == 1:
-                place(0, 0, GROUP, y_first[:], router_first[:])
+        for c in range(2):
             j0, j1 = c * BLOCK, (c + 1) * BLOCK
             quantize_h(h_second[:, j0:j1], GROUP + j0, GROUP + j1)
+        place(0, 0, GROUP, y_first[:], router_first[:])
         for n, offset in ((2, 32832), (3, 42944)):
             zeroed(lay([P, T], F32, "window%d" % n, offset))
 

@@ -151,7 +151,7 @@ def tile_list_modp_gsilu_none_kernel(
             pick_words(*piece)
         for piece in early:
             part_words(*piece)
-        last = (lay([P, BLOCK], U32, "pairs_last", 59264), J - BLOCK, J)
+        last = (lay([P, GROUP], U32, "pairs_last", 59264), J - GROUP, J)
         pick_words(*last)
 
         wd_w = lay([P, 4 * N], U8, "wd_w", 14336)
@@ -183,11 +183,13 @@ def tile_list_modp_gsilu_none_kernel(
         middle = P // 2
         round_wg(nc.scalar.copy, 0, wg_first, 0, 0, SCALAR_SHARE[0], 0, 4)
         round_wg(nc.vector.tensor_copy, 0, wg_first, 0, SCALAR_SHARE[0], LEAD // 4, 0, 4)
-        round_wg(nc.vector.tensor_copy, 0, wg_next, LEAD // 4, 0, P - LEAD // 4, 0, 4)
+        for t0 in (0, 2):
+            round_wg(nc.vector.tensor_copy, 0, wg_next, LEAD // 4, 0, P - LEAD // 4, t0, t0 + 2)
         for r0 in (0, WIDE):
             quantize_wg(0, r0, r0 + WIDE)
         round_wg(nc.scalar.copy, 1, wg_last[0], 0, 0, SCALAR_SHARE[1], 0, 4)
-        round_wg(nc.vector.tensor_copy, 1, wg_last[0], 0, SCALAR_SHARE[1], middle, 0, 4)
+        for t0 in (0, 2):
+            round_wg(nc.vector.tensor_copy, 1, wg_last[0], 0, SCALAR_SHARE[1], middle, t0, t0 + 2)
         for t in range(4):
             quantize_wg(1, t * P, t * P + middle)
         round_wg(nc.scalar.copy, 1, wg_last[1], middle, 0, SCALAR_SHARE[2], 0, 4)
@@ -196,9 +198,9 @@ def tile_list_modp_gsilu_none_kernel(
         for t in range(4):
             quantize_wg(1, t * P + middle, (t + 1) * P)
 
-        late = (lay([P, GROUP], U32, "pairs_late", 8192), HALF + BLOCK, J - BLOCK)
+        late = (lay([P, BLOCK], U32, "pairs_late", 8192), HALF + BLOCK, J - GROUP)
         pick_words(*late)
-        part_words(*last, lay([P, 2, 2 * BLOCK], U8, "apart_last", 10240))
+        part_words(*last, lay([P, 2, 2 * GROUP], U8, "apart_last", 10240))
         part_words(*late)
 
         router_first = lay([P, GROUP], F32, "router_first", 16384)

from contextlib import ExitStack

import concourse.mybir as mybir
from concourse.masks import make_identity

K, R, N, T, J = 1024, 512, 512, 2048, 1024
FLOPS = 2 * J * (2 * K * R + R * N)

F32 = mybir.dt.float32
BF16 = mybir.dt.bfloat16
I32 = mybir.dt.int32
U32 = mybir.dt.uint32
U16 = mybir.dt.uint16
U8 = mybir.dt.uint8
FP8X4 = mybir.dt.float8_e4m3fn_x4
FP4X4 = mybir.dt.float4_e2m1fn_x4
MULT = mybir.AluOpType.mult
SILU = mybir.ActivationFunctionType.Silu
COPY = mybir.ActivationFunctionType.Copy

P = 128
BLOCK = 128
GROUP = 256
HALF = 512
WIDE = R // 2
LEAD = 3 * R // 4
SCALAR_SHARE = (60, 38, 20)
ZERO_PIECE = 512


def tile_list_modp_gsilu_none_kernel(
    tc, tab_words, tab_scales, wg, wu_words, wu_scales, wd_words, wd_scales, wgo, offs, out
):
    nc = tc.nc
    with ExitStack() as ctx:
        held = ctx.enter_context(tc.tile_pool(name="held", bufs=1))
        laid = ctx.enter_context(tc.tile_pool(name="laid", bufs=1))
        psum = ctx.enter_context(tc.psum_pool(name="psum", bufs=1))

        def lay(shape, dtype, name, offset):
            return laid.tile(shape, dtype, name=name, offset=offset, align_bytes=64)

        def keep(shape, dtype, name, tag=None):
            return held.tile(shape, dtype, name=name, tag=tag or name, align_bytes=64)

        def bank(number, shape):
            return psum.tile(shape, F32, name="acc", tag="bank%d" % number)

        offsets = held.tile([P, J // 16], U16, name="offsets")
        nc.sync.dma_start(offsets[:], offs)

        wu_s = keep([P, 2, R], U8, "wu_s")
        nc.gpsimd.memset(wu_s[:].bitcast(I32), 0)

        def load_wu_scales(queue, q):
            queue.dma_start(
                wu_s[32 * q : 32 * q + 4, :, :].bitcast(I32),
                wu_scales[:, 4 * q : 4 * q + 4, :].rearrange("a r n -> r a n").bitcast(I32),
            )

        table_scales = lay([P, T], U8, "table_scales", 4096)
        nc.sync.dma_start(table_scales[96:P, :].bitcast(I32), tab_scales.rearrange("a s t -> s a t").bitcast(I32))
        nc.gpsimd.memset(table_scales[0:96, :].bitcast(I32), 0)

        table = keep([P, T], I32, "table")
        nc.sync.dma_start(table[:], tab_words[0].rearrange("p t b -> p (t b)").bitcast(I32))
        for q in range(4):
            load_wu_scales((nc.sync, nc.scalar)[q % 2], q)
        wu_w = keep([P, 2, 2 * R], U8, "wu_w")
        nc.sync.dma_start(wu_w[:].bitcast(I32), wu_words.rearrange("a p b -> p a b").bitcast(I32))
        wg_rows = wg.rearrange("(a p i) r -> a p i r", a=2, i=4)
        wg_first = lay([P, 4, LEAD], F32, "wg_first", 16384)
        nc.sync.dma_start(wg_first[:], wg_rows[0][:, :, 0:LEAD])

        warm = keep([P, 2], F32, "warm")
        nc.gpsimd.memset(warm[:, 0:1], 0.0)
        nc.scalar.activation(warm[:, 1:2], warm[:, 0:1], SILU)

        wu_dealt = keep([P, 2, 2 * R], U8, "wu_dealt")
        for a in range(2):
            nc.scalar.copy(
                wu_dealt[:, a].bitcast(U16).rearrange("p (t m) -> p t m", t=4),
                wu_w[:, a].bitcast(U16).rearrange("p (m t) -> p t m", t=4),
            )
        planes = []
        for half in range(2):
            plane = keep([P, 2, HALF], U8, "plane%d" % half)
            nc.gpsimd.memset(plane[:].bitcast(I32), 0)
            planes.append(plane)
        identity = keep([P, P], F32, "identity")
        make_identity(nc, identity[:])

        windows = [keep([P, T], F32, "window0")]
        nc.vector.memset(windows[0][:, 0 : T // 2 + 1].bitcast(I32), 0)
        nc.vector.memset(windows[0][:, T // 2 + 1 : T].bitcast(I32), 0)

        def zeroed(window):
            for c in range(0, T, ZERO_PIECE):
                nc.gpsimd.memset(window[:, c : c + ZERO_PIECE].bitcast(I32), 0)
            windows.append(window)

        zeroed(keep([P, T], F32, "window1"))
        wu_s_dealt = keep([P, 2, R], U8, "wu_s_dealt")
        nc.gpsimd.tensor_copy(
            wu_s_dealt[:].rearrange("p a (t m) -> p a t m", t=4), wu_s[:].rearrange("p a (m t) -> p a t m", t=4)
        )

        def entries(j0, j1):
            return offsets[:, j0 // 16 : j1 // 16]

        picked = []
        for half in range(2):
            rows = keep([P, HALF], U8, "picked%d" % half)
            nc.vector.tensor_copy(rows[:], table_scales[:].indirect(entries(half * HALF, (half + 1) * HALF)))
            picked.append(rows)

        def move_scales(half):
            for q in range(4):
                nc.sync.dma_start(
                    planes[half][32 * q : 32 * q + 4].bitcast(I32),
                    picked[half][96 + 8 * q : 96 + 8 * q + 8, :].bitcast(I32),
                )

        move_scales(0)
        wg_next = lay([P, 4, R - LEAD], F32, "wg_next", 2112)
        nc.sync.dma_start(wg_next[:], wg_rows[0][:, :, LEAD:R])
        wg_halves = lay([P, 2, 4, WIDE], F32, "wg_halves", 6080)
        wg_last = []
        for half in range(2):
            nc.sync.dma_start(wg_halves[:, half], wg_rows[1][:, :, half * WIDE : (half + 1) * WIDE])
            wg_last.append(wg_halves[:, half])
        move_scales(1)

        parted = {}

        def pick_words(pairs, j0, j1):
            nc.vector.tensor_copy(pairs[:], table[:].bitcast(U32).indirect(entries(j0, j1)))

        def part_words(pairs, j0, j1, apart=None):
            if apart is None:
                apart = keep([P, 2, 2 * (j1 - j0)], U8, "apart%d" % j0)
            nc.vector.tensor_copy(apart[:].bitcast(U16), pairs[:].bitcast(U16).rearrange("p (j d) -> p d j", d=2))
            for j in range(j0, j1, BLOCK):
                parted[j // BLOCK] = (apart, j - j0)

        early = [
            (lay([P, GROUP], U32, "pairs_first", 59264), 0, GROUP),
            (lay([P, GROUP + BLOCK], U32, "pairs_next", 14336), GROUP, HALF + BLOCK),
        ]
        for piece in early:
            pick_words(*piece)
        for piece in early:
            part_words(*piece)
        last = (lay([P, GROUP], U32, "pairs_last", 59264), J - GROUP, J)
        pick_words(*last)

        wd_w = lay([P, 4 * N], U8, "wd_w", 14336)
        nc.sync.dma_start(wd_w[:].bitcast(I32), wd_words[0].rearrange("p n i -> p (n i)").bitcast(I32))
        wd_s = lay([P, N], U8, "wd_s", 4608)
        nc.gpsimd.memset(wd_s[:].bitcast(I32), 0)
        for q in range(4):
            nc.sync.dma_start(
                wd_s[32 * q : 32 * q + 4, :].bitcast(I32), wd_scales[0, 4 * q : 4 * q + 4, :].bitcast(I32)
            )

        wg_q = keep([P, 2, R], U32, "wg_q")
        wg_s = keep([P, 2, R], U8, "wg_s", tag="wu_s")
        rounded = [keep([P, 4, P, 4], BF16, "wg_bf%d" % a) for a in range(2)]

        def round_wg(copy, a, raw, base, m0, m1, t0, t1):
            copy(
                rounded[a][:, t0:t1, base + m0 : base + m1].rearrange("p t m i -> p m i t"),
                raw[:].rearrange("p i (m t) -> p m i t", t=4)[:, m0:m1, :, t0:t1],
            )

        def quantize_wg(a, r0, r1):
            nc.vector.quantize_mx(
                out=wg_q[:, a, r0:r1].bitcast(FP8X4),
                scales=wg_s[:, a, r0:r1],
                in_=rounded[a][:].rearrange("p t m i -> p (t m i)")[:, 4 * r0 : 4 * r1],
            )

        middle = P // 2
        round_wg(nc.scalar.copy, 0, wg_first, 0, 0, SCALAR_SHARE[0], 0, 4)
        round_wg(nc.vector.tensor_copy, 0, wg_first, 0, SCALAR_SHARE[0], LEAD // 4, 0, 4)
        for t0 in (0, 2):
            round_wg(nc.vector.tensor_copy, 0, wg_next, LEAD // 4, 0, P - LEAD // 4, t0, t0 + 2)
        for r0 in (0, WIDE):
            quantize_wg(0, r0, r0 + WIDE)
        round_wg(nc.scalar.copy, 1, wg_last[0], 0, 0, SCALAR_SHARE[1], 0, 4)
        for t0 in (0, 2):
            round_wg(nc.vector.tensor_copy, 1, wg_last[0], 0, SCALAR_SHARE[1], middle, t0, t0 + 2)
        for t in range(4):
            quantize_wg(1, t * P, t * P + middle)
        round_wg(nc.scalar.copy, 1, wg_last[1], middle, 0, SCALAR_SHARE[2], 0, 4)
        for t0 in (0, 2):
            round_wg(nc.vector.tensor_copy, 1, wg_last[1], middle, SCALAR_SHARE[2], middle, t0, t0 + 2)
        for t in range(4):
            quantize_wg(1, t * P + middle, (t + 1) * P)

        late = (lay([P, BLOCK], U32, "pairs_late", 8192), HALF + BLOCK, J - GROUP)
        pick_words(*late)
        part_words(*last, lay([P, 2, 2 * GROUP], U8, "apart_last", 10240))
        part_words(*late)

        router_first = lay([P, GROUP], F32, "router_first", 16384)
        nc.sync.dma_start(router_first[:], wgo[:, 0:GROUP])
        router_turned = lay([P, 2], F32, "router_turned", 17408)
        with nc.allow_non_contiguous_dma(reason="one router weight for each partition"):
            nc.sync.dma_start(router_turned[:], wgo[0, GROUP:HALF].rearrange("(c p) -> p c", p=P))
        router_last = lay([P, HALF], F32, "router_last", 17472)
        nc.sync.dma_start(router_last[:], wgo[:, HALF:J])

        h_codes = [keep([P, HALF], U32, "h_codes")]
        h_scales = keep([P, J], U8, "h_scales")

        def codes_of(j0, j1):
            return h_codes[j0 // HALF][:, j0 % HALF : (j1 - 1) % HALF + 1].bitcast(FP8X4)

        def first_stage(acc, b, tokens, slices, passes, codes, width, dtype, scales):
            apart, j = parted[b]
            c = b * BLOCK % HALF
            steps = [(a, t) for a in passes for t in slices]
            for a, t in steps:
                nc.tensor.matmul_mx(
                    out=acc[:, t - slices[0]],
                    lhsT=codes[:, a, width * P * t : width * P * (t + 1)].bitcast(dtype),
                    lhsT_scale=scales[:, a, P * t : P * (t + 1)],
                    rhs=apart[:, a, 2 * j : 2 * (j + tokens)].bitcast(FP4X4),
                    rhs_scale=planes[b * BLOCK // HALF][:, a, c : c + tokens],
                    start=(a, t) == steps[0],
                    stop=(a, t) == steps[-1],
                )
            return acc

        def up_sums(number, b):
            return first_stage(bank(number, [P, 4, BLOCK]), b, BLOCK, range(4), (0, 1), wu_dealt, 2, FP4X4, wu_s_dealt)

        def gate_sums(number, b):
            return first_stage(bank(number, [P, 4, BLOCK]), b, BLOCK, range(4), (0, 1), wg_q, 1, FP8X4, wg_s)

        def gate_pair(number, b, tokens, u, passes):
            acc = bank(number, [P, 2, tokens])
            return first_stage(acc, b, tokens, range(2 * u, 2 * u + 2), passes, wg_q, 1, FP8X4, wg_s)

        def silu_pair(act, gates, c, u, j0, j1):
            nc.scalar.activation(
                act[:, u, j0:j1], gates[u][:, :, c * BLOCK + j0 : c * BLOCK + j1].rearrange("p e j -> p j e"), SILU
            )

        def product(h, c, up, act, j0, j1):
            nc.vector.tensor_tensor(
                h[:, c * BLOCK + j0 : c * BLOCK + j1].rearrange("p j (u e) -> p j u e", u=2),
                up[:, :, j0:j1].rearrange("p (u e) j -> p j u e", u=2),
                act[:, :, j0:j1].rearrange("p u j e -> p j u e"),
                MULT,
            )

        def quantize_h(h, j0, j1):
            nc.vector.quantize_mx(
                out=codes_of(j0, j1),
                scales=h_scales[:, j0:j1],
                in_=h.rearrange("p j i -> p (j i)"),
            )

        def down(acc, n, j0, j1):
            nc.tensor.matmul_mx(
                out=acc,
                lhsT=wd_w[:, 4 * P * n : 4 * P * (n + 1)].bitcast(FP8X4),
                lhsT_scale=wd_s[:, P * n : P * (n + 1)],
                rhs=codes_of(j0, j1),
                rhs_scale=h_scales[:, j0:j1],
                start=True,
                stop=True,
            )

        def place(n, j0, j1, y, router):
            nc.vector.tensor_tensor(windows[n][:].indirect(entries(j0, j1)), y, router, MULT)

        def put(n, j0, j1, y):
            nc.vector.tensor_copy(windows[n][:].indirect(entries(j0, j1)), y)

        ups = [up_sums(b, b) for b in range(2)]
        gates = [[gate_pair(first + u, b, BLOCK, u, (0, 1)) for u in range(2)] for b, first in enumerate((2, 6))]
        gates.append([gate_pair(4 + u, 2, GROUP, u, (1, 0)) for u in range(2)])
        acts = [keep([P, 2, BLOCK, 2], F32, "act%d" % b) for b in range(3)]
        acts.append(lay([P, 2, BLOCK, 2], F32, "act3", 24576))
        h_first = keep([P, GROUP, 4], BF16, "h_first")
        h_second = lay([P, GROUP, 4], BF16, "h_second", 40960)

        y_first = keep([P, GROUP], F32, "y_first")
        for c in range(2):
            silu_pair(acts[c], gates[c], 0, 0, 0, BLOCK)
            for j0, j1 in ((0, middle), (middle, BLOCK)):
                silu_pair(acts[c], gates[c], 0, 1, j0, j1)
                product(h_first, c, ups[c], acts[c], j0, j1)
        for c in range(2):
            j0, j1 = c * BLOCK, (c + 1) * BLOCK
            quantize_h(h_first[:, j0:j1], j0, j1)
            acc = bank(6 + c, [P, BLOCK])
            down(acc[:], 0, j0, j1)
            nc.scalar.copy(y_first[:, j0:j1], acc[:])

        ups.extend(up_sums(2 + c, 2 + c) for c in range(2))
        for c in range(2):
            for u in range(2):
                silu_pair(acts[2 + c], gates[2], c, u, 0, BLOCK)
        for c in range(2):
            for j0, j1 in ((0, middle), (middle, BLOCK)):
                product(h_second, c, ups[2 + c], acts[2 + c], j0, j1)
        for c in range(2):
            j0, j1 = c * BLOCK, (c + 1) * BLOCK
            quantize_h(h_second[:, j0:j1], GROUP + j0, GROUP + j1)
        place(0, 0, GROUP, y_first[:], router_first[:])
        for n, offset in ((2, 32832), (3, 42944)):
            zeroed(lay([P, T], F32, "window%d" % n, offset))

        acc = bank(0, [P, 2, GROUP])
        for n in (1, 2):
            down(acc[:, n - 1], n, 0, GROUP)
        y_next = lay([P, 2, GROUP], F32, "y_next", 24576)
        nc.scalar.copy(y_next[:], acc[:])
        for n in (1, 2):
            place(n, 0, GROUP, y_next[:, n - 1], router_first[:])

        weighted = []
        for c in range(2):
            j0, j1 = GROUP + c * BLOCK, GROUP + (c + 1) * BLOCK
            rows = keep([P, N], F32, "weighted%d" % c)
            acc = bank((1, 4)[c], [P, N])
            for n0 in (0, N // 2):
                n1 = n0 + N // 2
                nc.tensor.matmul_mx(
                    out=acc[:, n0:n1],
                    lhsT=codes_of(j0, j1),
                    lhsT_scale=h_scales[:, j0:j1],
                    rhs=wd_w[:, 4 * n0 : 4 * n1].bitcast(FP8X4),
                    rhs_scale=wd_s[:, n0:n1],
                    start=True,
                    stop=True,
                )
            for n0 in (0, N // 2):
                n1 = n0 + N // 2
                nc.scalar.activation(rows[:, n0:n1], acc[:, n0:n1], COPY, scale=router_turned[:, c : c + 1])
            weighted.append(rows)

        for n in range(N // P):
            back = bank(2 + n % 2, [P, GROUP])
            for c in range(2):
                nc.tensor.transpose(
                    back[:, c * BLOCK : (c + 1) * BLOCK], weighted[c][:, n * P : (n + 1) * P], identity[:]
                )
            y = keep([P, GROUP], F32, "y_back%d" % n)
            nc.scalar.copy(y[:], back[:])
            put(n, GROUP, HALF, y[:])

        def by_token(acc):
            return acc[:].rearrange("p t j -> p j t")

        h_late = lay([P, HALF, 4], BF16, "h_late", 25600)
        for b in range(4, 8):
            gate = gate_sums((7, 0)[b % 2], b)
            up = up_sums((6, 1)[b % 2], b)
            act = keep([P, BLOCK, 4], F32, "act%d" % b)
            nc.scalar.activation(act[:], by_token(gate), SILU)
            up_out = keep([P, BLOCK, 4], F32, "up_out%d" % b)
            nc.scalar.copy(up_out[:], by_token(up))
            nc.gpsimd.tensor_tensor(h_late[:, (b - 4) * BLOCK : (b - 3) * BLOCK], up_out[:], act[:], MULT)
        h_codes.append(keep([P, HALF], U32, "late_codes", tag="up_out7"))
        for j0 in (HALF, HALF + GROUP):
            quantize_h(h_late[:, j0 - HALF : j0 - HALF + GROUP], j0, j0 + GROUP)

        acc = bank(2, [P, GROUP])
        down(acc[:], 3, 0, GROUP)
        y_rest = keep([P, GROUP], F32, "y_rest", tag="act7")
        nc.scalar.copy(y_rest[:], acc[:])
        place(3, 0, GROUP, y_rest[:], router_first[:])

        y_last = [keep([P, HALF], F32, "y_last%d" % n) for n in range(N // P)]
        pieces = ((0, 0, GROUP), (1, 0, HALF), (0, GROUP, HALF), (2, 0, HALF), (3, 0, HALF))
        for turn, (n, c0, c1) in enumerate(pieces):
            acc = bank(4 + turn % 2, [P, c1 - c0])
            down(acc[:], n, HALF + c0, HALF + c1)
            nc.scalar.copy(y_last[n][:, c0:c1], acc[:])
            place(n, HALF + c0, HALF + c1, y_last[n][:, c0:c1], router_last[:, c0:c1])
            if c1 == HALF:
                nc.sync.dma_start(out[n * P : (n + 1) * P, :], windows[n][:])
